import numpy as np
import ml_dtypes


def mxq(x, axis, fmt="e4m3"):
    dtype, down = {"e4m3": (ml_dtypes.float8_e4m3fn, 7), "e5m2": (ml_dtypes.float8_e5m2, 14)}[fmt]
    v = np.moveaxis(np.asarray(x, np.float32).astype(ml_dtypes.bfloat16).astype(np.float64), axis, -1)
    blocks = v.reshape(v.shape[:-1] + (-1, 32))
    amax = np.abs(blocks).max(-1, keepdims=True)
    byte = np.maximum(np.where(amax > 0, np.frexp(amax)[1] - 1 + 127, 0) - down, 1)
    scale = np.exp2(byte - 127.0)
    codes = (blocks / scale).astype(np.float32).astype(dtype).astype(np.float64)
    return np.moveaxis((codes * scale).reshape(v.shape), -1, axis)


WIDE = False


def mx_kscale(k):
    if not WIDE:
        return np.ones(k)
    levels = np.array([10, -10, 5, -5, 0])
    if k % 512:
        return np.exp2(np.random.permutation(np.resize(levels, k // 32))).repeat(32)
    a = np.empty((k // 512, 16))
    for p in range(k // 512):
        a[p, :8] = np.random.permutation(np.resize(levels, 8))
        for g in range(8):
            far = levels[np.abs(levels - a[p, g]) >= 10]
            a[p, g + 8] = far[np.random.randint(len(far))]
    return np.exp2(a.ravel()).repeat(32)


def f64(x):
    return np.asarray(x).astype(np.float64)


def striped(idx):
    return np.tile(idx.reshape(-1, 16).T, (8, 1)).astype(np.uint16)


def unstriped(offs):
    return offs[:16].T.reshape(-1).astype(np.int64)


E2M1 = np.array([0.0, 0.5, 1.0, 1.5, 2.0, 3.0, 4.0, 6.0, -0.0, -0.5, -1.0, -1.5, -2.0, -3.0, -4.0, -6.0])


def pack_weight(w, fmt):
    k, n = w.shape
    w = f64(np.asarray(w, np.float32).astype(ml_dtypes.bfloat16)).reshape(k // 32, 32, n)
    amax = np.abs(w).max(1)
    if fmt == "e4m3":
        byte = np.frexp(amax)[1] - 1 + 127 - 7
    else:
        mant, ex = np.frexp(amax / 6.0)
        byte = np.where(mant > 0.5, ex, ex - 1) + 127
    byte = np.clip(np.where(amax > 0, byte, 1), 1, 254)
    scaled = (w * np.exp2(127.0 - byte)[:, None, :]).reshape(k, n).astype(np.float32)
    by_word = np.ascontiguousarray(scaled.reshape(k // 512, 128, 4, n).transpose(0, 1, 3, 2))
    if fmt == "e4m3":
        words = by_word.astype(ml_dtypes.float8_e4m3fn).view(np.uint8)
    else:
        c = by_word.astype(ml_dtypes.float4_e2m1fn).view(np.uint8) & 0xF
        words = (c[..., 0::2] | (c[..., 1::2] << 4)).reshape(k // 512, 128, 2 * n)
    return np.ascontiguousarray(words), np.ascontiguousarray(byte.astype(np.uint8).reshape(k // 512, 16, n))


def unpack_weight(words, scales, fmt):
    g, _, n = scales.shape
    words = np.ascontiguousarray(words).reshape(g, 128, n, -1)
    if fmt == "e4m3":
        vals = words.view(ml_dtypes.float8_e4m3fn).astype(np.float64)
    else:
        nib = np.empty((g, 128, n, 4), np.uint8)
        nib[..., 0::2] = words & 0xF
        nib[..., 1::2] = words >> 4
        vals = E2M1[nib]
    vals = vals * np.repeat(np.exp2(scales.astype(np.float64) - 127.0), 8, axis=1)[..., None]
    return vals.transpose(0, 1, 3, 2).reshape(g * 512, n)


def gelu(v):
    return 0.5 * v * (1.0 + np.tanh(np.sqrt(2.0 / np.pi) * (v + 0.044715 * v**3)))


K, T, E, C, H, N = 512, 512, 4, 128, 512, 256


def by_expert(wq, xq):
    return np.concatenate([wq[e].T @ xq[:, e * C:(e + 1) * C] for e in range(E)], axis=1)


def setup_inputs():
    n = np.random.standard_normal
    s = mx_kscale(K)[:, None]
    u = mx_kscale(H)
    w1 = [pack_weight(m, "e2m1") for m in n((E + 1, K, H)) / np.sqrt(K) / s[None]]
    w3 = [pack_weight(m, "e2m1") for m in n((E + 1, K, H)) / np.sqrt(K) / s[None] * u[None, None, :]]
    w2 = [pack_weight(m, "e2m1") for m in n((E + 1, H, N)) / np.sqrt(H) / u[None, :, None]]
    return {
        "xT": (n((K, T)) * s).astype(np.float32),
        "w1_words": np.stack([m[0] for m in w1]),
        "w1_scales": np.stack([m[1] for m in w1]),
        "w3_words": np.stack([m[0] for m in w3]),
        "w3_scales": np.stack([m[1] for m in w3]),
        "w2_words": np.stack([m[0] for m in w2]),
        "w2_scales": np.stack([m[1] for m in w2]),
        "gate": np.tile(np.random.uniform(0.2, 1.0, E * C), (N, 1)).astype(np.float32),
        "offs": striped(np.random.permutation(T)[:E * C]),
    }


def reference(xT, w1_words, w1_scales, w3_words, w3_scales, w2_words, w2_scales, gate, offs):
    idx = unstriped(offs)
    w1 = np.stack([unpack_weight(w1_words[e], w1_scales[e], "e2m1") for e in range(E + 1)])
    w3 = np.stack([unpack_weight(w3_words[e], w3_scales[e], "e2m1") for e in range(E + 1)])
    w2 = np.stack([unpack_weight(w2_words[e], w2_scales[e], "e2m1") for e in range(E + 1)])
    w1q, w3q, w2q = w1, w3, w2
    xs = mxq(f64(xT), 0, "e4m3")
    hs = gelu(w1q[E].T @ xs) * (w3q[E].T @ xs)
    ys = w2q[E].T @ mxq(hs, 0, "e4m3")
    xq = mxq(f64(xT)[:, idx], 0, "e4m3")
    h = gelu(by_expert(w1q, xq))
    h = h * by_expert(w3q, xq)
    y = by_expert(w2q, mxq(h, 0, "e4m3"))
    out = ys
    out[:, idx] += f64(gate) * y
    return out

@@ -1,0 +1,252 @@
+from contextlib import ExitStack
+
+import concourse.mybir as mybir
+from concourse.masks import make_identity
+
+K, T, E, C, H, N = 512, 512, 4, 128, 512, 256
+FLOPS = 2 * 2 * T * (2 * K * H + H * N)
+
+F32 = mybir.dt.float32
+BF16 = mybir.dt.bfloat16
+I32 = mybir.dt.int32
+U32 = mybir.dt.uint32
+U16 = mybir.dt.uint16
+U8 = mybir.dt.uint8
+FP8X4 = mybir.dt.float8_e4m3fn_x4
+FP4X4 = mybir.dt.float4_e2m1fn_x4
+GELU = mybir.ActivationFunctionType.Gelu_apprx_tanh
+MULT = mybir.AluOpType.mult
+ADD = mybir.AluOpType.add
+P = 128
+GP = ()
+V_TOK = (0, 128)
+
+
+def tile_moe_shr_glu_gelu_kernel(
+    tc, xT, w1_words, w1_scales, w3_words, w3_scales, w2_words, w2_scales, gate, offs, out
+):
+    nc = tc.nc
+    with ExitStack() as ctx:
+        keep = ctx.enter_context(tc.tile_pool(name="keep", bufs=1))
+        work = ctx.enter_context(tc.tile_pool(name="work", bufs=2))
+        psum = ctx.enter_context(tc.psum_pool(name="psum", bufs=2))
+
+        offsets = keep.tile([P, T // 16], U16, name="offsets")
+        nc.sync.dma_start(offsets[:], offs)
+
+        x_rows = xT.rearrange("(p j) t -> p j t", j=4)
+        x_raw = [keep.tile([P, 2, T], F32, name="x_raw%d" % u) for u in range(2)]
+
+        def load_x(u):
+            nc.sync.dma_start(x_raw[u][:], x_rows[:, 2 * u : 2 * u + 2, :])
+
+        load_x(0)
+        warm = keep.tile([P, 1], F32, name="warm")
+        nc.vector.memset(warm[:], 0.0)
+        warm_out = keep.tile([P, 1], F32, name="warm_out")
+
+        w1s = keep.tile([P, 5 * H], U8, name="w1s", align_bytes=64)
+        w3s = keep.tile([P, 5 * H], U8, name="w3s", align_bytes=64)
+        w2s = keep.tile([P, 5 * N], U8, name="w2s", align_bytes=64)
+        nc.gpsimd.memset(w1s[:].bitcast(I32), 0)
+        nc.vector.memset(w3s[:].bitcast(I32), 0)
+        nc.vector.memset(w2s[:].bitcast(I32), 0)
+        ident = keep.tile([P, P], F32, name="ident")
+        nc.scalar.activation(warm_out[:], warm[:], GELU)
+
+        def load_scales(queue, plane, scales, rows):
+            src = scales[:, 0].rearrange("e (q r) i -> r q e i", r=4)
+            dst = plane[:].bitcast(I32)
+            for r in rows:
+                queue.dma_start(
+                    dst[r:P:32, :].rearrange("q (e i) -> q e i", e=5), src[r].bitcast(I32)
+                )
+
+        w1w = keep.tile([P, 5, 2 * H], U8, name="w1w", align_bytes=64)
+        w3w = keep.tile([P, 5, 2 * H], U8, name="w3w", align_bytes=64)
+        w2w = keep.tile([P, 5, 2 * N], U8, name="w2w", align_bytes=64)
+
+        def load_words(queue, tile, words, experts):
+            queue.dma_start(
+                tile[:, experts, :].bitcast(I32), words[experts, 0].rearrange("e p b -> p e b").bitcast(I32)
+            )
+
+        gates = keep.tile([P, T], F32, name="gates")
+        for tile in (w1w[:, 1, 0:4], w3w[:, 1, 0:4], w2w[:, 0, 0:4]):
+            nc.vector.memset(tile.bitcast(I32), 0)
+        nc.vector.memset(gates[:, 0:1], 0.0)
+        load_words(nc.gpsimd, w1w, w1_words, slice(0, 5, 4))
+        load_words(nc.gpsimd, w3w, w3_words, slice(0, 5, 4))
+        make_identity(nc, ident[:])
+        load_x(1)
+        load_scales(nc.sync, w1s, w1_scales, (0, 1, 2, 3))
+        load_scales(nc.sync, w3s, w3_scales, (0, 1, 2, 3))
+        load_words(nc.sync, w1w, w1_words, slice(1, 4))
+        load_words(nc.sync, w3w, w3_words, slice(1, 4))
+        load_words(nc.sync, w2w, w2_words, slice(0, 5))
+        load_scales(nc.sync, w2s, w2_scales, (0, 1, 2, 3))
+        nc.sync.dma_start(gates[:], gate[0:P, :])
+
+        x_pair = [keep.tile([P, T, 2], BF16, name="x_pair%d" % u) for u in range(2)]
+
+        def cast(u):
+            for eng, lo, hi in ((nc.vector.tensor_copy, 0, V_TOK[u]), (nc.scalar.copy, V_TOK[u], T)):
+                if hi > lo:
+                    eng(x_pair[u][:, lo:hi, :], x_raw[u][:, :, lo:hi].rearrange("p e t -> p t e"))
+
+        x_slot = {}
+        x_codes = keep.tile([P, T], U32, name="x_codes", align_bytes=64)
+        x_scales = keep.tile([P, T], U8, name="x_scales", align_bytes=64)
+        window = [keep.tile([P, T], F32, name="window%d" % u) for u in range(2)]
+
+        def gather(c, u):
+            if u == 0:
+                x_slot[c] = work.tile([P, C, 4], BF16, name="x_slot", align_bytes=64)
+            if c == 0:
+                for e in range(2):
+                    nc.vector.tensor_copy(x_slot[c][:, :, 2 * u + e], x_raw[u][:, e, :].indirect(offsets[:, 0:8]))
+                return
+            words = x_slot[c][:].rearrange("p s d -> p (s d)").bitcast(U32)
+            nc.vector.tensor_copy(
+                words.rearrange("p (s u) -> p u s", u=2)[:, u, :],
+                x_pair[u][:].rearrange("p t e -> p (t e)").bitcast(U32).indirect(offsets[:, 8 * c : 8 * c + 8]),
+            )
+
+        def quant_x(c):
+            nc.vector.quantize_mx(
+                out=x_codes[:, c * C : (c + 1) * C].bitcast(FP8X4),
+                scales=x_scales[:, c * C : (c + 1) * C],
+                in_=x_slot[c][:].rearrange("p s d -> p (s d)"),
+            )
+
+        hidden, h_codes, h_scales, banks, results = {}, {}, {}, {}, {}
+
+        def project(c, sub):
+            e = (c, E)[sub]
+            a = psum.tile([P, H], F32, name="a")
+            b = psum.tile([P, H], F32, name="b")
+            for bank, words, scales in ((a, w1w, w1s), (b, w3w, w3s)):
+                nc.tensor.matmul_mx(
+                    out=bank[:],
+                    lhsT=x_codes[:, c * C : (c + 1) * C].bitcast(FP8X4),
+                    lhsT_scale=x_scales[:, c * C : (c + 1) * C],
+                    rhs=words[:, e, :].bitcast(FP4X4),
+                    rhs_scale=scales[:, e * H : (e + 1) * H],
+                    start=True,
+                    stop=True,
+                )
+            banks[c, sub] = (a, b)
+
+        def glu(c, sub):
+            a, b = banks[c, sub]
+            if sub == 0:
+                hidden[c] = work.tile([P, 2, 2, P, 2], BF16, name="hidden", align_bytes=64)
+            g = work.tile([P, 2, P, 2], F32, name="g")
+            nc.scalar.activation(g[:], a[:].rearrange("s (q u e) -> s u q e", u=2, e=2), GELU)
+            nc.vector.tensor_tensor(hidden[c][:, sub], g[:], b[:].rearrange("s (q u e) -> s u q e", u=2, e=2), MULT)
+
+        def turn(c, lo, hi):
+            m = hi - lo
+            t = psum.tile([P, m, 2, C], F32, name="t")
+            words = hidden[c][:].rearrange("s b u q e -> s (b u q e)").bitcast(F32)
+            for sub in range(lo, hi):
+                for u in range(2):
+                    k = (2 * sub + u) * P
+                    nc.tensor.transpose(t[:, sub - lo, u, :], words[:, k : k + P], ident[:])
+            grouped = work.tile([P, m, C, 4], BF16, name="grouped%d" % m, align_bytes=64)
+            nc.scalar.copy(
+                grouped[:].rearrange("p b s d -> p (b s d)").bitcast(F32).rearrange("p (b s u) -> p b s u", b=m, u=2),
+                t[:].rearrange("p b u s -> p b s u"),
+            )
+            h_codes[c, lo] = grouped
+
+        def quant_h(c, lo, hi):
+            m = hi - lo
+            codes = work.tile([P, m * C], U32, name="h_code%d" % m, align_bytes=64)
+            scales = work.tile([P, m * C], U8, name="h_scale%d" % m, align_bytes=64)
+            nc.vector.quantize_mx(
+                out=codes[:].bitcast(FP8X4),
+                scales=scales[:],
+                in_=h_codes[c, lo][:].rearrange("p b s d -> p (b s d)"),
+            )
+            for sub in range(lo, hi):
+                k = (sub - lo) * C
+                h_codes[c, sub] = (codes[:, k : k + C], scales[:, k : k + C])
+
+        def last_layer(c, lo, hi):
+            if lo == 0:
+                results[c] = psum.tile([P, 2, 2, C], F32, name="y")
+            y = results[c]
+            for sub in range(lo, hi):
+                e = (c, E)[sub]
+                codes, scales = h_codes[c, sub]
+                for u in range(2):
+                    nc.tensor.matmul_mx(
+                        out=y[:, sub, u, :],
+                        lhsT=w2w[:, e, 2 * u * P : 2 * (u + 1) * P].bitcast(FP4X4),
+                        lhsT_scale=w2s[:, e * N + u * P : e * N + (u + 1) * P],
+                        rhs=codes.bitcast(FP8X4),
+                        rhs_scale=scales,
+                        start=True,
+                        stop=True,
+                    )
+
+        def combine(c):
+            y = results[c]
+            gcol = gates[:, c * C : (c + 1) * C].unsqueeze(1).to_broadcast([P, 2, C])
+            gated = work.tile([P, 2, C], F32, name="gated")
+            total = keep.tile([P, 2, C], F32, name="total%d" % c)
+            if c in GP:
+                y_sb = work.tile([P, 2, 2, C], F32, name="y_sb")
+                nc.scalar.copy(y_sb[:], y[:])
+                nc.gpsimd.tensor_tensor(gated[:], y_sb[:, 0], gcol, MULT)
+                nc.gpsimd.tensor_tensor(total[:], gated[:], y_sb[:, 1], ADD)
+            else:
+                nc.vector.tensor_tensor(gated[:], y[:, 0], gcol, MULT)
+                nc.vector.tensor_tensor(total[:], gated[:], y[:, 1], ADD)
+            results[c] = total
+
+        def scatter(c):
+            for u in range(2):
+                nc.vector.tensor_copy(window[u][:].indirect(offsets[:, 8 * c : 8 * c + 8]), results[c][:, u, :])
+
+        gather(0, 0)
+        cast(0)
+        gather(0, 1)
+        cast(1)
+        quant_x(0)
+        gather(1, 0)
+        gather(1, 1)
+        quant_x(1)
+        gather(2, 0)
+        gather(2, 1)
+        quant_x(2)
+        gather(3, 0)
+        gather(3, 1)
+        quant_x(3)
+        project(0, 0)
+        project(0, 1)
+        glu(0, 0)
+        project(1, 0)
+        glu(0, 1)
+        for c in range(E):
+            pieces = ((0, 2),) if c < E - 1 else ((0, 1), (1, 2))
+            for lo, hi in pieces:
+                turn(c, lo, hi)
+            if c + 1 < E:
+                project(c + 1, 1)
+                glu(c + 1, 0)
+            for lo, hi in pieces:
+                quant_h(c, lo, hi)
+            if c + 2 < E:
+                project(c + 2, 0)
+            if c + 1 < E:
+                glu(c + 1, 1)
+            for lo, hi in pieces:
+                last_layer(c, lo, hi)
+            if c > 0:
+                scatter(c - 1)
+            combine(c)
+        scatter(E - 1)
+        for u in range(2):
+            nc.sync.dma_start(out[u * P : (u + 1) * P, :], window[u][:])

@@ -15,11 +15,11 @@ U8 = mybir.dt.uint8
 FP8X4 = mybir.dt.float8_e4m3fn_x4
 FP4X4 = mybir.dt.float4_e2m1fn_x4
 GELU = mybir.ActivationFunctionType.Gelu_apprx_tanh
+COPY = mybir.ActivationFunctionType.Copy
 MULT = mybir.AluOpType.mult
 ADD = mybir.AluOpType.add
 P = 128
-GP = ()
-V_TOK = (0, 128)
+V_TOK = (320, 0)
 
 
 def tile_moe_shr_glu_gelu_kernel(
@@ -32,62 +32,43 @@ def tile_moe_shr_glu_gelu_kernel(
         psum = ctx.enter_context(tc.psum_pool(name="psum", bufs=2))
 
         offsets = keep.tile([P, T // 16], U16, name="offsets")
-        nc.sync.dma_start(offsets[:], offs)
-
         x_rows = xT.rearrange("(p j) t -> p j t", j=4)
-        x_raw = [keep.tile([P, 2, T], F32, name="x_raw%d" % u) for u in range(2)]
-
-        def load_x(u):
-            nc.sync.dma_start(x_raw[u][:], x_rows[:, 2 * u : 2 * u + 2, :])
-
-        load_x(0)
+        x_raw = [keep.tile([P, 2, T], F32, name="x_raw%d" % u, tag="big%d" % u, align_bytes=64) for u in range(2)]
+        w1s = keep.tile([P, 5 * H], U8, name="w1s", align_bytes=64)
+        w3s = keep.tile([P, 5 * H], U8, name="w3s", align_bytes=64)
+        nc.gpsimd.memset(w1s[:].bitcast(I32), 0)
+        nc.vector.memset(w3s[:].bitcast(I32), 0)
         warm = keep.tile([P, 1], F32, name="warm")
         nc.vector.memset(warm[:], 0.0)
         warm_out = keep.tile([P, 1], F32, name="warm_out")
-
-        w1s = keep.tile([P, 5 * H], U8, name="w1s", align_bytes=64)
-        w3s = keep.tile([P, 5 * H], U8, name="w3s", align_bytes=64)
-        w2s = keep.tile([P, 5 * N], U8, name="w2s", align_bytes=64)
-        nc.gpsimd.memset(w1s[:].bitcast(I32), 0)
-        nc.vector.memset(w3s[:].bitcast(I32), 0)
-        nc.vector.memset(w2s[:].bitcast(I32), 0)
-        ident = keep.tile([P, P], F32, name="ident")
         nc.scalar.activation(warm_out[:], warm[:], GELU)
+        ident = keep.tile([P, P], F32, name="ident")
+        make_identity(nc, ident[:])
 
-        def load_scales(queue, plane, scales, rows):
+        nc.sync.dma_start(offsets[:], offs)
+        nc.sync.dma_start(x_raw[0][:], x_rows[:, 0:2, :])
+
+        def load_scales(plane, scales):
             src = scales[:, 0].rearrange("e (q r) i -> r q e i", r=4)
-            dst = plane[:].bitcast(I32)
-            for r in rows:
-                queue.dma_start(
-                    dst[r:P:32, :].rearrange("q (e i) -> q e i", e=5), src[r].bitcast(I32)
-                )
+            dst = plane.bitcast(I32)
+            for r in range(4):
+                nc.sync.dma_start(dst[r:P:32, :].rearrange("q (e i) -> q e i", e=5), src[r].bitcast(I32))
 
-        w1w = keep.tile([P, 5, 2 * H], U8, name="w1w", align_bytes=64)
-        w3w = keep.tile([P, 5, 2 * H], U8, name="w3w", align_bytes=64)
-        w2w = keep.tile([P, 5, 2 * N], U8, name="w2w", align_bytes=64)
-
-        def load_words(queue, tile, words, experts):
+        def load_words(queue, dst, words, experts, count):
             queue.dma_start(
-                tile[:, experts, :].bitcast(I32), words[experts, 0].rearrange("e p b -> p e b").bitcast(I32)
+                dst.bitcast(I32).rearrange("p (e b) -> p e b", e=count),
+                words[experts, 0].rearrange("e p b -> p e b").bitcast(I32),
             )
 
-        gates = keep.tile([P, T], F32, name="gates")
-        for tile in (w1w[:, 1, 0:4], w3w[:, 1, 0:4], w2w[:, 0, 0:4]):
-            nc.vector.memset(tile.bitcast(I32), 0)
-        nc.vector.memset(gates[:, 0:1], 0.0)
-        load_words(nc.gpsimd, w1w, w1_words, slice(0, 5, 4))
-        load_words(nc.gpsimd, w3w, w3_words, slice(0, 5, 4))
-        make_identity(nc, ident[:])
-        load_x(1)
-        load_scales(nc.sync, w1s, w1_scales, (0, 1, 2, 3))
-        load_scales(nc.sync, w3s, w3_scales, (0, 1, 2, 3))
-        load_words(nc.sync, w1w, w1_words, slice(1, 4))
-        load_words(nc.sync, w3w, w3_words, slice(1, 4))
-        load_words(nc.sync, w2w, w2_words, slice(0, 5))
-        load_scales(nc.sync, w2s, w2_scales, (0, 1, 2, 3))
-        nc.sync.dma_start(gates[:], gate[0:P, :])
+        w1_first = keep.tile([P, 2 * 2 * H], U8, name="w1_first", align_bytes=64)
+        w3_first = keep.tile([P, 2 * 2 * H], U8, name="w3_first", align_bytes=64)
+        load_scales(w1s[:], w1_scales)
+        nc.sync.dma_start(x_raw[1][:], x_rows[:, 2:4, :])
+        load_words(nc.sync, w1_first[:], w1_words, slice(0, 5, 4), 2)
+        load_words(nc.sync, w3_first[:], w3_words, slice(0, 5, 4), 2)
+        load_scales(w3s[:], w3_scales)
 
-        x_pair = [keep.tile([P, T, 2], BF16, name="x_pair%d" % u) for u in range(2)]
+        x_pair = [keep.tile([P, T, 2], BF16, name="x_pair%d" % u, tag="pair%d" % u) for u in range(2)]
 
         def cast(u):
             for eng, lo, hi in ((nc.vector.tensor_copy, 0, V_TOK[u]), (nc.scalar.copy, V_TOK[u], T)):
@@ -99,46 +80,76 @@ def tile_moe_shr_glu_gelu_kernel(
         x_scales = keep.tile([P, T], U8, name="x_scales", align_bytes=64)
         window = [keep.tile([P, T], F32, name="window%d" % u) for u in range(2)]
 
-        def gather(c, u):
+        def gather(lo, hi, u):
             if u == 0:
-                x_slot[c] = work.tile([P, C, 4], BF16, name="x_slot", align_bytes=64)
-            if c == 0:
+                x_slot[lo] = keep.tile([P, (hi - lo) * C, 4], BF16, name="x_slot%d" % lo, tag="slot%d" % (lo % 2), align_bytes=64)
+            elif lo == 0:
                 for e in range(2):
-                    nc.vector.tensor_copy(x_slot[c][:, :, 2 * u + e], x_raw[u][:, e, :].indirect(offsets[:, 0:8]))
+                    nc.vector.tensor_copy(x_slot[0][:, :, 2 + e], x_raw[1][:, e, :].indirect(offsets[:, 0:8]))
                 return
-            words = x_slot[c][:].rearrange("p s d -> p (s d)").bitcast(U32)
+            words = x_slot[lo][:].rearrange("p s d -> p (s d)").bitcast(U32)
             nc.vector.tensor_copy(
                 words.rearrange("p (s u) -> p u s", u=2)[:, u, :],
-                x_pair[u][:].rearrange("p t e -> p (t e)").bitcast(U32).indirect(offsets[:, 8 * c : 8 * c + 8]),
+                x_pair[u][:].rearrange("p t e -> p (t e)").bitcast(U32).indirect(offsets[:, 8 * lo : 8 * hi]),
             )
 
-        def quant_x(c):
+        def quant_x(lo, hi):
             nc.vector.quantize_mx(
-                out=x_codes[:, c * C : (c + 1) * C].bitcast(FP8X4),
-                scales=x_scales[:, c * C : (c + 1) * C],
-                in_=x_slot[c][:].rearrange("p s d -> p (s d)"),
+                out=x_codes[:, lo * C : hi * C].bitcast(FP8X4),
+                scales=x_scales[:, lo * C : hi * C],
+                in_=x_slot[lo][:].rearrange("p s d -> p (s d)"),
             )
 
-        hidden, h_codes, h_scales, banks, results = {}, {}, {}, {}, {}
+        cast(0)
+        gather(0, 1, 0)
+        gather(0, 1, 1)
+        cast(1)
+        quant_x(0, 1)
+        gather(1, 2, 0)
+        gather(1, 2, 1)
+        quant_x(1, 2)
+        gather(2, 4, 0)
+        gather(2, 4, 1)
+        quant_x(2, 4)
 
-        def project(c, sub):
+        late0 = keep.tile([P, 12 * H], U8, name="late0", tag="big0", align_bytes=64)
+        late1 = keep.tile([P, 15 * N], U8, name="late1", tag="big1", align_bytes=64)
+        w1_late, w3_late = late0[:, : 6 * H], late0[:, 6 * H :]
+        w2w, w2s = late1[:, : 10 * N], late1[:, 10 * N :]
+        load_words(nc.sync, w1_late, w1_words, slice(1, 4), 3)
+        load_words(nc.sync, w3_late, w3_words, slice(1, 4), 3)
+        load_words(nc.sync, w2w, w2_words, slice(0, 5), 5)
+        nc.gpsimd.memset(w2s.bitcast(I32), 0)
+        load_scales(w2s, w2_scales)
+        gates = keep.tile([P, E], F32, name="gates", tag="pair0")
+        with nc.allow_non_contiguous_dma(reason="one gate value a partition"):
+            nc.sync.dma_start(gates[:], gate[0].rearrange("(c p) -> p c", p=P))
+
+        def first_words(first, late, e):
+            if e in (0, E):
+                k = e // E
+                return first[:, k * 2 * H : (k + 1) * 2 * H]
+            return late[:, (e - 1) * 2 * H : e * 2 * H]
+
+        hidden, h_codes, banks, results, summands = {}, {}, {}, {}, {}
+
+        def project(c, sub, which):
             e = (c, E)[sub]
-            a = psum.tile([P, H], F32, name="a")
-            b = psum.tile([P, H], F32, name="b")
-            for bank, words, scales in ((a, w1w, w1s), (b, w3w, w3s)):
-                nc.tensor.matmul_mx(
-                    out=bank[:],
-                    lhsT=x_codes[:, c * C : (c + 1) * C].bitcast(FP8X4),
-                    lhsT_scale=x_scales[:, c * C : (c + 1) * C],
-                    rhs=words[:, e, :].bitcast(FP4X4),
-                    rhs_scale=scales[:, e * H : (e + 1) * H],
-                    start=True,
-                    stop=True,
-                )
-            banks[c, sub] = (a, b)
+            first, late, scales = ((w1_first, w1_late, w1s), (w3_first, w3_late, w3s))[which]
+            bank = psum.tile([P, H], F32, name="ab"[which])
+            nc.tensor.matmul_mx(
+                out=bank[:],
+                lhsT=x_codes[:, c * C : (c + 1) * C].bitcast(FP8X4),
+                lhsT_scale=x_scales[:, c * C : (c + 1) * C],
+                rhs=first_words(first, late, e).bitcast(FP4X4),
+                rhs_scale=scales[:, e * H : (e + 1) * H],
+                start=True,
+                stop=True,
+            )
+            banks[c, sub, which] = bank
 
         def glu(c, sub):
-            a, b = banks[c, sub]
+            a, b = banks[c, sub, 0], banks[c, sub, 1]
             if sub == 0:
                 hidden[c] = work.tile([P, 2, 2, P, 2], BF16, name="hidden", align_bytes=64)
             g = work.tile([P, 2, P, 2], F32, name="g")
@@ -180,11 +191,23 @@ def tile_moe_shr_glu_gelu_kernel(
             for sub in range(lo, hi):
                 e = (c, E)[sub]
                 codes, scales = h_codes[c, sub]
+                if sub == 0:
+                    nc.tensor.matmul_mx(
+                        out=y[:, 0].rearrange("p u s -> p (u s)"),
+                        lhsT=codes.bitcast(FP8X4),
+                        lhsT_scale=scales,
+                        rhs=w2w[:, 2 * e * N : 2 * (e + 1) * N].bitcast(FP4X4),
+                        rhs_scale=w2s[:, e * N : (e + 1) * N],
+                        start=True,
+                        stop=True,
+                    )
+                    continue
                 for u in range(2):
+                    k = e * N + u * P
                     nc.tensor.matmul_mx(
                         out=y[:, sub, u, :],
-                        lhsT=w2w[:, e, 2 * u * P : 2 * (u + 1) * P].bitcast(FP4X4),
-                        lhsT_scale=w2s[:, e * N + u * P : e * N + (u + 1) * P],
+                        lhsT=w2w[:, 2 * k : 2 * (k + P)].bitcast(FP4X4),
+                        lhsT_scale=w2s[:, k : k + P],
                         rhs=codes.bitcast(FP8X4),
                         rhs_scale=scales,
                         start=True,
@@ -193,60 +216,34 @@ def tile_moe_shr_glu_gelu_kernel(
 
         def combine(c):
             y = results[c]
-            gcol = gates[:, c * C : (c + 1) * C].unsqueeze(1).to_broadcast([P, 2, C])
-            gated = work.tile([P, 2, C], F32, name="gated")
-            total = keep.tile([P, 2, C], F32, name="total%d" % c)
-            if c in GP:
-                y_sb = work.tile([P, 2, 2, C], F32, name="y_sb")
-                nc.scalar.copy(y_sb[:], y[:])
-                nc.gpsimd.tensor_tensor(gated[:], y_sb[:, 0], gcol, MULT)
-                nc.gpsimd.tensor_tensor(total[:], gated[:], y_sb[:, 1], ADD)
-            else:
-                nc.vector.tensor_tensor(gated[:], y[:, 0], gcol, MULT)
-                nc.vector.tensor_tensor(total[:], gated[:], y[:, 1], ADD)
-            results[c] = total
-
-        def scatter(c):
+            gated = work.tile([P, 2, P], F32, name="gated")
+            nc.scalar.activation(gated[:], y[:, 0], COPY, scale=gates[:, c : c + 1])
             for u in range(2):
-                nc.vector.tensor_copy(window[u][:].indirect(offsets[:, 8 * c : 8 * c + 8]), results[c][:, u, :])
+                nc.tensor.transpose(y[:, 0, u, :], gated[:, u, :], ident[:])
+            both = keep.tile([P, 2, 2, C], F32, name="both%d" % c)
+            nc.scalar.copy(both[:], y[:])
+            summands[c] = (both[:, 0], both[:, 1])
 
-        gather(0, 0)
-        cast(0)
-        gather(0, 1)
-        cast(1)
-        quant_x(0)
-        gather(1, 0)
-        gather(1, 1)
-        quant_x(1)
-        gather(2, 0)
-        gather(2, 1)
-        quant_x(2)
-        gather(3, 0)
-        gather(3, 1)
-        quant_x(3)
-        project(0, 0)
-        project(0, 1)
-        glu(0, 0)
-        project(1, 0)
-        glu(0, 1)
+        def scatter(c, u):
+            gated, shared = summands[c]
+            nc.vector.tensor_tensor(
+                window[u][:].indirect(offsets[:, 8 * c : 8 * c + 8]), gated[:, u, :], shared[:, u, :], ADD
+            )
+
         for c in range(E):
+            for which in range(2):
+                for sub in range(2):
+                    project(c, sub, which)
+            glu(c, 0)
+            glu(c, 1)
             pieces = ((0, 2),) if c < E - 1 else ((0, 1), (1, 2))
             for lo, hi in pieces:
                 turn(c, lo, hi)
-            if c + 1 < E:
-                project(c + 1, 1)
-                glu(c + 1, 0)
-            for lo, hi in pieces:
                 quant_h(c, lo, hi)
-            if c + 2 < E:
-                project(c + 2, 0)
-            if c + 1 < E:
-                glu(c + 1, 1)
-            for lo, hi in pieces:
                 last_layer(c, lo, hi)
-            if c > 0:
-                scatter(c - 1)
             combine(c)
-        scatter(E - 1)
+        for c in range(E):
+            for u in range(2):
+                scatter(c, u)
         for u in range(2):
             nc.sync.dma_start(out[u * P : (u + 1) * P, :], window[u][:])

@@ -19,7 +19,8 @@ COPY = mybir.ActivationFunctionType.Copy
 MULT = mybir.AluOpType.mult
 ADD = mybir.AluOpType.add
 P = 128
-V_TOK = (320, 0)
+V_TOK = 320
+DIRECT = (0,)
 
 
 def tile_moe_shr_glu_gelu_kernel(
@@ -28,25 +29,28 @@ def tile_moe_shr_glu_gelu_kernel(
     nc = tc.nc
     with ExitStack() as ctx:
         keep = ctx.enter_context(tc.tile_pool(name="keep", bufs=1))
-        work = ctx.enter_context(tc.tile_pool(name="work", bufs=2))
-        psum = ctx.enter_context(tc.psum_pool(name="psum", bufs=2))
+        work = ctx.enter_context(tc.tile_pool(name="work", bufs=4))
+        psum = ctx.enter_context(tc.psum_pool(name="psum", bufs=1))
 
         offsets = keep.tile([P, T // 16], U16, name="offsets")
         x_rows = xT.rearrange("(p j) t -> p j t", j=4)
-        x_raw = [keep.tile([P, 2, T], F32, name="x_raw%d" % u, tag="big%d" % u, align_bytes=64) for u in range(2)]
+        x_low = keep.tile([P, 2, T], F32, name="x_low")
+        x_high = keep.tile([P, 2 * T], F32, name="x_high")
         w1s = keep.tile([P, 5 * H], U8, name="w1s", align_bytes=64)
         w3s = keep.tile([P, 5 * H], U8, name="w3s", align_bytes=64)
         nc.gpsimd.memset(w1s[:].bitcast(I32), 0)
-        nc.vector.memset(w3s[:].bitcast(I32), 0)
         warm = keep.tile([P, 1], F32, name="warm")
         nc.vector.memset(warm[:], 0.0)
+        nc.vector.memset(w3s[:].bitcast(I32), 0)
+        w2s = keep.tile([P, 5 * N], U8, name="w2s", align_bytes=64)
+        nc.vector.memset(w2s[:].bitcast(I32), 0)
         warm_out = keep.tile([P, 1], F32, name="warm_out")
         nc.scalar.activation(warm_out[:], warm[:], GELU)
         ident = keep.tile([P, P], F32, name="ident")
         make_identity(nc, ident[:])
 
         nc.sync.dma_start(offsets[:], offs)
-        nc.sync.dma_start(x_raw[0][:], x_rows[:, 0:2, :])
+        nc.sync.dma_start(x_low[:], x_rows[:, 0:2, :])
 
         def load_scales(plane, scales):
             src = scales[:, 0].rearrange("e (q r) i -> r q e i", r=4)
@@ -54,144 +58,133 @@ def tile_moe_shr_glu_gelu_kernel(
             for r in range(4):
                 nc.sync.dma_start(dst[r:P:32, :].rearrange("q (e i) -> q e i", e=5), src[r].bitcast(I32))
 
-        def load_words(queue, dst, words, experts, count):
-            queue.dma_start(
+        def load_words(dst, words, experts, count):
+            nc.sync.dma_start(
                 dst.bitcast(I32).rearrange("p (e b) -> p e b", e=count),
                 words[experts, 0].rearrange("e p b -> p e b").bitcast(I32),
             )
 
         w1_first = keep.tile([P, 2 * 2 * H], U8, name="w1_first", align_bytes=64)
         w3_first = keep.tile([P, 2 * 2 * H], U8, name="w3_first", align_bytes=64)
+        nc.sync.dma_start(x_high[:].rearrange("p (e t) -> p e t", e=2), x_rows[:, 2:4, :])
+        load_words(w1_first[:], w1_words, slice(0, 5, 4), 2)
         load_scales(w1s[:], w1_scales)
-        nc.sync.dma_start(x_raw[1][:], x_rows[:, 2:4, :])
-        load_words(nc.sync, w1_first[:], w1_words, slice(0, 5, 4), 2)
-        load_words(nc.sync, w3_first[:], w3_words, slice(0, 5, 4), 2)
+        load_words(w3_first[:], w3_words, slice(0, 5, 4), 2)
         load_scales(w3s[:], w3_scales)
 
-        x_pair = [keep.tile([P, T, 2], BF16, name="x_pair%d" % u, tag="pair%d" % u) for u in range(2)]
+        x_pair = [keep.tile([P, T, 2], BF16, name="x_pair%d" % u) for u in range(2)]
+        x_codes, x_scales = {}, {}
 
-        def cast(u):
-            for eng, lo, hi in ((nc.vector.tensor_copy, 0, V_TOK[u]), (nc.scalar.copy, V_TOK[u], T)):
-                if hi > lo:
-                    eng(x_pair[u][:, lo:hi, :], x_raw[u][:, :, lo:hi].rearrange("p e t -> p t e"))
-
-        x_slot = {}
-        x_codes = keep.tile([P, T], U32, name="x_codes", align_bytes=64)
-        x_scales = keep.tile([P, T], U8, name="x_scales", align_bytes=64)
-        window = [keep.tile([P, T], F32, name="window%d" % u) for u in range(2)]
-
-        def gather(lo, hi, u):
-            if u == 0:
-                x_slot[lo] = keep.tile([P, (hi - lo) * C, 4], BF16, name="x_slot%d" % lo, tag="slot%d" % (lo % 2), align_bytes=64)
-            elif lo == 0:
-                for e in range(2):
-                    nc.vector.tensor_copy(x_slot[0][:, :, 2 + e], x_raw[1][:, e, :].indirect(offsets[:, 0:8]))
-                return
-            words = x_slot[lo][:].rearrange("p s d -> p (s d)").bitcast(U32)
+        def gather(out_words, lo, hi, u):
             nc.vector.tensor_copy(
-                words.rearrange("p (s u) -> p u s", u=2)[:, u, :],
+                out_words,
                 x_pair[u][:].rearrange("p t e -> p (t e)").bitcast(U32).indirect(offsets[:, 8 * lo : 8 * hi]),
             )
 
-        def quant_x(lo, hi):
-            nc.vector.quantize_mx(
-                out=x_codes[:, lo * C : hi * C].bitcast(FP8X4),
-                scales=x_scales[:, lo * C : hi * C],
-                in_=x_slot[lo][:].rearrange("p s d -> p (s d)"),
+        def quant_x(lo, hi, values, tag):
+            codes = keep.tile([P, (hi - lo) * C], U32, name="x_codes", tag=tag, align_bytes=64)
+            scales = keep.tile([P, (hi - lo) * C], U8, name="x_scales%d" % lo, align_bytes=64)
+            nc.vector.quantize_mx(out=codes[:].bitcast(FP8X4), scales=scales[:], in_=values)
+            for c in range(lo, hi):
+                x_codes[c] = codes[:, (c - lo) * C : (c - lo + 1) * C]
+                x_scales[c] = scales[:, (c - lo) * C : (c - lo + 1) * C]
+
+        nc.vector.tensor_copy(x_pair[0][:, :V_TOK, :], x_low[:, :, :V_TOK].rearrange("p e t -> p t e"))
+        nc.scalar.copy(x_pair[0][:, V_TOK:, :], x_low[:, :, V_TOK:].rearrange("p e t -> p t e"))
+        rest = keep.tile([P, 4 * C], U32, name="rest", align_bytes=64)
+        gather(rest[:, : 2 * C].rearrange("p (s u) -> p s u", u=2)[:, :, 0], 0, 1, 0)
+        first_values = rest[:, : 2 * C].bitcast(BF16)
+        for e in range(2):
+            nc.vector.tensor_copy(
+                first_values.rearrange("p (s d) -> p s d", d=4)[:, :, 2 + e],
+                x_high[:, e * T : (e + 1) * T].indirect(offsets[:, 0:8]),
             )
+        nc.scalar.copy(x_pair[1][:], x_high[:].rearrange("p (e t) -> p t e", e=2))
+        quant_x(0, 1, first_values, "x_codes0")
+        second = keep.tile([P, 2 * C], U32, name="second", align_bytes=64)
+        for u in range(2):
+            gather(second[:].rearrange("p (s u) -> p s u", u=2)[:, :, u], 1, 2, u)
+        quant_x(1, 2, second[:].bitcast(BF16), "x_codes1")
+        woven = rest
+        for u in range(2):
+            gather(rest[:].rearrange("p (s u) -> p s u", u=2)[:, :, u], 2, 4, u)
 
-        cast(0)
-        gather(0, 1, 0)
-        gather(0, 1, 1)
-        cast(1)
-        quant_x(0, 1)
-        gather(1, 2, 0)
-        gather(1, 2, 1)
-        quant_x(1, 2)
-        gather(2, 4, 0)
-        gather(2, 4, 1)
-        quant_x(2, 4)
-
-        late0 = keep.tile([P, 12 * H], U8, name="late0", tag="big0", align_bytes=64)
-        late1 = keep.tile([P, 15 * N], U8, name="late1", tag="big1", align_bytes=64)
-        w1_late, w3_late = late0[:, : 6 * H], late0[:, 6 * H :]
-        w2w, w2s = late1[:, : 10 * N], late1[:, 10 * N :]
-        load_words(nc.sync, w1_late, w1_words, slice(1, 4), 3)
-        load_words(nc.sync, w3_late, w3_words, slice(1, 4), 3)
-        load_words(nc.sync, w2w, w2_words, slice(0, 5), 5)
-        nc.gpsimd.memset(w2s.bitcast(I32), 0)
-        load_scales(w2s, w2_scales)
-        gates = keep.tile([P, E], F32, name="gates", tag="pair0")
+        w1_late = keep.tile([P, 6 * H], U8, name="w1_late", align_bytes=64)
+        w3_late = keep.tile([P, 6 * H], U8, name="w3_late", align_bytes=64)
+        w2w = keep.tile([P, 10 * N], U8, name="w2w", align_bytes=64)
+        load_words(w1_late[:], w1_words, slice(1, 4), 3)
+        load_words(w3_late[:], w3_words, slice(1, 4), 3)
+        load_words(w2w[:], w2_words, slice(0, 5), 5)
+        load_scales(w2s[:], w2_scales)
+        gate_rows = {}
+        for c in DIRECT:
+            gate_rows[c] = keep.tile([P, C], F32, name="gate_rows%d" % c)
+            nc.sync.dma_start(gate_rows[c][:], gate[0:P, c * C : (c + 1) * C])
+        gates = keep.tile([P, E], F32, name="gates")
         with nc.allow_non_contiguous_dma(reason="one gate value a partition"):
             nc.sync.dma_start(gates[:], gate[0].rearrange("(c p) -> p c", p=P))
 
-        def first_words(first, late, e):
+        def first_words(first, late_words, e):
             if e in (0, E):
                 k = e // E
                 return first[:, k * 2 * H : (k + 1) * 2 * H]
-            return late[:, (e - 1) * 2 * H : e * 2 * H]
+            return late_words[:, (e - 1) * 2 * H : e * 2 * H]
 
-        hidden, h_codes, banks, results, summands = {}, {}, {}, {}, {}
+        hidden, h_codes, banks, results, summands, grouped = {}, {}, {}, {}, {}, {}
 
-        def project(c, sub, which):
+        def project(c, sub, which, bank_tag):
             e = (c, E)[sub]
-            first, late, scales = ((w1_first, w1_late, w1s), (w3_first, w3_late, w3s))[which]
-            bank = psum.tile([P, H], F32, name="ab"[which])
+            first, late_words, scales = ((w1_first, w1_late, w1s), (w3_first, w3_late, w3s))[which]
+            bank = psum.tile([P, H], F32, name="ab", tag=bank_tag)
             nc.tensor.matmul_mx(
                 out=bank[:],
-                lhsT=x_codes[:, c * C : (c + 1) * C].bitcast(FP8X4),
-                lhsT_scale=x_scales[:, c * C : (c + 1) * C],
-                rhs=first_words(first, late, e).bitcast(FP4X4),
+                lhsT=x_codes[c].bitcast(FP8X4),
+                lhsT_scale=x_scales[c],
+                rhs=first_words(first, late_words, e).bitcast(FP4X4),
                 rhs_scale=scales[:, e * H : (e + 1) * H],
                 start=True,
                 stop=True,
             )
             banks[c, sub, which] = bank
 
-        def glu(c, sub):
+        def glu(c, sub, g_tag):
             a, b = banks[c, sub, 0], banks[c, sub, 1]
-            if sub == 0:
-                hidden[c] = work.tile([P, 2, 2, P, 2], BF16, name="hidden", align_bytes=64)
-            g = work.tile([P, 2, P, 2], F32, name="g")
+            if c not in hidden:
+                hidden[c] = keep.tile([P, 2, 2, P, 2], BF16, name="hidden%d" % c, align_bytes=64)
+            g = keep.tile([P, 2, P, 2], F32, name="g", tag=g_tag, align_bytes=64)
+            banks[c, sub, 2] = g
             nc.scalar.activation(g[:], a[:].rearrange("s (q u e) -> s u q e", u=2, e=2), GELU)
             nc.vector.tensor_tensor(hidden[c][:, sub], g[:], b[:].rearrange("s (q u e) -> s u q e", u=2, e=2), MULT)
 
-        def turn(c, lo, hi):
-            m = hi - lo
-            t = psum.tile([P, m, 2, C], F32, name="t")
+        def turn(c, bank_tag):
+            t = psum.tile([P, 2, 2, C], F32, name="t", tag=bank_tag)
             words = hidden[c][:].rearrange("s b u q e -> s (b u q e)").bitcast(F32)
-            for sub in range(lo, hi):
+            for sub in range(2):
                 for u in range(2):
                     k = (2 * sub + u) * P
-                    nc.tensor.transpose(t[:, sub - lo, u, :], words[:, k : k + P], ident[:])
-            grouped = work.tile([P, m, C, 4], BF16, name="grouped%d" % m, align_bytes=64)
+                    nc.tensor.transpose(t[:, sub, u, :], words[:, k : k + P], ident[:])
+            grouped[c] = keep.tile([P, 2, C, 4], BF16, name="grouped%d" % c, align_bytes=64)
             nc.scalar.copy(
-                grouped[:].rearrange("p b s d -> p (b s d)").bitcast(F32).rearrange("p (b s u) -> p b s u", b=m, u=2),
+                grouped[c][:].rearrange("p b s d -> p (b s d)").bitcast(F32).rearrange("p (b s u) -> p b s u", b=2, u=2),
                 t[:].rearrange("p b u s -> p b s u"),
             )
-            h_codes[c, lo] = grouped
 
-        def quant_h(c, lo, hi):
-            m = hi - lo
-            codes = work.tile([P, m * C], U32, name="h_code%d" % m, align_bytes=64)
-            scales = work.tile([P, m * C], U8, name="h_scale%d" % m, align_bytes=64)
+        def quant_h(c):
+            codes = work.tile([P, 2 * C], U32, name="h_code", align_bytes=64)
+            scales = work.tile([P, 2 * C], U8, name="h_scale", align_bytes=64)
             nc.vector.quantize_mx(
-                out=codes[:].bitcast(FP8X4),
-                scales=scales[:],
-                in_=h_codes[c, lo][:].rearrange("p b s d -> p (b s d)"),
+                out=codes[:].bitcast(FP8X4), scales=scales[:], in_=grouped[c][:].rearrange("p b s d -> p (b s d)")
             )
-            for sub in range(lo, hi):
-                k = (sub - lo) * C
-                h_codes[c, sub] = (codes[:, k : k + C], scales[:, k : k + C])
+            for sub in range(2):
+                h_codes[c, sub] = (codes[:, sub * C : (sub + 1) * C], scales[:, sub * C : (sub + 1) * C])
 
-        def last_layer(c, lo, hi):
-            if lo == 0:
-                results[c] = psum.tile([P, 2, 2, C], F32, name="y")
-            y = results[c]
-            for sub in range(lo, hi):
+        def last_layer(c, bank_tag):
+            y = psum.tile([P, 2, 2, C], F32, name="y", tag=bank_tag)
+            results[c] = y
+            for sub in range(2):
                 e = (c, E)[sub]
                 codes, scales = h_codes[c, sub]
-                if sub == 0:
+                if sub == 0 and c not in DIRECT:
                     nc.tensor.matmul_mx(
                         out=y[:, 0].rearrange("p u s -> p (u s)"),
                         lhsT=codes.bitcast(FP8X4),
@@ -214,36 +207,59 @@ def tile_moe_shr_glu_gelu_kernel(
                         stop=True,
                     )
 
-        def combine(c):
+        def apply_gate(c):
             y = results[c]
+            summands[c] = keep.tile([P, 2, 2, C], F32, name="both", tag="hidden3" if c == 1 else "both%d" % c, align_bytes=64)
+            if c in DIRECT:
+                nc.scalar.copy(summands[c][:, 1], y[:, 1])
+                nc.vector.tensor_tensor(
+                    summands[c][:, 0], y[:, 0], gate_rows[c][:].unsqueeze(1).to_broadcast([P, 2, C]), MULT
+                )
+                return
             gated = work.tile([P, 2, P], F32, name="gated")
             nc.scalar.activation(gated[:], y[:, 0], COPY, scale=gates[:, c : c + 1])
             for u in range(2):
                 nc.tensor.transpose(y[:, 0, u, :], gated[:, u, :], ident[:])
-            both = keep.tile([P, 2, 2, C], F32, name="both%d" % c)
-            nc.scalar.copy(both[:], y[:])
-            summands[c] = (both[:, 0], both[:, 1])
 
-        def scatter(c, u):
-            gated, shared = summands[c]
-            nc.vector.tensor_tensor(
-                window[u][:].indirect(offsets[:, 8 * c : 8 * c + 8]), gated[:, u, :], shared[:, u, :], ADD
-            )
+        def empty(c):
+            if c not in DIRECT:
+                nc.scalar.copy(summands[c][:], results[c][:])
 
-        for c in range(E):
-            for which in range(2):
-                for sub in range(2):
-                    project(c, sub, which)
-            glu(c, 0)
-            glu(c, 1)
-            pieces = ((0, 2),) if c < E - 1 else ((0, 1), (1, 2))
-            for lo, hi in pieces:
-                turn(c, lo, hi)
-                quant_h(c, lo, hi)
-                last_layer(c, lo, hi)
-            combine(c)
+        units = ((0, 0), (0, 1), (1, 0), (1, 1), (2, 1), (3, 1), (2, 0), (3, 0))
+        a_bank = ("b0", "b2", "b4", "b1", "b2", "b5", "b4", "b2")
+        b_bank = ("b1", "b3", "b6", "b7", "b0", "b3", "b6", "b7")
+        for i, (c, sub) in enumerate(units):
+            project(c, sub, 0, a_bank[i])
+            project(c, sub, 1, b_bank[i])
+            glu(c, sub, "g%d" % (i % 4) if i else "g_first")
+            if i == 0:
+                quant_x(2, 4, woven[:].bitcast(BF16), "g_first")
+            if i == 4:
+                turn(0, "b1")
+                quant_h(0)
+            if i == 6:
+                turn(1, "b5")
+                quant_h(1)
+        last_layer(0, "b1")
+        apply_gate(0)
+        turn(2, "b4")
+        empty(0)
+        quant_h(2)
+        last_layer(1, "b0")
+        apply_gate(1)
+        turn(3, "b1")
+        quant_h(3)
+        empty(1)
+        for c in (2, 3):
+            last_layer(c, ("b3", "b6")[c - 2])
+            apply_gate(c)
+            empty(c)
+
+        window = [keep.tile([P, T], F32, name="window", tag=tag, align_bytes=64) for tag in ("g3", "grouped2")]
         for c in range(E):
             for u in range(2):
-                scatter(c, u)
+                nc.vector.tensor_tensor(
+                    window[u][:].indirect(offsets[:, 8 * c : 8 * c + 8]), summands[c][:, 0, u, :], summands[c][:, 1, u, :], ADD
+                )
         for u in range(2):
             nc.sync.dma_start(out[u * P : (u + 1) * P, :], window[u][:])

@@ -46,11 +46,27 @@ def tile_moe_shr_glu_gelu_kernel(
         nc.vector.memset(w2s[:].bitcast(I32), 0)
         warm_out = keep.tile([P, 1], F32, name="warm_out")
         nc.scalar.activation(warm_out[:], warm[:], GELU)
+        zeros = keep.tile([P, 4 * T], BF16, name="zeros", align_bytes=64)
+        nc.vector.memset(zeros[:].bitcast(I32), 0)
+        zero_codes = keep.tile([P, T], U32, name="zero_codes", align_bytes=64)
+        zero_scales = keep.tile([P, T], U8, name="zero_scales", align_bytes=64)
+        nc.vector.quantize_mx(out=zero_codes[:].bitcast(FP8X4), scales=zero_scales[:], in_=zeros[:])
+        unread = psum.tile([P, T], F32, name="unread", tag="b7")
+        for repeat in range(5):
+            nc.tensor.matmul_mx(
+                out=unread[:],
+                lhsT=zero_codes[:, :P].bitcast(FP8X4),
+                lhsT_scale=zero_scales[:, :P],
+                rhs=zero_codes[:, : T // 2].bitcast(U8).bitcast(FP4X4),
+                rhs_scale=zero_scales[:],
+                start=True,
+                stop=True,
+            )
         ident = keep.tile([P, P], F32, name="ident")
         make_identity(nc, ident[:])
 
-        nc.sync.dma_start(offsets[:], offs)
         nc.sync.dma_start(x_low[:], x_rows[:, 0:2, :])
+        nc.sync.dma_start(offsets[:], offs)
 
         def load_scales(plane, scales):
             src = scales[:, 0].rearrange("e (q r) i -> r q e i", r=4)
@@ -101,10 +117,12 @@ def tile_moe_shr_glu_gelu_kernel(
             )
         nc.scalar.copy(x_pair[1][:], x_high[:].rearrange("p (e t) -> p t e", e=2))
         quant_x(0, 1, first_values, "x_codes0")
-        second = keep.tile([P, 2 * C], U32, name="second", align_bytes=64)
+        second = keep.tile([P, 2 * C], U32, name="second")
         for u in range(2):
-            gather(second[:].rearrange("p (s u) -> p s u", u=2)[:, :, u], 1, 2, u)
-        quant_x(1, 2, second[:].bitcast(BF16), "x_codes1")
+            gather(second[:, u * C : (u + 1) * C], 1, 2, u)
+        second_woven = keep.tile([P, 2 * C], U32, name="second_woven", align_bytes=64)
+        nc.scalar.copy(second_woven[:].rearrange("p (s u) -> p s u", u=2), second[:].rearrange("p (u s) -> p s u", u=2))
+        quant_x(1, 2, second_woven[:].bitcast(BF16), "x_codes1")
         woven = rest
         for u in range(2):
             gather(rest[:].rearrange("p (s u) -> p s u", u=2)[:, :, u], 2, 4, u)

@@ -18,9 +18,27 @@ GELU = mybir.ActivationFunctionType.Gelu_apprx_tanh
 COPY = mybir.ActivationFunctionType.Copy
 MULT = mybir.AluOpType.mult
 ADD = mybir.AluOpType.add
+
 P = 128
-V_TOK = 320
-DIRECT = (0,)
+MATRICES = E + 1
+ROUTED, SHARED = 0, 1
+LIST_COLUMNS = C // 16
+WARM_PASSES = 5
+GELU_BUFFERS = 4
+CODE_BUFFERS = 4
+
+UNITS = (
+    (0, ROUTED, 0, 1),
+    (0, SHARED, 2, 3),
+    (1, ROUTED, 4, 6),
+    (1, SHARED, 1, 7),
+    (2, SHARED, 2, 0),
+    (3, SHARED, 5, 3),
+    (2, ROUTED, 4, 6),
+    (3, ROUTED, 2, 7),
+)
+TURN_BANK = (1, 5, 4, 1)
+RESULT_BANK = (1, 0, 3, 6)
 
 
 def tile_moe_shr_glu_gelu_kernel(
@@ -29,32 +47,36 @@ def tile_moe_shr_glu_gelu_kernel(
     nc = tc.nc
     with ExitStack() as ctx:
         keep = ctx.enter_context(tc.tile_pool(name="keep", bufs=1))
-        work = ctx.enter_context(tc.tile_pool(name="work", bufs=4))
+        work = ctx.enter_context(tc.tile_pool(name="work", bufs=CODE_BUFFERS))
         psum = ctx.enter_context(tc.psum_pool(name="psum", bufs=1))
 
         offsets = keep.tile([P, T // 16], U16, name="offsets")
-        x_rows = xT.rearrange("(p j) t -> p j t", j=4)
-        x_low = keep.tile([P, 2, T], F32, name="x_low")
-        x_high = keep.tile([P, 2 * T], F32, name="x_high")
-        w1s = keep.tile([P, 5 * H], U8, name="w1s", align_bytes=64)
-        w3s = keep.tile([P, 5 * H], U8, name="w3s", align_bytes=64)
-        nc.gpsimd.memset(w1s[:].bitcast(I32), 0)
-        warm = keep.tile([P, 1], F32, name="warm")
-        nc.vector.memset(warm[:], 0.0)
-        nc.vector.memset(w3s[:].bitcast(I32), 0)
-        w2s = keep.tile([P, 5 * N], U8, name="w2s", align_bytes=64)
-        nc.vector.memset(w2s[:].bitcast(I32), 0)
-        warm_out = keep.tile([P, 1], F32, name="warm_out")
-        nc.scalar.activation(warm_out[:], warm[:], GELU)
-        zeros = keep.tile([P, 4 * T], BF16, name="zeros", align_bytes=64)
+        x_rows = xT.rearrange("(p d) t -> p d t", d=4)
+        x_half = [keep.tile([P, 2 * T], F32, name="x_half%d" % u) for u in range(2)]
+
+        def x_plane(d):
+            return x_half[d // 2][:, (d % 2) * T : (d % 2 + 1) * T]
+
+        zeros = keep.tile([P, 2 * T], BF16, name="zeros", align_bytes=64)
         nc.vector.memset(zeros[:].bitcast(I32), 0)
+        gelu_unread = keep.tile([P, 1], F32, name="gelu_unread")
+        nc.scalar.activation(gelu_unread[:], zeros[:, 0:1], GELU)
+
+        w1s = keep.tile([P, MATRICES * H], U8, name="w1s", align_bytes=64)
+        w3s = keep.tile([P, MATRICES * H], U8, name="w3s", align_bytes=64)
+        w2s = keep.tile([P, MATRICES * N], U8, name="w2s", align_bytes=64)
+        nc.gpsimd.memset(w1s[:].bitcast(I32), 0)
+        nc.vector.memset(w3s[:].bitcast(I32), 0)
+        nc.vector.memset(w2s[:].bitcast(I32), 0)
+
         zero_codes = keep.tile([P, T], U32, name="zero_codes", align_bytes=64)
         zero_scales = keep.tile([P, T], U8, name="zero_scales", align_bytes=64)
-        nc.vector.quantize_mx(out=zero_codes[:].bitcast(FP8X4), scales=zero_scales[:], in_=zeros[:])
-        unread = psum.tile([P, T], F32, name="unread", tag="b7")
-        for repeat in range(5):
+        for columns in (slice(0, T // 2), slice(T // 2, T)):
+            nc.vector.quantize_mx(out=zero_codes[:, columns].bitcast(FP8X4), scales=zero_scales[:, columns], in_=zeros[:])
+        passes_unread = psum.tile([P, T], F32, name="passes_unread", tag="bank7")
+        for repeat in range(WARM_PASSES):
             nc.tensor.matmul_mx(
-                out=unread[:],
+                out=passes_unread[:],
                 lhsT=zero_codes[:, :P].bitcast(FP8X4),
                 lhsT_scale=zero_scales[:, :P],
                 rhs=zero_codes[:, : T // 2].bitcast(U8).bitcast(FP4X4),
@@ -62,149 +84,150 @@ def tile_moe_shr_glu_gelu_kernel(
                 start=True,
                 stop=True,
             )
-        ident = keep.tile([P, P], F32, name="ident")
-        make_identity(nc, ident[:])
 
-        nc.sync.dma_start(x_low[:], x_rows[:, 0:2, :])
-        nc.sync.dma_start(offsets[:], offs)
+        identity = keep.tile([P, P], F32, name="identity")
+        make_identity(nc, identity[:])
 
         def load_scales(plane, scales):
-            src = scales[:, 0].rearrange("e (q r) i -> r q e i", r=4)
-            dst = plane.bitcast(I32)
+            source = scales[:, 0].rearrange("e (q r) i -> r q e i", r=4)
             for r in range(4):
-                nc.sync.dma_start(dst[r:P:32, :].rearrange("q (e i) -> q e i", e=5), src[r].bitcast(I32))
+                nc.sync.dma_start(
+                    plane[:].bitcast(I32)[r:P:32, :].rearrange("q (e i) -> q e i", e=MATRICES), source[r].bitcast(I32)
+                )
 
-        def load_words(dst, words, experts, count):
+        def load_words(tile, words, experts, count):
             nc.sync.dma_start(
-                dst.bitcast(I32).rearrange("p (e b) -> p e b", e=count),
+                tile[:].bitcast(I32).rearrange("p (e b) -> p e b", e=count),
                 words[experts, 0].rearrange("e p b -> p e b").bitcast(I32),
             )
 
+        nc.sync.dma_start(x_plane(0), x_rows[:, 0, :])
+        nc.sync.dma_start(offsets[:], offs)
+        for d in range(1, 4):
+            nc.sync.dma_start(x_plane(d), x_rows[:, d, :])
         w1_first = keep.tile([P, 2 * 2 * H], U8, name="w1_first", align_bytes=64)
         w3_first = keep.tile([P, 2 * 2 * H], U8, name="w3_first", align_bytes=64)
-        nc.sync.dma_start(x_high[:].rearrange("p (e t) -> p e t", e=2), x_rows[:, 2:4, :])
-        load_words(w1_first[:], w1_words, slice(0, 5, 4), 2)
-        load_scales(w1s[:], w1_scales)
-        load_words(w3_first[:], w3_words, slice(0, 5, 4), 2)
-        load_scales(w3s[:], w3_scales)
+        load_words(w1_first, w1_words, slice(0, MATRICES, E), 2)
+        load_scales(w1s, w1_scales)
+        load_words(w3_first, w3_words, slice(0, MATRICES, E), 2)
+        load_scales(w3s, w3_scales)
 
-        x_pair = [keep.tile([P, T, 2], BF16, name="x_pair%d" % u) for u in range(2)]
+        x_pairs = [keep.tile([P, T, 2], BF16, name="x_pairs%d" % u) for u in range(2)]
         x_codes, x_scales = {}, {}
 
-        def gather(out_words, lo, hi, u):
-            nc.vector.tensor_copy(
-                out_words,
-                x_pair[u][:].rearrange("p t e -> p (t e)").bitcast(U32).indirect(offsets[:, 8 * lo : 8 * hi]),
-            )
+        def chunk_offsets(first, end):
+            return offsets[:, LIST_COLUMNS * first : LIST_COLUMNS * end]
 
-        def quant_x(lo, hi, values, tag):
-            codes = keep.tile([P, (hi - lo) * C], U32, name="x_codes", tag=tag, align_bytes=64)
-            scales = keep.tile([P, (hi - lo) * C], U8, name="x_scales%d" % lo, align_bytes=64)
+        def cast_pairs(u):
+            nc.scalar.copy(x_pairs[u][:], x_half[u][:].rearrange("p (e t) -> p t e", e=2))
+
+        def gather_pairs(out_words, first, end, u):
+            window = x_pairs[u][:].rearrange("p t e -> p (t e)").bitcast(U32)
+            nc.vector.tensor_copy(out_words, window.indirect(chunk_offsets(first, end)))
+
+        def quantise_tokens(first, end, values, tag):
+            codes = keep.tile([P, (end - first) * C], U32, name="x_codes", tag=tag, align_bytes=64)
+            scales = keep.tile([P, (end - first) * C], U8, name="x_scales%d" % first, align_bytes=64)
             nc.vector.quantize_mx(out=codes[:].bitcast(FP8X4), scales=scales[:], in_=values)
-            for c in range(lo, hi):
-                x_codes[c] = codes[:, (c - lo) * C : (c - lo + 1) * C]
-                x_scales[c] = scales[:, (c - lo) * C : (c - lo + 1) * C]
+            for c in range(first, end):
+                x_codes[c] = codes[:, (c - first) * C : (c - first + 1) * C]
+                x_scales[c] = scales[:, (c - first) * C : (c - first + 1) * C]
 
-        nc.vector.tensor_copy(x_pair[0][:, :V_TOK, :], x_low[:, :, :V_TOK].rearrange("p e t -> p t e"))
-        nc.scalar.copy(x_pair[0][:, V_TOK:, :], x_low[:, :, V_TOK:].rearrange("p e t -> p t e"))
-        rest = keep.tile([P, 4 * C], U32, name="rest", align_bytes=64)
-        gather(rest[:, : 2 * C].rearrange("p (s u) -> p s u", u=2)[:, :, 0], 0, 1, 0)
-        first_values = rest[:, : 2 * C].bitcast(BF16)
-        for e in range(2):
+        slot_words = keep.tile([P, 4 * C], U32, name="slot_words", align_bytes=64)
+        chunk0_values = slot_words[:, : 2 * C].bitcast(BF16)
+        cast_pairs(0)
+        for d in range(4):
             nc.vector.tensor_copy(
-                first_values.rearrange("p (s d) -> p s d", d=4)[:, :, 2 + e],
-                x_high[:, e * T : (e + 1) * T].indirect(offsets[:, 0:8]),
+                chunk0_values.rearrange("p (s d) -> p s d", d=4)[:, :, d], x_plane(d).indirect(chunk_offsets(0, 1))
             )
-        nc.scalar.copy(x_pair[1][:], x_high[:].rearrange("p (e t) -> p t e", e=2))
-        quant_x(0, 1, first_values, "x_codes0")
-        second = keep.tile([P, 2 * C], U32, name="second")
-        for u in range(2):
-            gather(second[:, u * C : (u + 1) * C], 1, 2, u)
-        second_woven = keep.tile([P, 2 * C], U32, name="second_woven", align_bytes=64)
-        nc.scalar.copy(second_woven[:].rearrange("p (s u) -> p s u", u=2), second[:].rearrange("p (u s) -> p s u", u=2))
-        quant_x(1, 2, second_woven[:].bitcast(BF16), "x_codes1")
-        woven = rest
-        for u in range(2):
-            gather(rest[:].rearrange("p (s u) -> p s u", u=2)[:, :, u], 2, 4, u)
+        cast_pairs(1)
+        quantise_tokens(0, 1, chunk0_values, "x_codes0")
 
-        w1_late = keep.tile([P, 6 * H], U8, name="w1_late", align_bytes=64)
-        w3_late = keep.tile([P, 6 * H], U8, name="w3_late", align_bytes=64)
-        w2w = keep.tile([P, 10 * N], U8, name="w2w", align_bytes=64)
-        load_words(w1_late[:], w1_words, slice(1, 4), 3)
-        load_words(w3_late[:], w3_words, slice(1, 4), 3)
-        load_words(w2w[:], w2_words, slice(0, 5), 5)
-        load_scales(w2s[:], w2_scales)
-        gate_rows = {}
-        for c in DIRECT:
-            gate_rows[c] = keep.tile([P, C], F32, name="gate_rows%d" % c)
-            nc.sync.dma_start(gate_rows[c][:], gate[0:P, c * C : (c + 1) * C])
-        gates = keep.tile([P, E], F32, name="gates")
+        chunk1_halves = keep.tile([P, 2 * C], U32, name="chunk1_halves")
+        for u in range(2):
+            gather_pairs(chunk1_halves[:, u * C : (u + 1) * C], 1, 2, u)
+        chunk1_words = keep.tile([P, 2 * C], U32, name="chunk1_words", align_bytes=64)
+        nc.scalar.copy(
+            chunk1_words[:].rearrange("p (s u) -> p s u", u=2), chunk1_halves[:].rearrange("p (u s) -> p s u", u=2)
+        )
+        quantise_tokens(1, 2, chunk1_words[:].bitcast(BF16), "x_codes1")
+
+        for u in range(2):
+            gather_pairs(slot_words[:].rearrange("p (s u) -> p s u", u=2)[:, :, u], 2, E, u)
+
+        w1_late = keep.tile([P, (E - 1) * 2 * H], U8, name="w1_late", align_bytes=64)
+        w3_late = keep.tile([P, (E - 1) * 2 * H], U8, name="w3_late", align_bytes=64)
+        w2w = keep.tile([P, MATRICES * 2 * N], U8, name="w2w", align_bytes=64)
+        load_words(w1_late, w1_words, slice(1, E), E - 1)
+        load_words(w3_late, w3_words, slice(1, E), E - 1)
+        load_words(w2w, w2_words, slice(0, MATRICES), MATRICES)
+        load_scales(w2s, w2_scales)
+        gate_rows = keep.tile([P, C], F32, name="gate_rows")
+        nc.sync.dma_start(gate_rows[:], gate[0:P, 0:C])
+        gate_columns = keep.tile([P, E - 1], F32, name="gate_columns")
         with nc.allow_non_contiguous_dma(reason="one gate value a partition"):
-            nc.sync.dma_start(gates[:], gate[0].rearrange("(c p) -> p c", p=P))
+            nc.sync.dma_start(gate_columns[:], gate[0, C:].rearrange("(c p) -> p c", p=P))
 
-        def first_words(first, late_words, e):
+        hidden, grouped, h_codes, results, summands = {}, {}, {}, {}, {}
+
+        def project(c, kind, first_words, late_words, scales, bank):
+            e = (c, E)[kind]
             if e in (0, E):
-                k = e // E
-                return first[:, k * 2 * H : (k + 1) * 2 * H]
-            return late_words[:, (e - 1) * 2 * H : e * 2 * H]
-
-        hidden, h_codes, banks, results, summands, grouped = {}, {}, {}, {}, {}, {}
-
-        def project(c, sub, which, bank_tag):
-            e = (c, E)[sub]
-            first, late_words, scales = ((w1_first, w1_late, w1s), (w3_first, w3_late, w3s))[which]
-            bank = psum.tile([P, H], F32, name="ab", tag=bank_tag)
+                words = first_words[:, (e // E) * 2 * H : (e // E + 1) * 2 * H]
+            else:
+                words = late_words[:, (e - 1) * 2 * H : e * 2 * H]
+            sums = psum.tile([P, H], F32, name="sums", tag="bank%d" % bank)
             nc.tensor.matmul_mx(
-                out=bank[:],
+                out=sums[:],
                 lhsT=x_codes[c].bitcast(FP8X4),
                 lhsT_scale=x_scales[c],
-                rhs=first_words(first, late_words, e).bitcast(FP4X4),
+                rhs=words.bitcast(FP4X4),
                 rhs_scale=scales[:, e * H : (e + 1) * H],
                 start=True,
                 stop=True,
             )
-            banks[c, sub, which] = bank
+            return sums[:].rearrange("s (q u e) -> s u q e", u=2, e=2)
 
-        def glu(c, sub, g_tag):
-            a, b = banks[c, sub, 0], banks[c, sub, 1]
+        def unit(c, kind, a_bank, b_bank, gelu_tag):
+            a = project(c, kind, w1_first, w1_late, w1s, a_bank)
+            b = project(c, kind, w3_first, w3_late, w3s, b_bank)
             if c not in hidden:
                 hidden[c] = keep.tile([P, 2, 2, P, 2], BF16, name="hidden%d" % c, align_bytes=64)
-            g = keep.tile([P, 2, P, 2], F32, name="g", tag=g_tag, align_bytes=64)
-            banks[c, sub, 2] = g
-            nc.scalar.activation(g[:], a[:].rearrange("s (q u e) -> s u q e", u=2, e=2), GELU)
-            nc.vector.tensor_tensor(hidden[c][:, sub], g[:], b[:].rearrange("s (q u e) -> s u q e", u=2, e=2), MULT)
+            gelu_a = keep.tile([P, 2, P, 2], F32, name="gelu_a", tag=gelu_tag, align_bytes=64)
+            nc.scalar.activation(gelu_a[:], a, GELU)
+            nc.vector.tensor_tensor(hidden[c][:, kind], gelu_a[:], b, MULT)
 
-        def turn(c, bank_tag):
-            t = psum.tile([P, 2, 2, C], F32, name="t", tag=bank_tag)
-            words = hidden[c][:].rearrange("s b u q e -> s (b u q e)").bitcast(F32)
-            for sub in range(2):
+        def turn(c):
+            turned = psum.tile([P, 2, 2, C], F32, name="turned", tag="bank%d" % TURN_BANK[c])
+            words = hidden[c][:].rearrange("s k u q e -> s (k u q e)").bitcast(F32)
+            for kind in (ROUTED, SHARED):
                 for u in range(2):
-                    k = (2 * sub + u) * P
-                    nc.tensor.transpose(t[:, sub, u, :], words[:, k : k + P], ident[:])
+                    start = (2 * kind + u) * P
+                    nc.tensor.transpose(turned[:, kind, u, :], words[:, start : start + P], identity[:])
             grouped[c] = keep.tile([P, 2, C, 4], BF16, name="grouped%d" % c, align_bytes=64)
             nc.scalar.copy(
-                grouped[c][:].rearrange("p b s d -> p (b s d)").bitcast(F32).rearrange("p (b s u) -> p b s u", b=2, u=2),
-                t[:].rearrange("p b u s -> p b s u"),
+                grouped[c][:].rearrange("p k s d -> p (k s d)").bitcast(F32).rearrange("p (k s u) -> p k s u", k=2, u=2),
+                turned[:].rearrange("p k u s -> p k s u"),
             )
 
-        def quant_h(c):
-            codes = work.tile([P, 2 * C], U32, name="h_code", align_bytes=64)
-            scales = work.tile([P, 2 * C], U8, name="h_scale", align_bytes=64)
+        def quantise_hidden(c):
+            codes = work.tile([P, 2 * C], U32, name="h_codes", align_bytes=64)
+            scales = work.tile([P, 2 * C], U8, name="h_scales", align_bytes=64)
             nc.vector.quantize_mx(
-                out=codes[:].bitcast(FP8X4), scales=scales[:], in_=grouped[c][:].rearrange("p b s d -> p (b s d)")
+                out=codes[:].bitcast(FP8X4), scales=scales[:], in_=grouped[c][:].rearrange("p k s d -> p (k s d)")
             )
-            for sub in range(2):
-                h_codes[c, sub] = (codes[:, sub * C : (sub + 1) * C], scales[:, sub * C : (sub + 1) * C])
+            for kind in (ROUTED, SHARED):
+                h_codes[c, kind] = (codes[:, kind * C : (kind + 1) * C], scales[:, kind * C : (kind + 1) * C])
 
-        def last_layer(c, bank_tag):
-            y = psum.tile([P, 2, 2, C], F32, name="y", tag=bank_tag)
+        def last_layer(c):
+            y = psum.tile([P, 2, 2, C], F32, name="y", tag="bank%d" % RESULT_BANK[c])
             results[c] = y
-            for sub in range(2):
-                e = (c, E)[sub]
-                codes, scales = h_codes[c, sub]
-                if sub == 0 and c not in DIRECT:
+            for kind in (ROUTED, SHARED):
+                e = (c, E)[kind]
+                codes, scales = h_codes[c, kind]
+                if kind == ROUTED and c > 0:
                     nc.tensor.matmul_mx(
-                        out=y[:, 0].rearrange("p u s -> p (u s)"),
+                        out=y[:, ROUTED].rearrange("p v s -> p (v s)"),
                         lhsT=codes.bitcast(FP8X4),
                         lhsT_scale=scales,
                         rhs=w2w[:, 2 * e * N : 2 * (e + 1) * N].bitcast(FP4X4),
@@ -213,71 +236,72 @@ def tile_moe_shr_glu_gelu_kernel(
                         stop=True,
                     )
                     continue
-                for u in range(2):
-                    k = e * N + u * P
+                for v in range(2):
+                    column = e * N + v * P
                     nc.tensor.matmul_mx(
-                        out=y[:, sub, u, :],
-                        lhsT=w2w[:, 2 * k : 2 * (k + P)].bitcast(FP4X4),
-                        lhsT_scale=w2s[:, k : k + P],
+                        out=y[:, kind, v, :],
+                        lhsT=w2w[:, 2 * column : 2 * (column + P)].bitcast(FP4X4),
+                        lhsT_scale=w2s[:, column : column + P],
                         rhs=codes.bitcast(FP8X4),
                         rhs_scale=scales,
                         start=True,
                         stop=True,
                     )
 
-        def apply_gate(c):
+        def new_summands(c, tag):
+            summands[c] = keep.tile([P, 2, 2, C], F32, name="summands", tag=tag, align_bytes=64)
+
+        def gate_on_vector(c):
             y = results[c]
-            summands[c] = keep.tile([P, 2, 2, C], F32, name="both", tag="hidden3" if c == 1 else "both%d" % c, align_bytes=64)
-            if c in DIRECT:
-                nc.scalar.copy(summands[c][:, 1], y[:, 1])
-                nc.vector.tensor_tensor(
-                    summands[c][:, 0], y[:, 0], gate_rows[c][:].unsqueeze(1).to_broadcast([P, 2, C]), MULT
-                )
-                return
+            nc.scalar.copy(summands[c][:, SHARED], y[:, SHARED])
+            nc.vector.tensor_tensor(
+                summands[c][:, ROUTED], y[:, ROUTED], gate_rows[:].unsqueeze(1).to_broadcast([P, 2, C]), MULT
+            )
+
+        def gate_on_scalar(c):
+            y = results[c]
             gated = work.tile([P, 2, P], F32, name="gated")
-            nc.scalar.activation(gated[:], y[:, 0], COPY, scale=gates[:, c : c + 1])
-            for u in range(2):
-                nc.tensor.transpose(y[:, 0, u, :], gated[:, u, :], ident[:])
+            nc.scalar.activation(gated[:], y[:, ROUTED], COPY, scale=gate_columns[:, c - 1 : c])
+            for v in range(2):
+                nc.tensor.transpose(y[:, ROUTED, v, :], gated[:, v, :], identity[:])
 
-        def empty(c):
-            if c not in DIRECT:
-                nc.scalar.copy(summands[c][:], results[c][:])
+        def empty_result(c):
+            nc.scalar.copy(summands[c][:], results[c][:])
 
-        units = ((0, 0), (0, 1), (1, 0), (1, 1), (2, 1), (3, 1), (2, 0), (3, 0))
-        a_bank = ("b0", "b2", "b4", "b1", "b2", "b5", "b4", "b2")
-        b_bank = ("b1", "b3", "b6", "b7", "b0", "b3", "b6", "b7")
-        for i, (c, sub) in enumerate(units):
-            project(c, sub, 0, a_bank[i])
-            project(c, sub, 1, b_bank[i])
-            glu(c, sub, "g%d" % (i % 4) if i else "g_first")
+        for i, (c, kind, a_bank, b_bank) in enumerate(UNITS):
+            unit(c, kind, a_bank, b_bank, "gelu%d" % (i % GELU_BUFFERS) if i else "gelu_first")
             if i == 0:
-                quant_x(2, 4, woven[:].bitcast(BF16), "g_first")
-            if i == 4:
-                turn(0, "b1")
-                quant_h(0)
-            if i == 6:
-                turn(1, "b5")
-                quant_h(1)
-        last_layer(0, "b1")
-        apply_gate(0)
-        turn(2, "b4")
-        empty(0)
-        quant_h(2)
-        last_layer(1, "b0")
-        apply_gate(1)
-        turn(3, "b1")
-        quant_h(3)
-        empty(1)
-        for c in (2, 3):
-            last_layer(c, ("b3", "b6")[c - 2])
-            apply_gate(c)
-            empty(c)
+                quantise_tokens(2, E, slot_words[:].bitcast(BF16), "gelu_first")
+            if c == 2:
+                turn(1 - kind)
+                quantise_hidden(1 - kind)
 
-        window = [keep.tile([P, T], F32, name="window", tag=tag, align_bytes=64) for tag in ("g3", "grouped2")]
+        last_layer(0)
+        new_summands(0, "summands0")
+        gate_on_vector(0)
+        turn(2)
+        quantise_hidden(2)
+        last_layer(1)
+        new_summands(1, "hidden3")
+        gate_on_scalar(1)
+        turn(3)
+        quantise_hidden(3)
+        empty_result(1)
+        for c in range(2, E):
+            last_layer(c)
+            new_summands(c, "summands%d" % c)
+            gate_on_scalar(c)
+            empty_result(c)
+
+        last_gelu_tag = "gelu%d" % ((len(UNITS) - 1) % GELU_BUFFERS)
+        windows = [keep.tile([P, T], F32, name="window", tag=tag, align_bytes=64) for tag in (last_gelu_tag, "grouped2")]
         for c in range(E):
-            for u in range(2):
+            for v in range(2):
                 nc.vector.tensor_tensor(
-                    window[u][:].indirect(offsets[:, 8 * c : 8 * c + 8]), summands[c][:, 0, u, :], summands[c][:, 1, u, :], ADD
+                    windows[v][:].indirect(chunk_offsets(c, c + 1)),
+                    summands[c][:, ROUTED, v, :],
+                    summands[c][:, SHARED, v, :],
+                    ADD,
                 )
-        for u in range(2):
-            nc.sync.dma_start(out[u * P : (u + 1) * P, :], window[u][:])
+        for v in range(2):
+            nc.sync.dma_start(out[v * P : (v + 1) * P, :], windows[v][:])

@@ -24,21 +24,14 @@ MATRICES = E + 1
 ROUTED, SHARED = 0, 1
 LIST_COLUMNS = C // 16
 WARM_PASSES = 5
-GELU_BUFFERS = 4
 CODE_BUFFERS = 4
 
-UNITS = (
-    (0, ROUTED, 0, 1),
-    (0, SHARED, 2, 3),
-    (1, ROUTED, 4, 6),
-    (1, SHARED, 1, 7),
-    (2, SHARED, 2, 0),
-    (3, SHARED, 5, 3),
-    (2, ROUTED, 4, 6),
-    (3, ROUTED, 2, 7),
-)
-TURN_BANK = (1, 5, 4, 1)
-RESULT_BANK = (1, 0, 3, 6)
+UNITS = ((0, ROUTED), (0, SHARED), (1, SHARED), (1, ROUTED), (2, SHARED), (2, ROUTED), (3, SHARED), (3, ROUTED))
+A_BANK = (0, 2, 4, 5, 1, 4, 5, 7)
+B_BANK = (1, 3, 0, 6, 2, 3, 0, 6)
+TURN_BANK = (1, 4, 5, 7)
+RESULT_BANK = (1, 2, 3, 0)
+GATED_BANK = (None, 4, 5, 6)
 
 
 def tile_moe_shr_glu_gelu_kernel(
@@ -133,27 +126,37 @@ def tile_moe_shr_glu_gelu_kernel(
                 x_codes[c] = codes[:, (c - first) * C : (c - first + 1) * C]
                 x_scales[c] = scales[:, (c - first) * C : (c - first + 1) * C]
 
-        slot_words = keep.tile([P, 4 * C], U32, name="slot_words", align_bytes=64)
-        chunk0_values = slot_words[:, : 2 * C].bitcast(BF16)
+        slot_words = {}
+
+        def new_slot_words(c):
+            slot_words[c] = keep.tile([P, 2 * C], U32, name="slot_words", tag="slot_words%d" % (c % 2), align_bytes=64)
+
+        def gather_half(c, u):
+            gather_pairs(slot_words[c][:].rearrange("p (s u) -> p s u", u=2)[:, :, u], c, c + 1, u)
+
+        def quantise_chunk(c, tag):
+            quantise_tokens(c, c + 1, slot_words[c][:].bitcast(BF16), tag)
+
+        new_slot_words(0)
+        new_slot_words(1)
+        chunk0_values = slot_words[0][:].bitcast(BF16)
         cast_pairs(0)
         for d in range(4):
             nc.vector.tensor_copy(
                 chunk0_values.rearrange("p (s d) -> p s d", d=4)[:, :, d], x_plane(d).indirect(chunk_offsets(0, 1))
             )
         cast_pairs(1)
-        quantise_tokens(0, 1, chunk0_values, "x_codes0")
-
-        chunk1_halves = keep.tile([P, 2 * C], U32, name="chunk1_halves")
-        for u in range(2):
-            gather_pairs(chunk1_halves[:, u * C : (u + 1) * C], 1, 2, u)
-        chunk1_words = keep.tile([P, 2 * C], U32, name="chunk1_words", align_bytes=64)
-        nc.scalar.copy(
-            chunk1_words[:].rearrange("p (s u) -> p s u", u=2), chunk1_halves[:].rearrange("p (u s) -> p s u", u=2)
-        )
-        quantise_tokens(1, 2, chunk1_words[:].bitcast(BF16), "x_codes1")
-
-        for u in range(2):
-            gather_pairs(slot_words[:].rearrange("p (s u) -> p s u", u=2)[:, :, u], 2, E, u)
+        gather_half(1, 0)
+        quantise_chunk(0, "x_codes0")
+        new_slot_words(2)
+        gather_half(2, 0)
+        gather_half(1, 1)
+        gather_half(2, 1)
+        quantise_chunk(1, "x_codes1")
+        quantise_chunk(2, "x_codes2")
+        new_slot_words(3)
+        gather_half(3, 0)
+        gather_half(3, 1)
 
         w1_late = keep.tile([P, (E - 1) * 2 * H], U8, name="w1_late", align_bytes=64)
         w3_late = keep.tile([P, (E - 1) * 2 * H], U8, name="w3_late", align_bytes=64)
@@ -168,7 +171,7 @@ def tile_moe_shr_glu_gelu_kernel(
         with nc.allow_non_contiguous_dma(reason="one gate value a partition"):
             nc.sync.dma_start(gate_columns[:], gate[0, C:].rearrange("(c p) -> p c", p=P))
 
-        hidden, grouped, h_codes, results, summands = {}, {}, {}, {}, {}
+        hidden, grouped, h_codes, results = {}, {}, {}, {}
 
         def project(c, kind, first_words, late_words, scales, bank):
             e = (c, E)[kind]
@@ -188,26 +191,39 @@ def tile_moe_shr_glu_gelu_kernel(
             )
             return sums[:].rearrange("s (q u e) -> s u q e", u=2, e=2)
 
-        def unit(c, kind, a_bank, b_bank, gelu_tag):
-            a = project(c, kind, w1_first, w1_late, w1s, a_bank)
-            b = project(c, kind, w3_first, w3_late, w3s, b_bank)
+        a_sums, b_sums, gelus = {}, {}, {}
+
+        def a_pass(i):
+            a_sums[i] = project(*UNITS[i], w1_first, w1_late, w1s, A_BANK[i])
+
+        def b_pass(i):
+            b_sums[i] = project(*UNITS[i], w3_first, w3_late, w3s, B_BANK[i])
+
+        def gelu(i):
+            gelus[i] = keep.tile([P, 2, P, 2], F32, name="gelu%d" % i, align_bytes=64)
+            nc.scalar.activation(gelus[i][:], a_sums[i], GELU)
+
+        def product(i):
+            c, kind = UNITS[i]
             if c not in hidden:
                 hidden[c] = keep.tile([P, 2, 2, P, 2], BF16, name="hidden%d" % c, align_bytes=64)
-            gelu_a = keep.tile([P, 2, P, 2], F32, name="gelu_a", tag=gelu_tag, align_bytes=64)
-            nc.scalar.activation(gelu_a[:], a, GELU)
-            nc.vector.tensor_tensor(hidden[c][:, kind], gelu_a[:], b, MULT)
+            nc.vector.tensor_tensor(hidden[c][:, kind], gelus[i][:], b_sums[i], MULT)
+
+        turned = {}
 
         def turn(c):
-            turned = psum.tile([P, 2, 2, C], F32, name="turned", tag="bank%d" % TURN_BANK[c])
+            turned[c] = psum.tile([P, 2, 2, C], F32, name="turned", tag="bank%d" % TURN_BANK[c])
             words = hidden[c][:].rearrange("s k u q e -> s (k u q e)").bitcast(F32)
             for kind in (ROUTED, SHARED):
                 for u in range(2):
                     start = (2 * kind + u) * P
-                    nc.tensor.transpose(turned[:, kind, u, :], words[:, start : start + P], identity[:])
+                    nc.tensor.transpose(turned[c][:, kind, u, :], words[:, start : start + P], identity[:])
+
+        def group(c):
             grouped[c] = keep.tile([P, 2, C, 4], BF16, name="grouped%d" % c, align_bytes=64)
             nc.scalar.copy(
                 grouped[c][:].rearrange("p k s d -> p (k s d)").bitcast(F32).rearrange("p (k s u) -> p k s u", k=2, u=2),
-                turned[:].rearrange("p k u s -> p k s u"),
+                turned[c][:].rearrange("p k u s -> p k s u"),
             )
 
         def quantise_hidden(c):
@@ -248,60 +264,103 @@ def tile_moe_shr_glu_gelu_kernel(
                         stop=True,
                     )
 
-        def new_summands(c, tag):
-            summands[c] = keep.tile([P, 2, 2, C], F32, name="summands", tag=tag, align_bytes=64)
+        gated, gated_turned, routed_part, shared_part = {}, {}, {}, {}
+
+        def copy_shared(c):
+            shared_part[c] = keep.tile([P, 2, C], F32, name="shared_part%d" % c, align_bytes=64)
+            nc.scalar.copy(shared_part[c][:], results[c][:, SHARED])
 
         def gate_on_vector(c):
-            y = results[c]
-            nc.scalar.copy(summands[c][:, SHARED], y[:, SHARED])
+            routed_part[c] = keep.tile([P, 2, C], F32, name="routed_part%d" % c, align_bytes=64)
             nc.vector.tensor_tensor(
-                summands[c][:, ROUTED], y[:, ROUTED], gate_rows[:].unsqueeze(1).to_broadcast([P, 2, C]), MULT
+                routed_part[c][:], results[c][:, ROUTED], gate_rows[:].unsqueeze(1).to_broadcast([P, 2, C]), MULT
             )
 
         def gate_on_scalar(c):
-            y = results[c]
-            gated = work.tile([P, 2, P], F32, name="gated")
-            nc.scalar.activation(gated[:], y[:, ROUTED], COPY, scale=gate_columns[:, c - 1 : c])
+            gated[c] = work.tile([P, 2, P], F32, name="gated")
+            nc.scalar.activation(gated[c][:], results[c][:, ROUTED], COPY, scale=gate_columns[:, c - 1 : c])
+
+        def turn_gated(c):
+            gated_turned[c] = psum.tile([P, 2, C], F32, name="gated_turned", tag="bank%d" % GATED_BANK[c])
             for v in range(2):
-                nc.tensor.transpose(y[:, ROUTED, v, :], gated[:, v, :], identity[:])
+                nc.tensor.transpose(gated_turned[c][:, v, :], gated[c][:, v, :], identity[:])
 
-        def empty_result(c):
-            nc.scalar.copy(summands[c][:], results[c][:])
+        def copy_gated(c):
+            routed_part[c] = keep.tile([P, 2, C], F32, name="routed_part%d" % c, align_bytes=64)
+            nc.scalar.copy(routed_part[c][:], gated_turned[c][:])
 
-        for i, (c, kind, a_bank, b_bank) in enumerate(UNITS):
-            unit(c, kind, a_bank, b_bank, "gelu%d" % (i % GELU_BUFFERS) if i else "gelu_first")
-            if i == 0:
-                quantise_tokens(2, E, slot_words[:].bitcast(BF16), "gelu_first")
-            if c == 2:
-                turn(1 - kind)
-                quantise_hidden(1 - kind)
+        windows = {}
 
+        def scatter(c, v):
+            if v not in windows:
+                windows[v] = keep.tile([P, T], F32, name="window", tag=("gelu7", "grouped2")[v], align_bytes=64)
+            nc.vector.tensor_tensor(
+                windows[v][:].indirect(chunk_offsets(c, c + 1)), routed_part[c][:, v, :], shared_part[c][:, v, :], ADD
+            )
+
+        a_pass(0)
+        a_pass(1)
+        gelu(0)
+        gelu(1)
+        a_pass(2)
+        b_pass(0)
+        b_pass(1)
+        gelu(2)
+        a_pass(3)
+        b_pass(2)
+        gelu(3)
+        b_pass(3)
+        product(0)
+        a_pass(4)
+        product(1)
+        quantise_chunk(3, "gelu0")
+        gelu(4)
+        a_pass(5)
+        b_pass(4)
+        product(2)
+        gelu(5)
+        a_pass(6)
+        b_pass(5)
+        product(3)
+        gelu(6)
+        turn(0)
+        group(0)
+        a_pass(7)
+        b_pass(6)
+        product(4)
+        b_pass(7)
+        gelu(7)
+        product(5)
+        turn(1)
+        group(1)
+        product(6)
+        quantise_hidden(0)
         last_layer(0)
-        new_summands(0, "summands0")
+        product(7)
+        quantise_hidden(1)
+        copy_shared(0)
         gate_on_vector(0)
         turn(2)
-        quantise_hidden(2)
+        group(2)
         last_layer(1)
-        new_summands(1, "hidden3")
+        quantise_hidden(2)
         gate_on_scalar(1)
         turn(3)
+        group(3)
+        turn_gated(1)
+        copy_shared(1)
+        copy_gated(1)
+        scatter(0, 0)
         quantise_hidden(3)
-        empty_result(1)
+        scatter(0, 1)
         for c in range(2, E):
             last_layer(c)
-            new_summands(c, "summands%d" % c)
             gate_on_scalar(c)
-            empty_result(c)
-
-        last_gelu_tag = "gelu%d" % ((len(UNITS) - 1) % GELU_BUFFERS)
-        windows = [keep.tile([P, T], F32, name="window", tag=tag, align_bytes=64) for tag in (last_gelu_tag, "grouped2")]
-        for c in range(E):
+            turn_gated(c)
+            copy_shared(c)
+            copy_gated(c)
+        for c in range(1, E):
             for v in range(2):
-                nc.vector.tensor_tensor(
-                    windows[v][:].indirect(chunk_offsets(c, c + 1)),
-                    summands[c][:, ROUTED, v, :],
-                    summands[c][:, SHARED, v, :],
-                    ADD,
-                )
+                scatter(c, v)
         for v in range(2):
             nc.sync.dma_start(out[v * P : (v + 1) * P, :], windows[v][:])

@@ -27,10 +27,10 @@ WARM_PASSES = 5
 CODE_BUFFERS = 4
 
 UNITS = ((0, ROUTED), (0, SHARED), (1, SHARED), (1, ROUTED), (2, SHARED), (2, ROUTED), (3, SHARED), (3, ROUTED))
-A_BANK = (0, 2, 4, 5, 1, 4, 5, 7)
+A_BANK = (0, 2, 4, 5, 1, 4, 5, 1)
 B_BANK = (1, 3, 0, 6, 2, 3, 0, 6)
-TURN_BANK = (1, 4, 5, 7)
-RESULT_BANK = (1, 2, 3, 0)
+TURN_BANK = (7, 4, 5, 7)
+RESULT_BANK = (7, 2, 3, 0)
 GATED_BANK = (None, 4, 5, 6)
 
 
@@ -81,9 +81,9 @@ def tile_moe_shr_glu_gelu_kernel(
         identity = keep.tile([P, P], F32, name="identity")
         make_identity(nc, identity[:])
 
-        def load_scales(plane, scales):
+        def load_scales(plane, scales, rows=range(4)):
             source = scales[:, 0].rearrange("e (q r) i -> r q e i", r=4)
-            for r in range(4):
+            for r in rows:
                 nc.sync.dma_start(
                     plane[:].bitcast(I32)[r:P:32, :].rearrange("q (e i) -> q e i", e=MATRICES), source[r].bitcast(I32)
                 )
@@ -98,12 +98,24 @@ def tile_moe_shr_glu_gelu_kernel(
         nc.sync.dma_start(offsets[:], offs)
         for d in range(1, 4):
             nc.sync.dma_start(x_plane(d), x_rows[:, d, :])
-        w1_first = keep.tile([P, 2 * 2 * H], U8, name="w1_first", align_bytes=64)
-        w3_first = keep.tile([P, 2 * 2 * H], U8, name="w3_first", align_bytes=64)
-        load_words(w1_first, w1_words, slice(0, MATRICES, E), 2)
-        load_scales(w1s, w1_scales)
-        load_words(w3_first, w3_words, slice(0, MATRICES, E), 2)
+        w1w, w3w = {}, {}
+
+        def load_matrices(words, source, experts):
+            members = range(experts.start, experts.stop, experts.step)
+            tile = keep.tile([P, len(members) * 2 * H], U8, name="words%d" % (len(w1w) + len(w3w)), align_bytes=64)
+            load_words(tile, source, experts, len(members))
+            for n, e in enumerate(members):
+                words[e] = tile[:, n * 2 * H : (n + 1) * 2 * H]
+
+        load_scales(w1s, w1_scales, range(2))
+        load_matrices(w1w, w1_words, slice(0, MATRICES, E))
+        load_scales(w1s, w1_scales, range(2, 4))
+        load_matrices(w3w, w3_words, slice(0, 1, 1))
         load_scales(w3s, w3_scales)
+        load_matrices(w3w, w3_words, slice(1, MATRICES, E - 1))
+        load_matrices(w1w, w1_words, slice(1, 2, 1))
+        load_matrices(w1w, w1_words, slice(2, E, 1))
+        load_matrices(w3w, w3_words, slice(2, E, 1))
 
         x_pairs = [keep.tile([P, T, 2], BF16, name="x_pairs%d" % u) for u in range(2)]
         x_codes, x_scales = {}, {}
@@ -148,21 +160,29 @@ def tile_moe_shr_glu_gelu_kernel(
         cast_pairs(1)
         gather_half(1, 0)
         quantise_chunk(0, "x_codes0")
+        halves = {}
+
+        def gather_run(c, u):
+            if u == 0:
+                halves[c] = keep.tile([P, 2 * C], U32, name="halves", tag="slot_words%d" % (c % 2), align_bytes=64)
+            gather_pairs(halves[c][:, u * C : (u + 1) * C], c, c + 1, u)
+
+        def weave(c, tag):
+            slot_words[c] = keep.tile([P, 2 * C], U32, name="woven", tag=tag, align_bytes=64)
+            nc.scalar.copy(
+                slot_words[c][:].rearrange("p (s u) -> p s u", u=2), halves[c][:].rearrange("p (u s) -> p s u", u=2)
+            )
+
         new_slot_words(2)
         gather_half(2, 0)
         gather_half(1, 1)
         gather_half(2, 1)
         quantise_chunk(1, "x_codes1")
         quantise_chunk(2, "x_codes2")
-        new_slot_words(3)
-        gather_half(3, 0)
-        gather_half(3, 1)
+        gather_run(3, 0)
+        gather_run(3, 1)
 
-        w1_late = keep.tile([P, (E - 1) * 2 * H], U8, name="w1_late", align_bytes=64)
-        w3_late = keep.tile([P, (E - 1) * 2 * H], U8, name="w3_late", align_bytes=64)
         w2w = keep.tile([P, MATRICES * 2 * N], U8, name="w2w", align_bytes=64)
-        load_words(w1_late, w1_words, slice(1, E), E - 1)
-        load_words(w3_late, w3_words, slice(1, E), E - 1)
         load_words(w2w, w2_words, slice(0, MATRICES), MATRICES)
         load_scales(w2s, w2_scales)
         gate_rows = keep.tile([P, C], F32, name="gate_rows")
@@ -173,18 +193,14 @@ def tile_moe_shr_glu_gelu_kernel(
 
         hidden, grouped, h_codes, results = {}, {}, {}, {}
 
-        def project(c, kind, first_words, late_words, scales, bank):
+        def project(c, kind, words, scales, bank):
             e = (c, E)[kind]
-            if e in (0, E):
-                words = first_words[:, (e // E) * 2 * H : (e // E + 1) * 2 * H]
-            else:
-                words = late_words[:, (e - 1) * 2 * H : e * 2 * H]
             sums = psum.tile([P, H], F32, name="sums", tag="bank%d" % bank)
             nc.tensor.matmul_mx(
                 out=sums[:],
                 lhsT=x_codes[c].bitcast(FP8X4),
                 lhsT_scale=x_scales[c],
-                rhs=words.bitcast(FP4X4),
+                rhs=words[e].bitcast(FP4X4),
                 rhs_scale=scales[:, e * H : (e + 1) * H],
                 start=True,
                 stop=True,
@@ -194,10 +210,10 @@ def tile_moe_shr_glu_gelu_kernel(
         a_sums, b_sums, gelus = {}, {}, {}
 
         def a_pass(i):
-            a_sums[i] = project(*UNITS[i], w1_first, w1_late, w1s, A_BANK[i])
+            a_sums[i] = project(*UNITS[i], w1w, w1s, A_BANK[i])
 
         def b_pass(i):
-            b_sums[i] = project(*UNITS[i], w3_first, w3_late, w3s, B_BANK[i])
+            b_sums[i] = project(*UNITS[i], w3w, w3s, B_BANK[i])
 
         def gelu(i):
             gelus[i] = keep.tile([P, 2, P, 2], F32, name="gelu%d" % i, align_bytes=64)
@@ -286,14 +302,15 @@ def tile_moe_shr_glu_gelu_kernel(
                 nc.tensor.transpose(gated_turned[c][:, v, :], gated[c][:, v, :], identity[:])
 
         def copy_gated(c):
-            routed_part[c] = keep.tile([P, 2, C], F32, name="routed_part%d" % c, align_bytes=64)
+            tag = "hidden3" if c == 1 else "routed_part%d" % c
+            routed_part[c] = keep.tile([P, 2, C], F32, name="routed_part", tag=tag, align_bytes=64)
             nc.scalar.copy(routed_part[c][:], gated_turned[c][:])
 
         windows = {}
 
         def scatter(c, v):
             if v not in windows:
-                windows[v] = keep.tile([P, T], F32, name="window", tag=("gelu7", "grouped2")[v], align_bytes=64)
+                windows[v] = keep.tile([P, T], F32, name="window", tag=("grouped1", "grouped2")[v], align_bytes=64)
             nc.vector.tensor_tensor(
                 windows[v][:].indirect(chunk_offsets(c, c + 1)), routed_part[c][:, v, :], shared_part[c][:, v, :], ADD
             )
@@ -312,30 +329,31 @@ def tile_moe_shr_glu_gelu_kernel(
         b_pass(3)
         product(0)
         a_pass(4)
+        weave(3, "gelu0")
         product(1)
-        quantise_chunk(3, "gelu0")
+        quantise_chunk(3, "x_codes3")
         gelu(4)
         a_pass(5)
         b_pass(4)
         product(2)
         gelu(5)
+        turn(0)
+        group(0)
         a_pass(6)
         b_pass(5)
         product(3)
         gelu(6)
-        turn(0)
-        group(0)
         a_pass(7)
-        b_pass(6)
         product(4)
+        quantise_hidden(0)
+        b_pass(6)
         b_pass(7)
+        last_layer(0)
         gelu(7)
         product(5)
         turn(1)
         group(1)
         product(6)
-        quantise_hidden(0)
-        last_layer(0)
         product(7)
         quantise_hidden(1)
         copy_shared(0)

@@ -29,9 +29,9 @@ CODE_BUFFERS = 4
 UNITS = ((0, ROUTED), (0, SHARED), (1, SHARED), (1, ROUTED), (2, SHARED), (2, ROUTED), (3, SHARED), (3, ROUTED))
 A_BANK = (0, 2, 4, 5, 1, 4, 5, 1)
 B_BANK = (1, 3, 0, 6, 2, 3, 0, 6)
-TURN_BANK = (7, 4, 5, 7)
-RESULT_BANK = (7, 2, 3, 0)
-GATED_BANK = (None, 4, 5, 6)
+TURN_BANK = (7, 4, 5, 5)
+RESULT_BANKS = ((3, 7), (2,), (3,), (3,))
+GATED_BANKS = (None, (4, 0), (7, 1), (5, 4))
 
 
 def tile_moe_shr_glu_gelu_kernel(
@@ -236,14 +236,15 @@ def tile_moe_shr_glu_gelu_kernel(
                     nc.tensor.transpose(turned[c][:, kind, u, :], words[:, start : start + P], identity[:])
 
         def group(c):
-            grouped[c] = keep.tile([P, 2, C, 4], BF16, name="grouped%d" % c, align_bytes=64)
+            tag = "h_codes0" if c == 2 else "grouped%d" % c
+            grouped[c] = keep.tile([P, 2, C, 4], BF16, name="grouped", tag=tag, align_bytes=64)
             nc.scalar.copy(
                 grouped[c][:].rearrange("p k s d -> p (k s d)").bitcast(F32).rearrange("p (k s u) -> p k s u", k=2, u=2),
                 turned[c][:].rearrange("p k u s -> p k s u"),
             )
 
         def quantise_hidden(c):
-            codes = work.tile([P, 2 * C], U32, name="h_codes", align_bytes=64)
+            codes = keep.tile([P, 2 * C], U32, name="h_codes%d" % c, align_bytes=64)
             scales = work.tile([P, 2 * C], U8, name="h_scales", align_bytes=64)
             nc.vector.quantize_mx(
                 out=codes[:].bitcast(FP8X4), scales=scales[:], in_=grouped[c][:].rearrange("p k s d -> p (k s d)")
@@ -252,14 +253,18 @@ def tile_moe_shr_glu_gelu_kernel(
                 h_codes[c, kind] = (codes[:, kind * C : (kind + 1) * C], scales[:, kind * C : (kind + 1) * C])
 
         def last_layer(c):
-            y = psum.tile([P, 2, 2, C], F32, name="y", tag="bank%d" % RESULT_BANK[c])
+            if len(RESULT_BANKS[c]) == 2:
+                y = [psum.tile([P, 2, C], F32, name="y", tag="bank%d" % bank)[:] for bank in RESULT_BANKS[c]]
+            else:
+                both = psum.tile([P, 2, 2, C], F32, name="y", tag="bank%d" % RESULT_BANKS[c][0])
+                y = [both[:, ROUTED], both[:, SHARED]]
             results[c] = y
             for kind in (ROUTED, SHARED):
                 e = (c, E)[kind]
                 codes, scales = h_codes[c, kind]
                 if kind == ROUTED and c > 0:
                     nc.tensor.matmul_mx(
-                        out=y[:, ROUTED].rearrange("p v s -> p (v s)"),
+                        out=y[ROUTED].rearrange("p v s -> p (v s)"),
                         lhsT=codes.bitcast(FP8X4),
                         lhsT_scale=scales,
                         rhs=w2w[:, 2 * e * N : 2 * (e + 1) * N].bitcast(FP4X4),
@@ -271,7 +276,7 @@ def tile_moe_shr_glu_gelu_kernel(
                 for v in range(2):
                     column = e * N + v * P
                     nc.tensor.matmul_mx(
-                        out=y[:, kind, v, :],
+                        out=y[kind][:, v, :],
                         lhsT=w2w[:, 2 * column : 2 * (column + P)].bitcast(FP4X4),
                         lhsT_scale=w2s[:, column : column + P],
                         rhs=codes.bitcast(FP8X4),
@@ -284,33 +289,37 @@ def tile_moe_shr_glu_gelu_kernel(
 
         def copy_shared(c):
             shared_part[c] = keep.tile([P, 2, C], F32, name="shared_part%d" % c, align_bytes=64)
-            nc.scalar.copy(shared_part[c][:], results[c][:, SHARED])
+            nc.scalar.copy(shared_part[c][:], results[c][SHARED])
 
         def gate_on_vector(c):
             routed_part[c] = keep.tile([P, 2, C], F32, name="routed_part%d" % c, align_bytes=64)
             nc.vector.tensor_tensor(
-                routed_part[c][:], results[c][:, ROUTED], gate_rows[:].unsqueeze(1).to_broadcast([P, 2, C]), MULT
+                routed_part[c][:], results[c][ROUTED], gate_rows[:].unsqueeze(1).to_broadcast([P, 2, C]), MULT
             )
 
         def gate_on_scalar(c):
             gated[c] = work.tile([P, 2, P], F32, name="gated")
-            nc.scalar.activation(gated[c][:], results[c][:, ROUTED], COPY, scale=gate_columns[:, c - 1 : c])
+            for v in range(2):
+                nc.scalar.activation(
+                    gated[c][:, v, :], results[c][ROUTED][:, v, :], COPY, scale=gate_columns[:, c - 1 : c]
+                )
 
         def turn_gated(c):
-            gated_turned[c] = psum.tile([P, 2, C], F32, name="gated_turned", tag="bank%d" % GATED_BANK[c])
+            gated_turned[c] = [psum.tile([P, C], F32, name="gated_turned", tag="bank%d" % b) for b in GATED_BANKS[c]]
             for v in range(2):
-                nc.tensor.transpose(gated_turned[c][:, v, :], gated[c][:, v, :], identity[:])
+                nc.tensor.transpose(gated_turned[c][v][:], gated[c][:, v, :], identity[:])
 
         def copy_gated(c):
             tag = "hidden3" if c == 1 else "routed_part%d" % c
             routed_part[c] = keep.tile([P, 2, C], F32, name="routed_part", tag=tag, align_bytes=64)
-            nc.scalar.copy(routed_part[c][:], gated_turned[c][:])
+            for v in range(2):
+                nc.scalar.copy(routed_part[c][:, v, :], gated_turned[c][v][:])
 
         windows = {}
 
         def scatter(c, v):
             if v not in windows:
-                windows[v] = keep.tile([P, T], F32, name="window", tag=("grouped1", "grouped2")[v], align_bytes=64)
+                windows[v] = keep.tile([P, T], F32, name="window", tag=("gelu7", "h_codes0")[v], align_bytes=64)
             nc.vector.tensor_tensor(
                 windows[v][:].indirect(chunk_offsets(c, c + 1)), routed_part[c][:, v, :], shared_part[c][:, v, :], ADD
             )
@@ -356,10 +365,10 @@ def tile_moe_shr_glu_gelu_kernel(
         product(6)
         product(7)
         quantise_hidden(1)
-        copy_shared(0)
         gate_on_vector(0)
         turn(2)
         group(2)
+        copy_shared(0)
         last_layer(1)
         quantise_hidden(2)
         gate_on_scalar(1)

@@ -160,27 +160,15 @@ def tile_moe_shr_glu_gelu_kernel(
         cast_pairs(1)
         gather_half(1, 0)
         quantise_chunk(0, "x_codes0")
-        halves = {}
-
-        def gather_run(c, u):
-            if u == 0:
-                halves[c] = keep.tile([P, 2 * C], U32, name="halves", tag="slot_words%d" % (c % 2), align_bytes=64)
-            gather_pairs(halves[c][:, u * C : (u + 1) * C], c, c + 1, u)
-
-        def weave(c, tag):
-            slot_words[c] = keep.tile([P, 2 * C], U32, name="woven", tag=tag, align_bytes=64)
-            nc.scalar.copy(
-                slot_words[c][:].rearrange("p (s u) -> p s u", u=2), halves[c][:].rearrange("p (u s) -> p s u", u=2)
-            )
-
         new_slot_words(2)
         gather_half(2, 0)
         gather_half(1, 1)
         gather_half(2, 1)
         quantise_chunk(1, "x_codes1")
         quantise_chunk(2, "x_codes2")
-        gather_run(3, 0)
-        gather_run(3, 1)
+        new_slot_words(3)
+        gather_half(3, 0)
+        gather_half(3, 1)
 
         w2w = keep.tile([P, MATRICES * 2 * N], U8, name="w2w", align_bytes=64)
         load_words(w2w, w2_words, slice(0, MATRICES), MATRICES)
@@ -236,7 +224,7 @@ def tile_moe_shr_glu_gelu_kernel(
                     nc.tensor.transpose(turned[c][:, kind, u, :], words[:, start : start + P], identity[:])
 
         def group(c):
-            tag = "h_codes0" if c == 2 else "grouped%d" % c
+            tag = ("grouped0", "words6", "h_codes0", "grouped3")[c]
             grouped[c] = keep.tile([P, 2, C, 4], BF16, name="grouped", tag=tag, align_bytes=64)
             nc.scalar.copy(
                 grouped[c][:].rearrange("p k s d -> p (k s d)").bitcast(F32).rearrange("p (k s u) -> p k s u", k=2, u=2),
@@ -338,9 +326,8 @@ def tile_moe_shr_glu_gelu_kernel(
         b_pass(3)
         product(0)
         a_pass(4)
-        weave(3, "gelu0")
         product(1)
-        quantise_chunk(3, "x_codes3")
+        quantise_chunk(3, "gelu0")
         gelu(4)
         a_pass(5)
         b_pass(4)

@@ -23,7 +23,6 @@ P = 128
 MATRICES = E + 1
 ROUTED, SHARED = 0, 1
 LIST_COLUMNS = C // 16
-WARM_PASSES = 5
 CODE_BUFFERS = 4
 
 UNITS = ((0, ROUTED), (0, SHARED), (1, SHARED), (1, ROUTED), (2, SHARED), (2, ROUTED), (3, SHARED), (3, ROUTED))
@@ -50,8 +49,8 @@ def tile_moe_shr_glu_gelu_kernel(
         def x_plane(d):
             return x_half[d // 2][:, (d % 2) * T : (d % 2 + 1) * T]
 
-        zeros = keep.tile([P, 2 * T], BF16, name="zeros", align_bytes=64)
-        nc.vector.memset(zeros[:].bitcast(I32), 0)
+        zeros = keep.tile([P, 1], F32, name="zeros")
+        nc.vector.memset(zeros[:], 0.0)
         gelu_unread = keep.tile([P, 1], F32, name="gelu_unread")
         nc.scalar.activation(gelu_unread[:], zeros[:, 0:1], GELU)
 
@@ -61,22 +60,6 @@ def tile_moe_shr_glu_gelu_kernel(
         nc.gpsimd.memset(w1s[:].bitcast(I32), 0)
         nc.vector.memset(w3s[:].bitcast(I32), 0)
         nc.vector.memset(w2s[:].bitcast(I32), 0)
-
-        zero_codes = keep.tile([P, T], U32, name="zero_codes", align_bytes=64)
-        zero_scales = keep.tile([P, T], U8, name="zero_scales", align_bytes=64)
-        for columns in (slice(0, T // 2), slice(T // 2, T)):
-            nc.vector.quantize_mx(out=zero_codes[:, columns].bitcast(FP8X4), scales=zero_scales[:, columns], in_=zeros[:])
-        passes_unread = psum.tile([P, T], F32, name="passes_unread", tag="bank7")
-        for repeat in range(WARM_PASSES):
-            nc.tensor.matmul_mx(
-                out=passes_unread[:],
-                lhsT=zero_codes[:, :P].bitcast(FP8X4),
-                lhsT_scale=zero_scales[:, :P],
-                rhs=zero_codes[:, : T // 2].bitcast(U8).bitcast(FP4X4),
-                rhs_scale=zero_scales[:],
-                start=True,
-                stop=True,
-            )
 
         identity = keep.tile([P, P], F32, name="identity")
         make_identity(nc, identity[:])

@@ -23,14 +23,19 @@ P = 128
 MATRICES = E + 1
 ROUTED, SHARED = 0, 1
 LIST_COLUMNS = C // 16
-CODE_BUFFERS = 4
 
 UNITS = ((0, ROUTED), (0, SHARED), (1, SHARED), (1, ROUTED), (2, SHARED), (2, ROUTED), (3, SHARED), (3, ROUTED))
 A_BANK = (0, 2, 4, 5, 1, 4, 5, 1)
 B_BANK = (1, 3, 0, 6, 2, 3, 0, 6)
+X_CODE_TAGS = ("x_codes0", "x_codes1", "x_codes2", "gelu0")
+WARM_PASSES = 4
 TURN_BANK = (7, 4, 5, 5)
-RESULT_BANKS = ((3, 7), (2,), (3,), (3,))
-GATED_BANKS = (None, (4, 0), (7, 1), (5, 4))
+RESULT_BANKS = ((3, 7), (2, 0), (3, 1), (7, 4))
+H_CODE_TAGS = ("h_codes0", "h_codes1", "h_codes2", "h_codes3")
+SUM_TAGS = ("hidden6", "summed1", "summed2", "summed3")
+SHARED_TAGS = (None, "hidden6", "shared_part2", "shared_part3")
+GATED_TAGS = ("gated0", "gated1", "gated2", "gated3")
+GROUP_TAGS = ("grouped0", "words6", "h_codes0", "grouped3")
 
 
 def tile_moe_shr_glu_gelu_kernel(
@@ -39,7 +44,6 @@ def tile_moe_shr_glu_gelu_kernel(
     nc = tc.nc
     with ExitStack() as ctx:
         keep = ctx.enter_context(tc.tile_pool(name="keep", bufs=1))
-        work = ctx.enter_context(tc.tile_pool(name="work", bufs=CODE_BUFFERS))
         psum = ctx.enter_context(tc.psum_pool(name="psum", bufs=1))
 
         offsets = keep.tile([P, T // 16], U16, name="offsets")
@@ -49,15 +53,16 @@ def tile_moe_shr_glu_gelu_kernel(
         def x_plane(d):
             return x_half[d // 2][:, (d % 2) * T : (d % 2 + 1) * T]
 
+        w1s = keep.tile([P, MATRICES * H], U8, name="w1s", align_bytes=64)
+        w3s = keep.tile([P, MATRICES * H], U8, name="w3s", align_bytes=64)
+        w2s = keep.tile([P, MATRICES * N], U8, name="w2s", align_bytes=64)
+        nc.gpsimd.memset(w1s[:].bitcast(I32), 0)
+
         zeros = keep.tile([P, 1], F32, name="zeros")
         nc.vector.memset(zeros[:], 0.0)
         gelu_unread = keep.tile([P, 1], F32, name="gelu_unread")
         nc.scalar.activation(gelu_unread[:], zeros[:, 0:1], GELU)
 
-        w1s = keep.tile([P, MATRICES * H], U8, name="w1s", align_bytes=64)
-        w3s = keep.tile([P, MATRICES * H], U8, name="w3s", align_bytes=64)
-        w2s = keep.tile([P, MATRICES * N], U8, name="w2s", align_bytes=64)
-        nc.gpsimd.memset(w1s[:].bitcast(I32), 0)
         nc.vector.memset(w3s[:].bitcast(I32), 0)
         nc.vector.memset(w2s[:].bitcast(I32), 0)
 
@@ -77,10 +82,6 @@ def tile_moe_shr_glu_gelu_kernel(
                 words[experts, 0].rearrange("e p b -> p e b").bitcast(I32),
             )
 
-        nc.sync.dma_start(x_plane(0), x_rows[:, 0, :])
-        nc.sync.dma_start(offsets[:], offs)
-        for d in range(1, 4):
-            nc.sync.dma_start(x_plane(d), x_rows[:, d, :])
         w1w, w3w = {}, {}
 
         def load_matrices(words, source, experts):
@@ -90,6 +91,10 @@ def tile_moe_shr_glu_gelu_kernel(
             for n, e in enumerate(members):
                 words[e] = tile[:, n * 2 * H : (n + 1) * 2 * H]
 
+        nc.sync.dma_start(x_plane(0), x_rows[:, 0, :])
+        nc.sync.dma_start(offsets[:], offs)
+        for d in range(1, 4):
+            nc.sync.dma_start(x_plane(d), x_rows[:, d, :])
         load_scales(w1s, w1_scales, range(2))
         load_matrices(w1w, w1_words, slice(0, MATRICES, E))
         load_scales(w1s, w1_scales, range(2, 4))
@@ -99,78 +104,83 @@ def tile_moe_shr_glu_gelu_kernel(
         load_matrices(w1w, w1_words, slice(1, 2, 1))
         load_matrices(w1w, w1_words, slice(2, E, 1))
         load_matrices(w3w, w3_words, slice(2, E, 1))
+        w2w = keep.tile([P, MATRICES * 2 * N], U8, name="w2w", align_bytes=64)
+        load_words(w2w, w2_words, slice(0, MATRICES), MATRICES)
+        load_scales(w2s, w2_scales)
+        gate_rows = keep.tile([P, T], F32, name="gate_rows")
+        nc.sync.dma_start(gate_rows[:], gate[0:P, :])
+
+        def chunk_offsets(c):
+            return offsets[:, LIST_COLUMNS * c : LIST_COLUMNS * (c + 1)]
 
         x_pairs = [keep.tile([P, T, 2], BF16, name="x_pairs%d" % u) for u in range(2)]
-        x_codes, x_scales = {}, {}
-
-        def chunk_offsets(first, end):
-            return offsets[:, LIST_COLUMNS * first : LIST_COLUMNS * end]
+        slot_words, x_codes, x_scales = {}, {}, {}
 
         def cast_pairs(u):
             nc.scalar.copy(x_pairs[u][:], x_half[u][:].rearrange("p (e t) -> p t e", e=2))
 
-        def gather_pairs(out_words, first, end, u):
-            window = x_pairs[u][:].rearrange("p t e -> p (t e)").bitcast(U32)
-            nc.vector.tensor_copy(out_words, window.indirect(chunk_offsets(first, end)))
-
-        def quantise_tokens(first, end, values, tag):
-            codes = keep.tile([P, (end - first) * C], U32, name="x_codes", tag=tag, align_bytes=64)
-            scales = keep.tile([P, (end - first) * C], U8, name="x_scales%d" % first, align_bytes=64)
-            nc.vector.quantize_mx(out=codes[:].bitcast(FP8X4), scales=scales[:], in_=values)
-            for c in range(first, end):
-                x_codes[c] = codes[:, (c - first) * C : (c - first + 1) * C]
-                x_scales[c] = scales[:, (c - first) * C : (c - first + 1) * C]
-
-        slot_words = {}
-
         def new_slot_words(c):
             slot_words[c] = keep.tile([P, 2 * C], U32, name="slot_words", tag="slot_words%d" % (c % 2), align_bytes=64)
 
-        def gather_half(c, u):
-            gather_pairs(slot_words[c][:].rearrange("p (s u) -> p s u", u=2)[:, :, u], c, c + 1, u)
+        def gather_pairs(c, u):
+            window = x_pairs[u][:].rearrange("p t e -> p (t e)").bitcast(U32)
+            words = slot_words[c][:].rearrange("p (s u) -> p s u", u=2)[:, :, u]
+            nc.vector.tensor_copy(words, window.indirect(chunk_offsets(c)))
 
-        def quantise_chunk(c, tag):
-            quantise_tokens(c, c + 1, slot_words[c][:].bitcast(BF16), tag)
+        def quantise_tokens(c):
+            x_codes[c] = keep.tile([P, C], U32, name="x_codes", tag=X_CODE_TAGS[c], align_bytes=64)
+            x_scales[c] = keep.tile([P, C], U8, name="x_scales%d" % c, align_bytes=64)
+            nc.vector.quantize_mx(
+                out=x_codes[c][:].bitcast(FP8X4), scales=x_scales[c][:], in_=slot_words[c][:].bitcast(BF16)
+            )
+
+        warm_values = keep.tile([P, T], BF16, name="warm_values", align_bytes=64)
+        warm_codes = keep.tile([P, 2 * C], U32, name="warm_codes", align_bytes=64)
+        warm_scales = keep.tile([P, 2 * C], U8, name="warm_scales", align_bytes=64)
+        nc.scalar.copy(warm_values[:], x_plane(0))
+        for n in range(2):
+            columns = slice(n * C, (n + 1) * C)
+            nc.vector.quantize_mx(out=warm_codes[:, columns].bitcast(FP8X4), scales=warm_scales[:, columns], in_=warm_values[:])
+        warm_unread = psum.tile([P, 2 * C], F32, name="warm_unread", tag="bank7")
+        for n in range(WARM_PASSES):
+            nc.tensor.matmul_mx(
+                out=warm_unread[:],
+                lhsT=warm_codes[:, C:].bitcast(FP8X4),
+                lhsT_scale=warm_scales[:, C:],
+                rhs=warm_codes[:, :C].bitcast(U8).bitcast(FP4X4),
+                rhs_scale=warm_scales[:],
+                start=True,
+                stop=True,
+            )
 
         new_slot_words(0)
         new_slot_words(1)
-        chunk0_values = slot_words[0][:].bitcast(BF16)
+        chunk0_values = slot_words[0][:].bitcast(BF16).rearrange("p (s d) -> p s d", d=4)
         cast_pairs(0)
         for d in range(4):
-            nc.vector.tensor_copy(
-                chunk0_values.rearrange("p (s d) -> p s d", d=4)[:, :, d], x_plane(d).indirect(chunk_offsets(0, 1))
-            )
+            nc.vector.tensor_copy(chunk0_values[:, :, d], x_plane(d).indirect(chunk_offsets(0)))
         cast_pairs(1)
-        gather_half(1, 0)
-        quantise_chunk(0, "x_codes0")
+        gather_pairs(1, 0)
+        quantise_tokens(0)
         new_slot_words(2)
-        gather_half(2, 0)
-        gather_half(1, 1)
-        gather_half(2, 1)
-        quantise_chunk(1, "x_codes1")
-        quantise_chunk(2, "x_codes2")
+        gather_pairs(2, 0)
+        gather_pairs(1, 1)
+        gather_pairs(2, 1)
+        quantise_tokens(1)
+        quantise_tokens(2)
         new_slot_words(3)
-        gather_half(3, 0)
-        gather_half(3, 1)
+        gather_pairs(3, 0)
+        gather_pairs(3, 1)
 
-        w2w = keep.tile([P, MATRICES * 2 * N], U8, name="w2w", align_bytes=64)
-        load_words(w2w, w2_words, slice(0, MATRICES), MATRICES)
-        load_scales(w2s, w2_scales)
-        gate_rows = keep.tile([P, C], F32, name="gate_rows")
-        nc.sync.dma_start(gate_rows[:], gate[0:P, 0:C])
-        gate_columns = keep.tile([P, E - 1], F32, name="gate_columns")
-        with nc.allow_non_contiguous_dma(reason="one gate value a partition"):
-            nc.sync.dma_start(gate_columns[:], gate[0, C:].rearrange("(c p) -> p c", p=P))
-
-        hidden, grouped, h_codes, results = {}, {}, {}, {}
+        hidden, grouped, h_codes = {}, {}, {}
 
         def project(c, kind, words, scales, bank):
             e = (c, E)[kind]
             sums = psum.tile([P, H], F32, name="sums", tag="bank%d" % bank)
             nc.tensor.matmul_mx(
                 out=sums[:],
-                lhsT=x_codes[c].bitcast(FP8X4),
-                lhsT_scale=x_scales[c],
+                lhsT=x_codes[c][:].bitcast(FP8X4),
+                lhsT_scale=x_scales[c][:],
                 rhs=words[e].bitcast(FP4X4),
                 rhs_scale=scales[:, e * H : (e + 1) * H],
                 start=True,
@@ -191,109 +201,96 @@ def tile_moe_shr_glu_gelu_kernel(
             nc.scalar.activation(gelus[i][:], a_sums[i], GELU)
 
         def product(i):
-            c, kind = UNITS[i]
-            if c not in hidden:
-                hidden[c] = keep.tile([P, 2, 2, P, 2], BF16, name="hidden%d" % c, align_bytes=64)
-            nc.vector.tensor_tensor(hidden[c][:, kind], gelus[i][:], b_sums[i], MULT)
+            hidden[UNITS[i]] = keep.tile([P, 2, P, 2], BF16, name="hidden%d" % i, align_bytes=64)
+            nc.vector.tensor_tensor(hidden[UNITS[i]][:], gelus[i][:], b_sums[i], MULT)
 
         turned = {}
 
         def turn(c):
             turned[c] = psum.tile([P, 2, 2, C], F32, name="turned", tag="bank%d" % TURN_BANK[c])
-            words = hidden[c][:].rearrange("s k u q e -> s (k u q e)").bitcast(F32)
             for kind in (ROUTED, SHARED):
+                words = hidden[c, kind][:].rearrange("s u q e -> s (u q e)").bitcast(F32)
                 for u in range(2):
-                    start = (2 * kind + u) * P
-                    nc.tensor.transpose(turned[c][:, kind, u, :], words[:, start : start + P], identity[:])
+                    nc.tensor.transpose(turned[c][:, kind, u, :], words[:, u * P : (u + 1) * P], identity[:])
 
         def group(c):
-            tag = ("grouped0", "words6", "h_codes0", "grouped3")[c]
-            grouped[c] = keep.tile([P, 2, C, 4], BF16, name="grouped", tag=tag, align_bytes=64)
+            grouped[c] = keep.tile([P, 2, C, 4], BF16, name="grouped", tag=GROUP_TAGS[c], align_bytes=64)
             nc.scalar.copy(
                 grouped[c][:].rearrange("p k s d -> p (k s d)").bitcast(F32).rearrange("p (k s u) -> p k s u", k=2, u=2),
                 turned[c][:].rearrange("p k u s -> p k s u"),
             )
 
         def quantise_hidden(c):
-            codes = keep.tile([P, 2 * C], U32, name="h_codes%d" % c, align_bytes=64)
-            scales = work.tile([P, 2 * C], U8, name="h_scales", align_bytes=64)
+            codes = keep.tile([P, 2 * C], U32, name="h_codes", tag=H_CODE_TAGS[c], align_bytes=64)
+            scales = keep.tile([P, 2 * C], U8, name="h_scales%d" % c, align_bytes=64)
             nc.vector.quantize_mx(
                 out=codes[:].bitcast(FP8X4), scales=scales[:], in_=grouped[c][:].rearrange("p k s d -> p (k s d)")
             )
             for kind in (ROUTED, SHARED):
                 h_codes[c, kind] = (codes[:, kind * C : (kind + 1) * C], scales[:, kind * C : (kind + 1) * C])
 
-        def last_layer(c):
-            if len(RESULT_BANKS[c]) == 2:
-                y = [psum.tile([P, 2, C], F32, name="y", tag="bank%d" % bank)[:] for bank in RESULT_BANKS[c]]
-            else:
-                both = psum.tile([P, 2, 2, C], F32, name="y", tag="bank%d" % RESULT_BANKS[c][0])
-                y = [both[:, ROUTED], both[:, SHARED]]
-            results[c] = y
-            for kind in (ROUTED, SHARED):
-                e = (c, E)[kind]
-                codes, scales = h_codes[c, kind]
-                if kind == ROUTED and c > 0:
-                    nc.tensor.matmul_mx(
-                        out=y[ROUTED].rearrange("p v s -> p (v s)"),
-                        lhsT=codes.bitcast(FP8X4),
-                        lhsT_scale=scales,
-                        rhs=w2w[:, 2 * e * N : 2 * (e + 1) * N].bitcast(FP4X4),
-                        rhs_scale=w2s[:, e * N : (e + 1) * N],
-                        start=True,
-                        stop=True,
-                    )
-                    continue
-                for v in range(2):
-                    column = e * N + v * P
-                    nc.tensor.matmul_mx(
-                        out=y[kind][:, v, :],
-                        lhsT=w2w[:, 2 * column : 2 * (column + P)].bitcast(FP4X4),
-                        lhsT_scale=w2s[:, column : column + P],
-                        rhs=codes.bitcast(FP8X4),
-                        rhs_scale=scales,
-                        start=True,
-                        stop=True,
-                    )
+        y, ys = {}, {}
 
-        gated, gated_turned, routed_part, shared_part = {}, {}, {}, {}
+        def last_pass(result, c, kind, v):
+            column = (c, E)[kind] * N + v * P
+            codes, scales = h_codes[c, kind]
+            nc.tensor.matmul_mx(
+                out=result,
+                lhsT=w2w[:, 2 * column : 2 * (column + P)].bitcast(FP4X4),
+                lhsT_scale=w2s[:, column : column + P],
+                rhs=codes.bitcast(FP8X4),
+                rhs_scale=scales,
+                start=True,
+                stop=True,
+            )
+
+        def last_layer(c):
+            vector_bank, scalar_bank = RESULT_BANKS[c]
+            mine = psum.tile([P, 3, C], F32, name="result", tag="bank%d" % vector_bank)
+            other = psum.tile([P, 2, C], F32, name="result", tag="bank%d" % scalar_bank)
+            y[c] = mine[:, 0:2, :]
+            ys[c] = other[:]
+            ys[c, 0] = other[:, 0, :]
+            ys[c, 1] = other[:, 1, :]
+            for v in range(2):
+                last_pass(y[c][:, v, :], c, ROUTED, v)
+            for v in (1, 0):
+                last_pass(ys[c, v], c, SHARED, v)
+
+        gated, summed, shared_part = {}, {}, {}
+
+        def apply_gate(c):
+            gated[c] = keep.tile([P, 2, C], F32, name="gated", tag=GATED_TAGS[c], align_bytes=64)
+            weights = gate_rows[:, c * C : (c + 1) * C].unsqueeze(1).to_broadcast([P, 2, C])
+            nc.vector.tensor_tensor(gated[c][:], y[c], weights, MULT)
+
+        def add_both(c):
+            both = keep.tile([P, 2, C], F32, name="summed", tag=SUM_TAGS[c], align_bytes=64)
+            nc.vector.tensor_tensor(both[:], gated[c][:], ys[c], ADD)
+            summed[c, 0], summed[c, 1] = both[:, 0, :], both[:, 1, :]
+
+        def add_half(c, v):
+            if (c, v) == (0, 1):
+                early = keep.tile([P, 2, C], F32, name="early_sums", tag="hidden7", align_bytes=64)
+                summed[0, 1], summed[1, 1] = early[:, 0, :], early[:, 1, :]
+            if (c, v) not in summed:
+                summed[c, v] = keep.tile([P, C], F32, name="summed%d" % c, align_bytes=64)[:]
+            nc.vector.tensor_tensor(summed[c, v], gated[c][:, v, :], ys[c, v], ADD)
 
         def copy_shared(c):
-            shared_part[c] = keep.tile([P, 2, C], F32, name="shared_part%d" % c, align_bytes=64)
-            nc.scalar.copy(shared_part[c][:], results[c][SHARED])
+            shared_part[c] = keep.tile([P, C], F32, name="shared_part", tag=SHARED_TAGS[c], align_bytes=64)
+            nc.scalar.copy(shared_part[c][:], ys[c, 0])
 
-        def gate_on_vector(c):
-            routed_part[c] = keep.tile([P, 2, C], F32, name="routed_part%d" % c, align_bytes=64)
-            nc.vector.tensor_tensor(
-                routed_part[c][:], results[c][ROUTED], gate_rows[:].unsqueeze(1).to_broadcast([P, 2, C]), MULT
-            )
+        windows = [keep.tile([P, T], F32, name="window%d" % v, align_bytes=64) for v in range(2)]
 
-        def gate_on_scalar(c):
-            gated[c] = work.tile([P, 2, P], F32, name="gated")
-            for v in range(2):
-                nc.scalar.activation(
-                    gated[c][:, v, :], results[c][ROUTED][:, v, :], COPY, scale=gate_columns[:, c - 1 : c]
-                )
+        def scatter_on_scalar(c, v):
+            nc.scalar.activation(windows[v][:].indirect(chunk_offsets(c)), summed[c, v], COPY)
 
-        def turn_gated(c):
-            gated_turned[c] = [psum.tile([P, C], F32, name="gated_turned", tag="bank%d" % b) for b in GATED_BANKS[c]]
-            for v in range(2):
-                nc.tensor.transpose(gated_turned[c][v][:], gated[c][:, v, :], identity[:])
+        def copy_scatter_on_vector(c):
+            nc.vector.tensor_copy(windows[0][:].indirect(chunk_offsets(c)), summed[c, 0])
 
-        def copy_gated(c):
-            tag = "hidden3" if c == 1 else "routed_part%d" % c
-            routed_part[c] = keep.tile([P, 2, C], F32, name="routed_part", tag=tag, align_bytes=64)
-            for v in range(2):
-                nc.scalar.copy(routed_part[c][:, v, :], gated_turned[c][v][:])
-
-        windows = {}
-
-        def scatter(c, v):
-            if v not in windows:
-                windows[v] = keep.tile([P, T], F32, name="window", tag=("gelu7", "h_codes0")[v], align_bytes=64)
-            nc.vector.tensor_tensor(
-                windows[v][:].indirect(chunk_offsets(c, c + 1)), routed_part[c][:, v, :], shared_part[c][:, v, :], ADD
-            )
+        def scatter_on_vector(c):
+            nc.vector.tensor_tensor(windows[0][:].indirect(chunk_offsets(c)), gated[c][:, 0, :], shared_part[c][:], ADD)
 
         a_pass(0)
         a_pass(1)
@@ -310,7 +307,7 @@ def tile_moe_shr_glu_gelu_kernel(
         product(0)
         a_pass(4)
         product(1)
-        quantise_chunk(3, "gelu0")
+        quantise_tokens(3)
         gelu(4)
         a_pass(5)
         b_pass(4)
@@ -335,29 +332,30 @@ def tile_moe_shr_glu_gelu_kernel(
         product(6)
         product(7)
         quantise_hidden(1)
-        gate_on_vector(0)
+        apply_gate(0)
         turn(2)
         group(2)
-        copy_shared(0)
         last_layer(1)
         quantise_hidden(2)
-        gate_on_scalar(1)
         turn(3)
         group(3)
-        turn_gated(1)
-        copy_shared(1)
-        copy_gated(1)
-        scatter(0, 0)
+        apply_gate(1)
+        last_layer(2)
+        add_both(0)
+        scatter_on_scalar(0, 0)
+        scatter_on_scalar(0, 1)
         quantise_hidden(3)
-        scatter(0, 1)
-        for c in range(2, E):
-            last_layer(c)
-            gate_on_scalar(c)
-            turn_gated(c)
-            copy_shared(c)
-            copy_gated(c)
-        for c in range(1, E):
-            for v in range(2):
-                scatter(c, v)
+        last_layer(3)
+        apply_gate(2)
+        add_both(1)
+        scatter_on_scalar(1, 1)
+        add_both(2)
+        apply_gate(3)
+        add_both(3)
+        copy_scatter_on_vector(1)
+        scatter_on_scalar(2, 1)
+        copy_scatter_on_vector(2)
+        scatter_on_scalar(3, 1)
+        copy_scatter_on_vector(3)
         for v in range(2):
             nc.sync.dma_start(out[v * P : (v + 1) * P, :], windows[v][:])

@@ -34,7 +34,7 @@ RESULT_BANKS = ((3, 7), (2, 0), (3, 1), (7, 4))
 H_CODE_TAGS = ("h_codes0", "h_codes1", "h_codes2", "h_codes3")
 SUM_TAGS = ("hidden6", "summed1", "summed2", "summed3")
 SHARED_TAGS = (None, "hidden6", "shared_part2", "shared_part3")
-GATED_TAGS = ("gated0", "gated1", "gated2", "gated3")
+GATED_TAGS = ("gated0", "gated1", "hidden7", "gated3")
 GROUP_TAGS = ("grouped0", "words6", "h_codes0", "grouped3")
 
 
@@ -110,8 +110,8 @@ def tile_moe_shr_glu_gelu_kernel(
         gate_rows = keep.tile([P, T], F32, name="gate_rows")
         nc.sync.dma_start(gate_rows[:], gate[0:P, :])
 
-        def chunk_offsets(c):
-            return offsets[:, LIST_COLUMNS * c : LIST_COLUMNS * (c + 1)]
+        def chunk_offsets(c, count=1):
+            return offsets[:, LIST_COLUMNS * c : LIST_COLUMNS * (c + count)]
 
         x_pairs = [keep.tile([P, T, 2], BF16, name="x_pairs%d" % u) for u in range(2)]
         slot_words, x_codes, x_scales = {}, {}, {}
@@ -265,9 +265,9 @@ def tile_moe_shr_glu_gelu_kernel(
             nc.vector.tensor_tensor(gated[c][:], y[c], weights, MULT)
 
         def add_both(c):
-            both = keep.tile([P, 2, C], F32, name="summed", tag=SUM_TAGS[c], align_bytes=64)
-            nc.vector.tensor_tensor(both[:], gated[c][:], ys[c], ADD)
-            summed[c, 0], summed[c, 1] = both[:, 0, :], both[:, 1, :]
+            if c % 2 == 0:
+                summed[c // 2] = keep.tile([P, 2, 2 * C], F32, name="summed", tag=SUM_TAGS[c], align_bytes=64)
+            nc.vector.tensor_tensor(summed[c // 2][:, :, (c % 2) * C : (c % 2 + 1) * C], gated[c][:], ys[c], ADD)
 
         def add_half(c, v):
             if (c, v) == (0, 1):
@@ -283,11 +283,14 @@ def tile_moe_shr_glu_gelu_kernel(
 
         windows = [keep.tile([P, T], F32, name="window%d" % v, align_bytes=64) for v in range(2)]
 
-        def scatter_on_scalar(c, v):
-            nc.scalar.activation(windows[v][:].indirect(chunk_offsets(c)), summed[c, v], COPY)
+        def sums(c, count, v):
+            return summed[c // 2][:, v, (c % 2) * C : (c % 2 + count) * C]
 
-        def copy_scatter_on_vector(c):
-            nc.vector.tensor_copy(windows[0][:].indirect(chunk_offsets(c)), summed[c, 0])
+        def scatter_on_scalar(c, count, v):
+            nc.scalar.activation(windows[v][:].indirect(chunk_offsets(c, count)), sums(c, count, v), COPY)
+
+        def copy_scatter_on_vector(c, count):
+            nc.vector.tensor_copy(windows[0][:].indirect(chunk_offsets(c, count)), sums(c, count, 0))
 
         def scatter_on_vector(c):
             nc.vector.tensor_tensor(windows[0][:].indirect(chunk_offsets(c)), gated[c][:, 0, :], shared_part[c][:], ADD)
@@ -342,20 +345,17 @@ def tile_moe_shr_glu_gelu_kernel(
         apply_gate(1)
         last_layer(2)
         add_both(0)
-        scatter_on_scalar(0, 0)
-        scatter_on_scalar(0, 1)
+        add_both(1)
+        apply_gate(2)
         quantise_hidden(3)
         last_layer(3)
-        apply_gate(2)
-        add_both(1)
-        scatter_on_scalar(1, 1)
-        add_both(2)
+        scatter_on_scalar(0, 2, 1)
+        copy_scatter_on_vector(0, 1)
+        scatter_on_scalar(1, 1, 0)
         apply_gate(3)
+        add_both(2)
         add_both(3)
-        copy_scatter_on_vector(1)
-        scatter_on_scalar(2, 1)
-        copy_scatter_on_vector(2)
-        scatter_on_scalar(3, 1)
-        copy_scatter_on_vector(3)
+        copy_scatter_on_vector(2, 2)
+        scatter_on_scalar(2, 2, 1)
         for v in range(2):
             nc.sync.dma_start(out[v * P : (v + 1) * P, :], windows[v][:])

@@ -27,7 +27,7 @@ LIST_COLUMNS = C // 16
 UNITS = ((0, ROUTED), (0, SHARED), (1, SHARED), (1, ROUTED), (2, SHARED), (2, ROUTED), (3, SHARED), (3, ROUTED))
 A_BANK = (0, 2, 4, 5, 1, 4, 5, 1)
 B_BANK = (1, 3, 0, 6, 2, 3, 0, 6)
-X_CODE_TAGS = ("x_codes0", "x_codes1", "x_codes2", "gelu0")
+X_CODE_TAGS = ("x_codes0", "x_codes1", "x_codes2", "x_codes3")
 WARM_PASSES = 4
 TURN_BANK = (7, 4, 5, 5)
 RESULT_BANKS = ((3, 7), (2, 0), (3, 1), (7, 4))
@@ -48,15 +48,16 @@ def tile_moe_shr_glu_gelu_kernel(
 
         offsets = keep.tile([P, T // 16], U16, name="offsets")
         x_rows = xT.rearrange("(p d) t -> p d t", d=4)
-        x_half = [keep.tile([P, 2 * T], F32, name="x_half%d" % u) for u in range(2)]
+        x_planes = [keep.tile([P, T], F32, name="x_plane%d" % d) for d in range(4)]
 
         def x_plane(d):
-            return x_half[d // 2][:, (d % 2) * T : (d % 2 + 1) * T]
+            return x_planes[d][:]
 
         w1s = keep.tile([P, MATRICES * H], U8, name="w1s", align_bytes=64)
         w3s = keep.tile([P, MATRICES * H], U8, name="w3s", align_bytes=64)
         w2s = keep.tile([P, MATRICES * N], U8, name="w2s", align_bytes=64)
-        nc.gpsimd.memset(w1s[:].bitcast(I32), 0)
+        nc.vector.memset(w1s[:].bitcast(I32), 0)
+        nc.gpsimd.memset(w2s[:].bitcast(I32), 0)
 
         zeros = keep.tile([P, 1], F32, name="zeros")
         nc.vector.memset(zeros[:], 0.0)
@@ -64,7 +65,6 @@ def tile_moe_shr_glu_gelu_kernel(
         nc.scalar.activation(gelu_unread[:], zeros[:, 0:1], GELU)
 
         nc.vector.memset(w3s[:].bitcast(I32), 0)
-        nc.vector.memset(w2s[:].bitcast(I32), 0)
 
         identity = keep.tile([P, P], F32, name="identity")
         make_identity(nc, identity[:])
@@ -95,9 +95,8 @@ def tile_moe_shr_glu_gelu_kernel(
         nc.sync.dma_start(offsets[:], offs)
         for d in range(1, 4):
             nc.sync.dma_start(x_plane(d), x_rows[:, d, :])
-        load_scales(w1s, w1_scales, range(2))
+        load_scales(w1s, w1_scales)
         load_matrices(w1w, w1_words, slice(0, MATRICES, E))
-        load_scales(w1s, w1_scales, range(2, 4))
         load_matrices(w3w, w3_words, slice(0, 1, 1))
         load_scales(w3s, w3_scales)
         load_matrices(w3w, w3_words, slice(1, MATRICES, E - 1))
@@ -113,25 +112,29 @@ def tile_moe_shr_glu_gelu_kernel(
         def chunk_offsets(c, count=1):
             return offsets[:, LIST_COLUMNS * c : LIST_COLUMNS * (c + count)]
 
-        x_pairs = [keep.tile([P, T, 2], BF16, name="x_pairs%d" % u) for u in range(2)]
-        slot_words, x_codes, x_scales = {}, {}, {}
+        gathered = {c: keep.tile([P, 4, C], F32, name="gathered%d" % c, align_bytes=64) for c in range(1, E)}
+        woven = [keep.tile([P, C, 4], BF16, name="woven%d" % c, align_bytes=64) for c in range(E)]
+        x_codes, x_scales = {}, {}
 
-        def cast_pairs(u):
-            nc.scalar.copy(x_pairs[u][:], x_half[u][:].rearrange("p (e t) -> p t e", e=2))
+        def gather_woven(c, d):
+            nc.vector.tensor_copy(woven[c][:, :, d], x_plane(d).indirect(chunk_offsets(c)))
 
-        def new_slot_words(c):
-            slot_words[c] = keep.tile([P, 2 * C], U32, name="slot_words", tag="slot_words%d" % (c % 2), align_bytes=64)
+        def gather_on_vector(c, d):
+            nc.vector.tensor_copy(gathered[c][:, d, :], x_plane(d).indirect(chunk_offsets(c)))
 
-        def gather_pairs(c, u):
-            window = x_pairs[u][:].rearrange("p t e -> p (t e)").bitcast(U32)
-            words = slot_words[c][:].rearrange("p (s u) -> p s u", u=2)[:, :, u]
-            nc.vector.tensor_copy(words, window.indirect(chunk_offsets(c)))
+        def gather_on_scalar(c, d):
+            nc.scalar.activation(gathered[c][:, d, :], x_plane(d).indirect(chunk_offsets(c)), COPY)
+
+        def weave(c):
+            nc.vector.tensor_copy(
+                woven[c][:].rearrange("p (s i) d -> p s d i", i=4), gathered[c][:].rearrange("p d (s i) -> p s d i", i=4)
+            )
 
         def quantise_tokens(c):
             x_codes[c] = keep.tile([P, C], U32, name="x_codes", tag=X_CODE_TAGS[c], align_bytes=64)
             x_scales[c] = keep.tile([P, C], U8, name="x_scales%d" % c, align_bytes=64)
             nc.vector.quantize_mx(
-                out=x_codes[c][:].bitcast(FP8X4), scales=x_scales[c][:], in_=slot_words[c][:].bitcast(BF16)
+                out=x_codes[c][:].bitcast(FP8X4), scales=x_scales[c][:], in_=woven[c][:].rearrange("p s d -> p (s d)")
             )
 
         warm_values = keep.tile([P, T], BF16, name="warm_values", align_bytes=64)
@@ -153,24 +156,18 @@ def tile_moe_shr_glu_gelu_kernel(
                 stop=True,
             )
 
-        new_slot_words(0)
-        new_slot_words(1)
-        chunk0_values = slot_words[0][:].bitcast(BF16).rearrange("p (s d) -> p s d", d=4)
-        cast_pairs(0)
         for d in range(4):
-            nc.vector.tensor_copy(chunk0_values[:, :, d], x_plane(d).indirect(chunk_offsets(0)))
-        cast_pairs(1)
-        gather_pairs(1, 0)
+            gather_woven(0, d)
+            gather_on_vector(1, d)
+            gather_on_scalar(2, d)
+            gather_on_scalar(3, d)
         quantise_tokens(0)
-        new_slot_words(2)
-        gather_pairs(2, 0)
-        gather_pairs(1, 1)
-        gather_pairs(2, 1)
+        weave(1)
+        weave(2)
         quantise_tokens(1)
+        weave(3)
         quantise_tokens(2)
-        new_slot_words(3)
-        gather_pairs(3, 0)
-        gather_pairs(3, 1)
+        quantise_tokens(3)
 
         hidden, grouped, h_codes = {}, {}, {}
 
@@ -310,7 +307,6 @@ def tile_moe_shr_glu_gelu_kernel(
         product(0)
         a_pass(4)
         product(1)
-        quantise_tokens(3)
         gelu(4)
         a_pass(5)
         b_pass(4)

@@ -137,13 +137,14 @@ def tile_moe_shr_glu_gelu_kernel(
                 out=x_codes[c][:].bitcast(FP8X4), scales=x_scales[c][:], in_=woven[c][:].rearrange("p s d -> p (s d)")
             )
 
-        warm_values = keep.tile([P, T], BF16, name="warm_values", align_bytes=64)
+        warm_values = keep.tile([P, T + T // 2], BF16, name="warm_values", align_bytes=64)
         warm_codes = keep.tile([P, 2 * C], U32, name="warm_codes", align_bytes=64)
         warm_scales = keep.tile([P, 2 * C], U8, name="warm_scales", align_bytes=64)
-        nc.scalar.copy(warm_values[:], x_plane(0))
+        nc.scalar.copy(warm_values[:, :T], x_plane(0))
+        nc.scalar.copy(warm_values[:, T:], x_plane(1)[:, : T // 2])
         for n in range(2):
             columns = slice(n * C, (n + 1) * C)
-            nc.vector.quantize_mx(out=warm_codes[:, columns].bitcast(FP8X4), scales=warm_scales[:, columns], in_=warm_values[:])
+            nc.vector.quantize_mx(out=warm_codes[:, columns].bitcast(FP8X4), scales=warm_scales[:, columns], in_=warm_values[:, n * T // 2 : n * T // 2 + T])
         warm_unread = psum.tile([P, 2 * C], F32, name="warm_unread", tag="bank7")
         for n in range(WARM_PASSES):
             nc.tensor.matmul_mx(

@@ -35,7 +35,7 @@ H_CODE_TAGS = ("h_codes0", "h_codes1", "h_codes2", "h_codes3")
 SUM_TAGS = ("hidden6", "summed1", "summed2", "summed3")
 SHARED_TAGS = (None, "hidden6", "shared_part2", "shared_part3")
 GATED_TAGS = ("gated0", "gated1", "hidden7", "gated3")
-GROUP_TAGS = ("grouped0", "words6", "h_codes0", "grouped3")
+GROUP_TAGS = ("grouped0", "w1_words2", "h_codes0", "grouped3")
 
 
 def tile_moe_shr_glu_gelu_kernel(
@@ -48,7 +48,8 @@ def tile_moe_shr_glu_gelu_kernel(
 
         offsets = keep.tile([P, T // 16], U16, name="offsets")
         x_rows = xT.rearrange("(p d) t -> p d t", d=4)
-        x_planes = [keep.tile([P, T], F32, name="x_plane%d" % d) for d in range(4)]
+        x_planes = [keep.tile([P, T if d else 6 * C], F32, name="x_plane%d" % d) for d in range(4)]
+        nc.gpsimd.memset(x_planes[0][:, T:], 0.0)
 
         def x_plane(d):
             return x_planes[d][:]
@@ -86,12 +87,13 @@ def tile_moe_shr_glu_gelu_kernel(
 
         def load_matrices(words, source, experts):
             members = range(experts.start, experts.stop, experts.step)
-            tile = keep.tile([P, len(members) * 2 * H], U8, name="words%d" % (len(w1w) + len(w3w)), align_bytes=64)
+            name = "w%d_words%d" % (1 if words is w1w else 3, experts.start)
+            tile = keep.tile([P, len(members) * 2 * H], U8, name=name, align_bytes=64)
             load_words(tile, source, experts, len(members))
             for n, e in enumerate(members):
                 words[e] = tile[:, n * 2 * H : (n + 1) * 2 * H]
 
-        nc.sync.dma_start(x_plane(0), x_rows[:, 0, :])
+        nc.sync.dma_start(x_plane(0)[:, :T], x_rows[:, 0, :])
         nc.sync.dma_start(offsets[:], offs)
         for d in range(1, 4):
             nc.sync.dma_start(x_plane(d), x_rows[:, d, :])
@@ -112,7 +114,7 @@ def tile_moe_shr_glu_gelu_kernel(
         def chunk_offsets(c, count=1):
             return offsets[:, LIST_COLUMNS * c : LIST_COLUMNS * (c + count)]
 
-        gathered = {c: keep.tile([P, 4, C], F32, name="gathered%d" % c, align_bytes=64) for c in range(1, E)}
+        gathered = keep.tile([P, 4, T - C], BF16, name="gathered", align_bytes=64)
         woven = [keep.tile([P, C, 4], BF16, name="woven%d" % c, align_bytes=64) for c in range(E)]
         x_codes, x_scales = {}, {}
 
@@ -120,14 +122,15 @@ def tile_moe_shr_glu_gelu_kernel(
             nc.vector.tensor_copy(woven[c][:, :, d], x_plane(d).indirect(chunk_offsets(c)))
 
         def gather_on_vector(c, d):
-            nc.vector.tensor_copy(gathered[c][:, d, :], x_plane(d).indirect(chunk_offsets(c)))
+            nc.vector.tensor_copy(gathered[:, d, (c - 1) * C : c * C], x_plane(d).indirect(chunk_offsets(c)))
 
         def gather_on_scalar(c, d):
-            nc.scalar.activation(gathered[c][:, d, :], x_plane(d).indirect(chunk_offsets(c)), COPY)
+            nc.scalar.activation(gathered[:, d, (c - 1) * C :], x_plane(d).indirect(chunk_offsets(c, E - c)), COPY)
 
         def weave(c):
             nc.vector.tensor_copy(
-                woven[c][:].rearrange("p (s i) d -> p s d i", i=4), gathered[c][:].rearrange("p d (s i) -> p s d i", i=4)
+                woven[c][:].rearrange("p (s i) d -> p s d i", i=4),
+                gathered[:, :, (c - 1) * C : c * C].rearrange("p d (s i) -> p s d i", i=4),
             )
 
         def quantise_tokens(c):
@@ -137,31 +140,36 @@ def tile_moe_shr_glu_gelu_kernel(
                 out=x_codes[c][:].bitcast(FP8X4), scales=x_scales[c][:], in_=woven[c][:].rearrange("p s d -> p (s d)")
             )
 
-        warm_values = keep.tile([P, T + T // 2], BF16, name="warm_values", align_bytes=64)
-        warm_codes = keep.tile([P, 2 * C], U32, name="warm_codes", align_bytes=64)
-        warm_scales = keep.tile([P, 2 * C], U8, name="warm_scales", align_bytes=64)
-        nc.scalar.copy(warm_values[:, :T], x_plane(0))
-        nc.scalar.copy(warm_values[:, T:], x_plane(1)[:, : T // 2])
-        for n in range(2):
-            columns = slice(n * C, (n + 1) * C)
-            nc.vector.quantize_mx(out=warm_codes[:, columns].bitcast(FP8X4), scales=warm_scales[:, columns], in_=warm_values[:, n * T // 2 : n * T // 2 + T])
-        warm_unread = psum.tile([P, 2 * C], F32, name="warm_unread", tag="bank7")
-        for n in range(WARM_PASSES):
-            nc.tensor.matmul_mx(
-                out=warm_unread[:],
-                lhsT=warm_codes[:, C:].bitcast(FP8X4),
-                lhsT_scale=warm_scales[:, C:],
-                rhs=warm_codes[:, :C].bitcast(U8).bitcast(FP4X4),
-                rhs_scale=warm_scales[:],
-                start=True,
-                stop=True,
-            )
+        def warm_up():
+            warm_codes = keep.tile([P, C], U32, name="warm_codes", align_bytes=64)
+            warm_scales = keep.tile([P, C], U8, name="warm_scales", align_bytes=64)
+            for n in range(2):
+                columns = slice(n * C // 2, (n + 1) * C // 2)
+                nc.vector.quantize_mx(
+                    out=warm_codes[:, columns].bitcast(FP8X4), scales=warm_scales[:, columns], in_=gathered[:, 0, n * C : (n + 2) * C]
+                )
+            warm_unread = psum.tile([P, 2 * C], F32, name="warm_unread", tag="bank7")
+            for n in range(WARM_PASSES):
+                nc.tensor.matmul_mx(
+                    out=warm_unread[:],
+                    lhsT=warm_codes[:].bitcast(FP8X4),
+                    lhsT_scale=warm_scales[:],
+                    rhs=warm_codes[:].bitcast(U8).bitcast(FP4X4),
+                    rhs_scale=warm_codes[:].bitcast(U8)[:, : 2 * C],
+                    start=True,
+                    stop=True,
+                )
 
-        for d in range(4):
+        gather_woven(0, 0)
+        gather_on_scalar(1, 0)
+        gather_woven(0, 1)
+        gather_on_vector(1, 1)
+        warm_up()
+        for d in range(2, 4):
             gather_woven(0, d)
             gather_on_vector(1, d)
+        for d in range(1, 4):
             gather_on_scalar(2, d)
-            gather_on_scalar(3, d)
         quantise_tokens(0)
         weave(1)
         weave(2)

@@ -29,13 +29,12 @@ A_BANK = (0, 2, 4, 5, 1, 4, 5, 1)
 B_BANK = (1, 3, 0, 6, 2, 3, 0, 6)
 X_CODE_TAGS = ("x_codes0", "x_codes1", "x_codes2", "x_codes3")
 WARM_PASSES = 4
-TURN_BANK = (7, 4, 5, 5)
+TURN_BANK = (7, 4, 5, 6)
 RESULT_BANKS = ((3, 7), (2, 0), (3, 1), (7, 4))
 H_CODE_TAGS = ("h_codes0", "h_codes1", "h_codes2", "h_codes3")
-SUM_TAGS = ("hidden6", "summed1", "summed2", "summed3")
-SHARED_TAGS = (None, "hidden6", "shared_part2", "shared_part3")
+SUM_TAG = "hidden6"
 GATED_TAGS = ("gated0", "gated1", "hidden7", "gated3")
-GROUP_TAGS = ("grouped0", "w1_words2", "h_codes0", "grouped3")
+GROUP_TAGS = ("grouped0", "w1_words2", "grouped2", "grouped3")
 
 
 def tile_moe_shr_glu_gelu_kernel(
@@ -143,11 +142,8 @@ def tile_moe_shr_glu_gelu_kernel(
         def warm_up():
             warm_codes = keep.tile([P, C], U32, name="warm_codes", align_bytes=64)
             warm_scales = keep.tile([P, C], U8, name="warm_scales", align_bytes=64)
-            for n in range(2):
-                columns = slice(n * C // 2, (n + 1) * C // 2)
-                nc.vector.quantize_mx(
-                    out=warm_codes[:, columns].bitcast(FP8X4), scales=warm_scales[:, columns], in_=gathered[:, 0, n * C : (n + 2) * C]
-                )
+            values = gathered[:].rearrange("p d s -> p (d s)")[:, T - C : 2 * T - C]
+            nc.vector.quantize_mx(out=warm_codes[:].bitcast(FP8X4), scales=warm_scales[:], in_=values)
             warm_unread = psum.tile([P, 2 * C], F32, name="warm_unread", tag="bank7")
             for n in range(WARM_PASSES):
                 nc.tensor.matmul_mx(
@@ -164,11 +160,13 @@ def tile_moe_shr_glu_gelu_kernel(
         gather_on_scalar(1, 0)
         gather_woven(0, 1)
         gather_on_vector(1, 1)
+        gather_on_scalar(2, 1)
+        gather_on_vector(1, 2)
+        gather_woven(0, 2)
         warm_up()
+        gather_woven(0, 3)
+        gather_on_vector(1, 3)
         for d in range(2, 4):
-            gather_woven(0, d)
-            gather_on_vector(1, d)
-        for d in range(1, 4):
             gather_on_scalar(2, d)
         quantise_tokens(0)
         weave(1)
@@ -252,9 +250,9 @@ def tile_moe_shr_glu_gelu_kernel(
 
         def last_layer(c):
             vector_bank, scalar_bank = RESULT_BANKS[c]
-            mine = psum.tile([P, 3, C], F32, name="result", tag="bank%d" % vector_bank)
+            mine = psum.tile([P, 2, C], F32, name="result", tag="bank%d" % vector_bank)
             other = psum.tile([P, 2, C], F32, name="result", tag="bank%d" % scalar_bank)
-            y[c] = mine[:, 0:2, :]
+            y[c] = mine[:]
             ys[c] = other[:]
             ys[c, 0] = other[:, 0, :]
             ys[c, 1] = other[:, 1, :]
@@ -271,35 +269,20 @@ def tile_moe_shr_glu_gelu_kernel(
             nc.vector.tensor_tensor(gated[c][:], y[c], weights, MULT)
 
         def add_both(c):
-            if c % 2 == 0:
-                summed[c // 2] = keep.tile([P, 2, 2 * C], F32, name="summed", tag=SUM_TAGS[c], align_bytes=64)
-            nc.vector.tensor_tensor(summed[c // 2][:, :, (c % 2) * C : (c % 2 + 1) * C], gated[c][:], ys[c], ADD)
+            if c == 0:
+                summed[0] = keep.tile([P, 2, T], F32, name="summed", tag=SUM_TAG, align_bytes=64)
+            nc.vector.tensor_tensor(summed[0][:, :, c * C : (c + 1) * C], gated[c][:], ys[c], ADD)
 
         def add_half(c, v):
-            if (c, v) == (0, 1):
-                early = keep.tile([P, 2, C], F32, name="early_sums", tag="hidden7", align_bytes=64)
-                summed[0, 1], summed[1, 1] = early[:, 0, :], early[:, 1, :]
-            if (c, v) not in summed:
-                summed[c, v] = keep.tile([P, C], F32, name="summed%d" % c, align_bytes=64)[:]
-            nc.vector.tensor_tensor(summed[c, v], gated[c][:, v, :], ys[c, v], ADD)
-
-        def copy_shared(c):
-            shared_part[c] = keep.tile([P, C], F32, name="shared_part", tag=SHARED_TAGS[c], align_bytes=64)
-            nc.scalar.copy(shared_part[c][:], ys[c, 0])
+            nc.vector.tensor_tensor(summed[0][:, v, c * C : (c + 1) * C], gated[c][:, v, :], ys[c, v], ADD)
 
         windows = [keep.tile([P, T], F32, name="window%d" % v, align_bytes=64) for v in range(2)]
 
-        def sums(c, count, v):
-            return summed[c // 2][:, v, (c % 2) * C : (c % 2 + count) * C]
+        def scatter_on_scalar(first, last, v):
+            nc.scalar.activation(windows[v][:].indirect(offsets[:, first // 16 : last // 16]), summed[0][:, v, first:last], COPY)
 
-        def scatter_on_scalar(c, count, v):
-            nc.scalar.activation(windows[v][:].indirect(chunk_offsets(c, count)), sums(c, count, v), COPY)
-
-        def copy_scatter_on_vector(c, count):
-            nc.vector.tensor_copy(windows[0][:].indirect(chunk_offsets(c, count)), sums(c, count, 0))
-
-        def scatter_on_vector(c):
-            nc.vector.tensor_tensor(windows[0][:].indirect(chunk_offsets(c)), gated[c][:, 0, :], shared_part[c][:], ADD)
+        def copy_scatter_on_vector(first, last, v):
+            nc.vector.tensor_copy(windows[v][:].indirect(offsets[:, first // 16 : last // 16]), summed[0][:, v, first:last])
 
         a_pass(0)
         a_pass(1)
@@ -347,20 +330,21 @@ def tile_moe_shr_glu_gelu_kernel(
         quantise_hidden(2)
         turn(3)
         group(3)
+        add_both(0)
         apply_gate(1)
         last_layer(2)
-        add_both(0)
-        add_both(1)
-        apply_gate(2)
         quantise_hidden(3)
         last_layer(3)
-        scatter_on_scalar(0, 2, 1)
-        copy_scatter_on_vector(0, 1)
-        scatter_on_scalar(1, 1, 0)
+        add_both(1)
+        apply_gate(2)
         apply_gate(3)
         add_both(2)
-        add_both(3)
-        copy_scatter_on_vector(2, 2)
-        scatter_on_scalar(2, 2, 1)
+        add_half(3, 0)
+        add_half(3, 1)
+        scatter_on_scalar(0, C, 1)
+        scatter_on_scalar(0, 2 * C, 0)
+        copy_scatter_on_vector(C, 2 * C, 1)
+        copy_scatter_on_vector(2 * C, T, 0)
+        scatter_on_scalar(2 * C, T, 1)
         for v in range(2):
             nc.sync.dma_start(out[v * P : (v + 1) * P, :], windows[v][:])

@@ -24,17 +24,15 @@ MATRICES = E + 1
 ROUTED, SHARED = 0, 1
 LIST_COLUMNS = C // 16
 
-UNITS = ((0, ROUTED), (0, SHARED), (1, SHARED), (1, ROUTED), (2, SHARED), (2, ROUTED), (3, SHARED), (3, ROUTED))
+UNITS = ((0, ROUTED), (0, SHARED), (1, SHARED), (1, ROUTED), (2, ROUTED), (3, ROUTED), (2, SHARED), (3, SHARED))
+TURNED_PAIRS = ((0, 1), (3, 2), (4, 5))
 A_BANK = (0, 2, 4, 5, 1, 4, 5, 1)
 B_BANK = (1, 3, 0, 6, 2, 3, 0, 6)
-X_CODE_TAGS = ("x_codes0", "x_codes1", "x_codes2", "x_codes3")
 WARM_PASSES = 4
-TURN_BANK = (7, 4, 5, 6)
-RESULT_BANKS = ((3, 7), (2, 0), (3, 1), (7, 4))
-H_CODE_TAGS = ("h_codes0", "h_codes1", "h_codes2", "h_codes3")
-SUM_TAG = "hidden6"
-GATED_TAGS = ("gated0", "gated1", "hidden7", "gated3")
-GROUP_TAGS = ("grouped0", "w1_words2", "grouped2", "grouped3")
+TURN_BANK = (7, 5, 4)
+RESULT_BANKS = ((3, 7), (1, 3), (2, 0))
+GROUP_TAGS = ("grouped0", "w1_permuted", "grouped2")
+PERMUTED_TAGS = ("woven2", "woven3")
 
 
 def tile_moe_shr_glu_gelu_kernel(
@@ -47,7 +45,7 @@ def tile_moe_shr_glu_gelu_kernel(
 
         offsets = keep.tile([P, T // 16], U16, name="offsets")
         x_rows = xT.rearrange("(p d) t -> p d t", d=4)
-        x_planes = [keep.tile([P, T if d else 6 * C], F32, name="x_plane%d" % d) for d in range(4)]
+        x_planes = [keep.tile([P, T if d else 6 * C], F32, name="x_plane%d" % d, align_bytes=64) for d in range(4)]
         nc.gpsimd.memset(x_planes[0][:, T:], 0.0)
 
         def x_plane(d):
@@ -55,9 +53,7 @@ def tile_moe_shr_glu_gelu_kernel(
 
         w1s = keep.tile([P, MATRICES * H], U8, name="w1s", align_bytes=64)
         w3s = keep.tile([P, MATRICES * H], U8, name="w3s", align_bytes=64)
-        w2s = keep.tile([P, MATRICES * N], U8, name="w2s", align_bytes=64)
         nc.vector.memset(w1s[:].bitcast(I32), 0)
-        nc.gpsimd.memset(w2s[:].bitcast(I32), 0)
 
         zeros = keep.tile([P, 1], F32, name="zeros")
         nc.vector.memset(zeros[:], 0.0)
@@ -69,10 +65,10 @@ def tile_moe_shr_glu_gelu_kernel(
         identity = keep.tile([P, P], F32, name="identity")
         make_identity(nc, identity[:])
 
-        def load_scales(plane, scales, rows=range(4)):
+        def load_scales(plane, scales, queue=nc.sync):
             source = scales[:, 0].rearrange("e (q r) i -> r q e i", r=4)
-            for r in rows:
-                nc.sync.dma_start(
+            for r in range(4):
+                queue.dma_start(
                     plane[:].bitcast(I32)[r:P:32, :].rearrange("q (e i) -> q e i", e=MATRICES), source[r].bitcast(I32)
                 )
 
@@ -106,7 +102,6 @@ def tile_moe_shr_glu_gelu_kernel(
         load_matrices(w3w, w3_words, slice(2, E, 1))
         w2w = keep.tile([P, MATRICES * 2 * N], U8, name="w2w", align_bytes=64)
         load_words(w2w, w2_words, slice(0, MATRICES), MATRICES)
-        load_scales(w2s, w2_scales)
         gate_rows = keep.tile([P, T], F32, name="gate_rows")
         nc.sync.dma_start(gate_rows[:], gate[0:P, :])
 
@@ -133,7 +128,7 @@ def tile_moe_shr_glu_gelu_kernel(
             )
 
         def quantise_tokens(c):
-            x_codes[c] = keep.tile([P, C], U32, name="x_codes", tag=X_CODE_TAGS[c], align_bytes=64)
+            x_codes[c] = keep.tile([P, C], U32, name="x_codes", tag="x_codes%d" % c, align_bytes=64)
             x_scales[c] = keep.tile([P, C], U8, name="x_scales%d" % c, align_bytes=64)
             nc.vector.quantize_mx(
                 out=x_codes[c][:].bitcast(FP8X4), scales=x_scales[c][:], in_=woven[c][:].rearrange("p s d -> p (s d)")
@@ -169,6 +164,9 @@ def tile_moe_shr_glu_gelu_kernel(
         for d in range(2, 4):
             gather_on_scalar(2, d)
         quantise_tokens(0)
+        w2s = keep.tile([P, MATRICES * N], U8, name="w2s", tag="x_plane2", align_bytes=64)
+        nc.gpsimd.memset(w2s[:].bitcast(I32), 0)
+        load_scales(w2s, w2_scales, nc.scalar)
         weave(1)
         weave(2)
         quantise_tokens(1)
@@ -176,113 +174,152 @@ def tile_moe_shr_glu_gelu_kernel(
         quantise_tokens(2)
         quantise_tokens(3)
 
-        hidden, grouped, h_codes = {}, {}, {}
+        permuted = {}
 
-        def project(c, kind, words, scales, bank):
-            e = (c, E)[kind]
-            sums = psum.tile([P, H], F32, name="sums", tag="bank%d" % bank)
-            nc.tensor.matmul_mx(
-                out=sums[:],
-                lhsT=x_codes[c][:].bitcast(FP8X4),
-                lhsT_scale=x_scales[c][:],
-                rhs=words[e].bitcast(FP4X4),
-                rhs_scale=scales[:, e * H : (e + 1) * H],
-                start=True,
-                stop=True,
+        def permute(name, words, scales, tag):
+            new_words = keep.tile([P, 2 * H], U8, name="new_words", tag=name + "_permuted", align_bytes=64)
+            new_scales = keep.tile([P, H], U8, name="new_scales", tag=tag, align_bytes=64)
+            nc.gpsimd.tensor_copy(
+                new_scales[:].rearrange("p (d m) -> p d m", d=4),
+                scales[:, E * H :].rearrange("p (m d) -> p d m", d=4),
             )
-            return sums[:].rearrange("s (q u e) -> s u q e", u=2, e=2)
+            nc.gpsimd.tensor_copy(
+                new_words[:].rearrange("p (d m b) -> p d m b", d=4, b=2),
+                words[E].rearrange("p (m d b) -> p d m b", d=4, b=2),
+            )
+            permuted[name] = (new_words, new_scales)
 
-        a_sums, b_sums, gelus = {}, {}, {}
+        permute("w1", w1w, w1s, PERMUTED_TAGS[0])
+        permute("w3", w3w, w3s, PERMUTED_TAGS[1])
+
+        def project(i, name, words, scales, bank):
+            c, kind = UNITS[i]
+            sums = psum.tile([P, H], F32, name="sums", tag="bank%d" % bank)
+            if i < 6:
+                e = (c, E)[kind]
+                nc.tensor.matmul_mx(
+                    out=sums[:],
+                    lhsT=x_codes[c][:].bitcast(FP8X4),
+                    lhsT_scale=x_scales[c][:],
+                    rhs=words[e].bitcast(FP4X4),
+                    rhs_scale=scales[:, e * H : (e + 1) * H],
+                    start=True,
+                    stop=True,
+                )
+                return sums[:].rearrange("s (q u e) -> s u q e", u=2, e=2)
+            new_words, new_scales = permuted[name]
+            for d in range(4):
+                nc.tensor.matmul_mx(
+                    out=sums[:, d * C : (d + 1) * C],
+                    lhsT=new_words[:, 2 * d * P : 2 * (d + 1) * P].bitcast(FP4X4),
+                    lhsT_scale=new_scales[:, d * P : (d + 1) * P],
+                    rhs=x_codes[c][:].bitcast(FP8X4),
+                    rhs_scale=x_scales[c][:],
+                    start=True,
+                    stop=True,
+                )
+            return sums[:].rearrange("p (d s) -> p s d", d=4)
+
+        a_sums, b_sums, gelus, hidden, turned, grouped, h_codes = {}, {}, {}, {}, {}, {}, {}
 
         def a_pass(i):
-            a_sums[i] = project(*UNITS[i], w1w, w1s, A_BANK[i])
+            a_sums[i] = project(i, "w1", w1w, w1s, A_BANK[i])
 
         def b_pass(i):
-            b_sums[i] = project(*UNITS[i], w3w, w3s, B_BANK[i])
+            b_sums[i] = project(i, "w3", w3w, w3s, B_BANK[i])
 
         def gelu(i):
-            gelus[i] = keep.tile([P, 2, P, 2], F32, name="gelu%d" % i, align_bytes=64)
+            gelus[i] = keep.tile([P, 2, P, 2] if i < 6 else [P, C, 4], F32, name="gelu%d" % i, align_bytes=64)
             nc.scalar.activation(gelus[i][:], a_sums[i], GELU)
 
+        grouped[3] = keep.tile([P, 2, C, 4], BF16, name="grouped3", align_bytes=64)
+
         def product(i):
-            hidden[UNITS[i]] = keep.tile([P, 2, P, 2], BF16, name="hidden%d" % i, align_bytes=64)
-            nc.vector.tensor_tensor(hidden[UNITS[i]][:], gelus[i][:], b_sums[i], MULT)
+            if i < 6:
+                hidden[i] = keep.tile([P, 2, P, 2], BF16, name="hidden%d" % i, align_bytes=64)[:]
+            else:
+                hidden[i] = grouped[3][:, i - 6]
+            nc.vector.tensor_tensor(hidden[i], gelus[i][:], b_sums[i], MULT)
 
-        turned = {}
-
-        def turn(c):
-            turned[c] = psum.tile([P, 2, 2, C], F32, name="turned", tag="bank%d" % TURN_BANK[c])
-            for kind in (ROUTED, SHARED):
-                words = hidden[c, kind][:].rearrange("s u q e -> s (u q e)").bitcast(F32)
+        def turn(n):
+            turned[n] = psum.tile([P, 2, 2, C], F32, name="turned", tag="bank%d" % TURN_BANK[n])
+            for k, i in enumerate(TURNED_PAIRS[n]):
+                words = hidden[i].rearrange("s u q e -> s (u q e)").bitcast(F32)
                 for u in range(2):
-                    nc.tensor.transpose(turned[c][:, kind, u, :], words[:, u * P : (u + 1) * P], identity[:])
+                    nc.tensor.transpose(turned[n][:, k, u, :], words[:, u * P : (u + 1) * P], identity[:])
 
-        def group(c):
-            grouped[c] = keep.tile([P, 2, C, 4], BF16, name="grouped", tag=GROUP_TAGS[c], align_bytes=64)
+        def group(n):
+            grouped[n] = keep.tile([P, 2, C, 4], BF16, name="grouped", tag=GROUP_TAGS[n], align_bytes=64)
             nc.scalar.copy(
-                grouped[c][:].rearrange("p k s d -> p (k s d)").bitcast(F32).rearrange("p (k s u) -> p k s u", k=2, u=2),
-                turned[c][:].rearrange("p k u s -> p k s u"),
+                grouped[n][:].rearrange("p k s d -> p (k s d)").bitcast(F32).rearrange("p (k s u) -> p k s u", k=2, u=2),
+                turned[n][:].rearrange("p k u s -> p k s u"),
             )
 
-        def quantise_hidden(c):
-            codes = keep.tile([P, 2 * C], U32, name="h_codes", tag=H_CODE_TAGS[c], align_bytes=64)
-            scales = keep.tile([P, 2 * C], U8, name="h_scales%d" % c, align_bytes=64)
+        def quantise_hidden(n):
+            codes = keep.tile([P, 2 * C], U32, name="h_codes%d" % n, align_bytes=64)
+            scales = keep.tile([P, 2 * C], U8, name="h_scales%d" % n, align_bytes=64)
             nc.vector.quantize_mx(
-                out=codes[:].bitcast(FP8X4), scales=scales[:], in_=grouped[c][:].rearrange("p k s d -> p (k s d)")
+                out=codes[:].bitcast(FP8X4), scales=scales[:], in_=grouped[n][:].rearrange("p k s d -> p (k s d)")
             )
-            for kind in (ROUTED, SHARED):
-                h_codes[c, kind] = (codes[:, kind * C : (kind + 1) * C], scales[:, kind * C : (kind + 1) * C])
+            h_codes[n] = (codes, scales)
 
-        y, ys = {}, {}
-
-        def last_pass(result, c, kind, v):
-            column = (c, E)[kind] * N + v * P
-            codes, scales = h_codes[c, kind]
+        def last_pass(result, e, v, n, first, last):
+            column = e * N + v * P
+            codes, scales = h_codes[n]
             nc.tensor.matmul_mx(
                 out=result,
                 lhsT=w2w[:, 2 * column : 2 * (column + P)].bitcast(FP4X4),
                 lhsT_scale=w2s[:, column : column + P],
-                rhs=codes.bitcast(FP8X4),
-                rhs_scale=scales,
+                rhs=codes[:, first:last].bitcast(FP8X4),
+                rhs_scale=scales[:, first:last],
                 start=True,
                 stop=True,
             )
 
+        y, ys, gated = {}, {}, {}
+        summed = keep.tile([P, 2, T], F32, name="summed", align_bytes=64)
+
         def last_layer(c):
-            vector_bank, scalar_bank = RESULT_BANKS[c]
-            mine = psum.tile([P, 2, C], F32, name="result", tag="bank%d" % vector_bank)
-            other = psum.tile([P, 2, C], F32, name="result", tag="bank%d" % scalar_bank)
-            y[c] = mine[:]
-            ys[c] = other[:]
-            ys[c, 0] = other[:, 0, :]
-            ys[c, 1] = other[:, 1, :]
+            y[c] = psum.tile([P, 2, C], F32, name="y", tag="bank%d" % RESULT_BANKS[c][0])
+            ys[c] = psum.tile([P, 2, C], F32, name="ys", tag="bank%d" % RESULT_BANKS[c][1])
             for v in range(2):
-                last_pass(y[c][:, v, :], c, ROUTED, v)
-            for v in (1, 0):
-                last_pass(ys[c, v], c, SHARED, v)
+                last_pass(y[c][:, v, :], c, v, c, 0, C)
+            for v in range(2):
+                last_pass(ys[c][:, v, :], E, v, c, C, 2 * C)
 
-        gated, summed, shared_part = {}, {}, {}
+        def last_routed():
+            y[2] = psum.tile([P, 2, 2 * C], F32, name="y", tag="bank%d" % RESULT_BANKS[2][0])
+            for k in range(2):
+                for v in range(2):
+                    last_pass(y[2][:, v, k * C : (k + 1) * C], 2 + k, v, 2, k * C, (k + 1) * C)
 
-        def apply_gate(c):
-            gated[c] = keep.tile([P, 2, C], F32, name="gated", tag=GATED_TAGS[c], align_bytes=64)
-            weights = gate_rows[:, c * C : (c + 1) * C].unsqueeze(1).to_broadcast([P, 2, C])
-            nc.vector.tensor_tensor(gated[c][:], y[c], weights, MULT)
+        def last_shared():
+            ys[2] = psum.tile([P, 2, 2 * C], F32, name="ys", tag="bank%d" % RESULT_BANKS[2][1])
+            for v in range(2):
+                last_pass(ys[2][:, v, :], E, v, 3, 0, 2 * C)
 
-        def add_both(c):
-            if c == 0:
-                summed[0] = keep.tile([P, 2, T], F32, name="summed", tag=SUM_TAG, align_bytes=64)
-            nc.vector.tensor_tensor(summed[0][:, :, c * C : (c + 1) * C], gated[c][:], ys[c], ADD)
+        def slots(n):
+            return slice(n * C, (n + 1) * C if n < 2 else T)
 
-        def add_half(c, v):
-            nc.vector.tensor_tensor(summed[0][:, v, c * C : (c + 1) * C], gated[c][:, v, :], ys[c, v], ADD)
+        def apply_gate(n):
+            width = C if n < 2 else 2 * C
+            gated[n] = keep.tile([P, 2, width], F32, name="gated%d" % n, align_bytes=64)
+            weights = gate_rows[:, slots(n)].unsqueeze(1).to_broadcast([P, 2, width])
+            nc.vector.tensor_tensor(gated[n][:], y[n][:], weights, MULT)
+
+        def add_both(n):
+            nc.vector.tensor_tensor(summed[:, :, slots(n)], gated[n][:], ys[n][:], ADD)
+
+        def add_half(n, v):
+            nc.vector.tensor_tensor(summed[:, v, slots(n)], gated[n][:, v, :], ys[n][:, v, :], ADD)
 
         windows = [keep.tile([P, T], F32, name="window%d" % v, align_bytes=64) for v in range(2)]
 
         def scatter_on_scalar(first, last, v):
-            nc.scalar.activation(windows[v][:].indirect(offsets[:, first // 16 : last // 16]), summed[0][:, v, first:last], COPY)
+            nc.scalar.activation(windows[v][:].indirect(offsets[:, first // 16 : last // 16]), summed[:, v, first:last], COPY)
 
         def copy_scatter_on_vector(first, last, v):
-            nc.vector.tensor_copy(windows[v][:].indirect(offsets[:, first // 16 : last // 16]), summed[0][:, v, first:last])
+            nc.vector.tensor_copy(windows[v][:].indirect(offsets[:, first // 16 : last // 16]), summed[:, v, first:last])
 
         a_pass(0)
         a_pass(1)
@@ -312,39 +349,35 @@ def tile_moe_shr_glu_gelu_kernel(
         gelu(6)
         a_pass(7)
         product(4)
-        quantise_hidden(0)
         b_pass(6)
         b_pass(7)
-        last_layer(0)
+        turn(1)
         gelu(7)
         product(5)
-        turn(1)
+        quantise_hidden(0)
+        last_layer(0)
+        turn(2)
         group(1)
         product(6)
-        product(7)
-        quantise_hidden(1)
-        apply_gate(0)
-        turn(2)
         group(2)
+        product(7)
+        apply_gate(0)
+        quantise_hidden(1)
         last_layer(1)
-        quantise_hidden(2)
-        turn(3)
-        group(3)
         add_both(0)
-        apply_gate(1)
-        last_layer(2)
+        quantise_hidden(2)
+        last_routed()
         quantise_hidden(3)
-        last_layer(3)
+        last_shared()
+        apply_gate(1)
         add_both(1)
         apply_gate(2)
-        apply_gate(3)
-        add_both(2)
-        add_half(3, 0)
-        add_half(3, 1)
+        add_half(2, 1)
+        add_half(2, 0)
+        scatter_on_scalar(0, C, 0)
         scatter_on_scalar(0, C, 1)
-        scatter_on_scalar(0, 2 * C, 0)
-        copy_scatter_on_vector(C, 2 * C, 1)
+        scatter_on_scalar(C, 2 * C, 0)
         copy_scatter_on_vector(2 * C, T, 0)
-        scatter_on_scalar(2 * C, T, 1)
-        for v in range(2):
-            nc.sync.dma_start(out[v * P : (v + 1) * P, :], windows[v][:])
+        scatter_on_scalar(C, T, 1)
+        nc.sync.dma_start(out[0:P, :], windows[0][:])
+        nc.scalar.dma_start(out[P : 2 * P, :], windows[1][:])

@@ -26,13 +26,15 @@ LIST_COLUMNS = C // 16
 
 UNITS = ((0, ROUTED), (0, SHARED), (1, SHARED), (1, ROUTED), (2, ROUTED), (3, ROUTED), (2, SHARED), (3, SHARED))
 TURNED_PAIRS = ((0, 1), (3, 2), (4, 5))
-A_BANK = (0, 2, 4, 5, 1, 4, 5, 1)
+A_BANK = (0, 2, 4, 5, 1, 4, 1, 4)
 B_BANK = (1, 3, 0, 6, 2, 3, 0, 6)
 WARM_PASSES = 4
-TURN_BANK = (7, 5, 4)
-RESULT_BANKS = ((3, 7), (1, 3), (2, 0))
-GROUP_TAGS = ("grouped0", "w1_permuted", "grouped2")
-PERMUTED_TAGS = ("woven2", "woven3")
+TURN_BANK = (7, 5, 2)
+RESULT_BANKS = ((3, 7), (1, 4), (5, 0))
+GROUP_TAGS = ("grouped0", "woven1", "grouped2")
+H_CODE_TAGS = ("h_codes0", "h_codes0", "gated0", "h_codes3")
+H_SCALE_TAGS = ("h_scales0", "h_scales1", "h_scales2", "h_scales0")
+PERMUTED_TAGS = (("gathered", "woven2"), ("woven1", "woven3"))
 
 
 def tile_moe_shr_glu_gelu_kernel(
@@ -45,7 +47,7 @@ def tile_moe_shr_glu_gelu_kernel(
 
         offsets = keep.tile([P, T // 16], U16, name="offsets")
         x_rows = xT.rearrange("(p d) t -> p d t", d=4)
-        x_planes = [keep.tile([P, T if d else 6 * C], F32, name="x_plane%d" % d, align_bytes=64) for d in range(4)]
+        x_planes = [keep.tile([P, T if d else 6 * C], F32, name="x_plane%d" % d) for d in range(4)]
         nc.gpsimd.memset(x_planes[0][:, T:], 0.0)
 
         def x_plane(d):
@@ -53,7 +55,9 @@ def tile_moe_shr_glu_gelu_kernel(
 
         w1s = keep.tile([P, MATRICES * H], U8, name="w1s", align_bytes=64)
         w3s = keep.tile([P, MATRICES * H], U8, name="w3s", align_bytes=64)
+        w2s = keep.tile([P, MATRICES * N], U8, name="w2s", align_bytes=64)
         nc.vector.memset(w1s[:].bitcast(I32), 0)
+        nc.gpsimd.memset(w2s[:].bitcast(I32), 0)
 
         zeros = keep.tile([P, 1], F32, name="zeros")
         nc.vector.memset(zeros[:], 0.0)
@@ -65,10 +69,10 @@ def tile_moe_shr_glu_gelu_kernel(
         identity = keep.tile([P, P], F32, name="identity")
         make_identity(nc, identity[:])
 
-        def load_scales(plane, scales, queue=nc.sync):
+        def load_scales(plane, scales, rows=range(4)):
             source = scales[:, 0].rearrange("e (q r) i -> r q e i", r=4)
-            for r in range(4):
-                queue.dma_start(
+            for r in rows:
+                nc.sync.dma_start(
                     plane[:].bitcast(I32)[r:P:32, :].rearrange("q (e i) -> q e i", e=MATRICES), source[r].bitcast(I32)
                 )
 
@@ -94,14 +98,14 @@ def tile_moe_shr_glu_gelu_kernel(
             nc.sync.dma_start(x_plane(d), x_rows[:, d, :])
         load_scales(w1s, w1_scales)
         load_matrices(w1w, w1_words, slice(0, MATRICES, E))
-        load_matrices(w3w, w3_words, slice(0, 1, 1))
+        load_matrices(w3w, w3_words, slice(0, MATRICES, E))
         load_scales(w3s, w3_scales)
-        load_matrices(w3w, w3_words, slice(1, MATRICES, E - 1))
-        load_matrices(w1w, w1_words, slice(1, 2, 1))
-        load_matrices(w1w, w1_words, slice(2, E, 1))
-        load_matrices(w3w, w3_words, slice(2, E, 1))
+        for experts in (slice(1, 3, 1), slice(3, E, 1)):
+            load_matrices(w1w, w1_words, experts)
+            load_matrices(w3w, w3_words, experts)
         w2w = keep.tile([P, MATRICES * 2 * N], U8, name="w2w", align_bytes=64)
         load_words(w2w, w2_words, slice(0, MATRICES), MATRICES)
+        load_scales(w2s, w2_scales)
         gate_rows = keep.tile([P, T], F32, name="gate_rows")
         nc.sync.dma_start(gate_rows[:], gate[0:P, :])
 
@@ -164,9 +168,6 @@ def tile_moe_shr_glu_gelu_kernel(
         for d in range(2, 4):
             gather_on_scalar(2, d)
         quantise_tokens(0)
-        w2s = keep.tile([P, MATRICES * N], U8, name="w2s", tag="x_plane2", align_bytes=64)
-        nc.gpsimd.memset(w2s[:].bitcast(I32), 0)
-        load_scales(w2s, w2_scales, nc.scalar)
         weave(1)
         weave(2)
         quantise_tokens(1)
@@ -177,8 +178,8 @@ def tile_moe_shr_glu_gelu_kernel(
         permuted = {}
 
         def permute(name, words, scales, tag):
-            new_words = keep.tile([P, 2 * H], U8, name="new_words", tag=name + "_permuted", align_bytes=64)
-            new_scales = keep.tile([P, H], U8, name="new_scales", tag=tag, align_bytes=64)
+            new_words = keep.tile([P, 2 * H], U8, name="new_words", tag=tag[0], align_bytes=64)
+            new_scales = keep.tile([P, H], U8, name="new_scales", tag=tag[1], align_bytes=64)
             nc.gpsimd.tensor_copy(
                 new_scales[:].rearrange("p (d m) -> p d m", d=4),
                 scales[:, E * H :].rearrange("p (m d) -> p d m", d=4),
@@ -256,8 +257,8 @@ def tile_moe_shr_glu_gelu_kernel(
             )
 
         def quantise_hidden(n):
-            codes = keep.tile([P, 2 * C], U32, name="h_codes%d" % n, align_bytes=64)
-            scales = keep.tile([P, 2 * C], U8, name="h_scales%d" % n, align_bytes=64)
+            codes = keep.tile([P, 2 * C], U32, name="h_codes", tag=H_CODE_TAGS[n], align_bytes=64)
+            scales = keep.tile([P, 2 * C], U8, name="h_scales", tag=H_SCALE_TAGS[n], align_bytes=64)
             nc.vector.quantize_mx(
                 out=codes[:].bitcast(FP8X4), scales=scales[:], in_=grouped[n][:].rearrange("p k s d -> p (k s d)")
             )

@@ -32,8 +32,8 @@ WARM_PASSES = 4
 TURN_BANK = (7, 5, 2)
 RESULT_BANKS = ((3, 7), (1, 4), (5, 0))
 GROUP_TAGS = ("grouped0", "woven1", "grouped2")
-H_CODE_TAGS = ("h_codes0", "h_codes0", "gated0", "h_codes3")
-H_SCALE_TAGS = ("h_scales0", "h_scales1", "h_scales2", "h_scales0")
+H_CODE_TAGS = ("h_codes0", "h_codes0", "h_codes2", "gated0")
+H_SCALE_TAGS = ("h_scales0", "h_scales1", "h_scales0", "h_scales3")
 PERMUTED_TAGS = (("gathered", "woven2"), ("woven1", "woven3"))
 
 
@@ -362,19 +362,19 @@ def tile_moe_shr_glu_gelu_kernel(
         product(6)
         group(2)
         product(7)
-        apply_gate(0)
         quantise_hidden(1)
+        apply_gate(0)
         last_layer(1)
-        add_both(0)
         quantise_hidden(2)
         last_routed()
+        add_both(0)
         quantise_hidden(3)
         last_shared()
         apply_gate(1)
-        add_both(1)
         apply_gate(2)
-        add_half(2, 1)
+        add_both(1)
         add_half(2, 0)
+        add_half(2, 1)
         scatter_on_scalar(0, C, 0)
         scatter_on_scalar(0, C, 1)
         scatter_on_scalar(C, 2 * C, 0)

@@ -34,6 +34,7 @@ RESULT_BANKS = ((3, 7), (1, 4), (5, 0))
 GROUP_TAGS = ("grouped0", "woven1", "grouped2")
 H_CODE_TAGS = ("h_codes0", "h_codes0", "h_codes2", "gated0")
 H_SCALE_TAGS = ("h_scales0", "h_scales1", "h_scales0", "h_scales3")
+SPLIT = 192
 PERMUTED_TAGS = (("gathered", "woven2"), ("woven1", "woven3"))
 
 
@@ -373,12 +374,12 @@ def tile_moe_shr_glu_gelu_kernel(
         apply_gate(1)
         apply_gate(2)
         add_both(1)
-        add_half(2, 0)
         add_half(2, 1)
+        add_half(2, 0)
         scatter_on_scalar(0, C, 0)
         scatter_on_scalar(0, C, 1)
-        scatter_on_scalar(C, 2 * C, 0)
-        copy_scatter_on_vector(2 * C, T, 0)
+        scatter_on_scalar(C, SPLIT, 0)
+        copy_scatter_on_vector(SPLIT, T, 0)
         scatter_on_scalar(C, T, 1)
         nc.sync.dma_start(out[0:P, :], windows[0][:])
         nc.scalar.dma_start(out[P : 2 * P, :], windows[1][:])

@@ -98,12 +98,13 @@ def tile_moe_shr_glu_gelu_kernel(
         for d in range(1, 4):
             nc.sync.dma_start(x_plane(d), x_rows[:, d, :])
         load_scales(w1s, w1_scales)
-        load_matrices(w1w, w1_words, slice(0, MATRICES, E))
-        load_matrices(w3w, w3_words, slice(0, MATRICES, E))
+        load_matrices(w1w, w1_words, slice(0, 1, 1))
+        load_matrices(w1w, w1_words, slice(1, MATRICES, E - 1))
+        load_matrices(w3w, w3_words, slice(0, 1, 1))
         load_scales(w3s, w3_scales)
-        for experts in (slice(1, 3, 1), slice(3, E, 1)):
-            load_matrices(w1w, w1_words, experts)
-            load_matrices(w3w, w3_words, experts)
+        load_matrices(w3w, w3_words, slice(1, MATRICES, E - 1))
+        load_matrices(w1w, w1_words, slice(2, E, 1))
+        load_matrices(w3w, w3_words, slice(2, E, 1))
         w2w = keep.tile([P, MATRICES * 2 * N], U8, name="w2w", align_bytes=64)
         load_words(w2w, w2_words, slice(0, MATRICES), MATRICES)
         load_scales(w2s, w2_scales)
@@ -230,9 +231,15 @@ def tile_moe_shr_glu_gelu_kernel(
         def b_pass(i):
             b_sums[i] = project(i, "w3", w3w, w3s, B_BANK[i])
 
+        def parts(i):
+            if i == len(UNITS) - 1:
+                return (slice(0, C // 2), slice(C // 2, C))
+            return (slice(None),)
+
         def gelu(i):
             gelus[i] = keep.tile([P, 2, P, 2] if i < 6 else [P, C, 4], F32, name="gelu%d" % i, align_bytes=64)
-            nc.scalar.activation(gelus[i][:], a_sums[i], GELU)
+            for part in parts(i):
+                nc.scalar.activation(gelus[i][:, part], a_sums[i][:, part], GELU)
 
         grouped[3] = keep.tile([P, 2, C, 4], BF16, name="grouped3", align_bytes=64)
 
@@ -241,7 +248,8 @@ def tile_moe_shr_glu_gelu_kernel(
                 hidden[i] = keep.tile([P, 2, P, 2], BF16, name="hidden%d" % i, align_bytes=64)[:]
             else:
                 hidden[i] = grouped[3][:, i - 6]
-            nc.vector.tensor_tensor(hidden[i], gelus[i][:], b_sums[i], MULT)
+            for part in parts(i):
+                nc.vector.tensor_tensor(hidden[i][:, part], gelus[i][:, part], b_sums[i][:, part], MULT)
 
         def turn(n):
             turned[n] = psum.tile([P, 2, 2, C], F32, name="turned", tag="bank%d" % TURN_BANK[n])

from contextlib import ExitStack

import concourse.mybir as mybir
from concourse.masks import make_identity

K, T, E, C, H, N = 512, 512, 4, 128, 512, 256
FLOPS = 2 * 2 * T * (2 * K * H + H * N)

F32 = mybir.dt.float32
BF16 = mybir.dt.bfloat16
I32 = mybir.dt.int32
U32 = mybir.dt.uint32
U16 = mybir.dt.uint16
U8 = mybir.dt.uint8
FP8X4 = mybir.dt.float8_e4m3fn_x4
FP4X4 = mybir.dt.float4_e2m1fn_x4
GELU = mybir.ActivationFunctionType.Gelu_apprx_tanh
COPY = mybir.ActivationFunctionType.Copy
MULT = mybir.AluOpType.mult
ADD = mybir.AluOpType.add

P = 128
MATRICES = E + 1
ROUTED, SHARED = 0, 1
LIST_COLUMNS = C // 16

UNITS = ((0, ROUTED), (0, SHARED), (1, SHARED), (1, ROUTED), (2, ROUTED), (3, ROUTED), (2, SHARED), (3, SHARED))
TURNED_PAIRS = ((0, 1), (3, 2), (4, 5))
A_BANK = (0, 2, 4, 5, 1, 4, 1, 4)
B_BANK = (1, 3, 0, 6, 2, 3, 0, 6)
WARM_PASSES = 4
TURN_BANK = (7, 5, 2)
RESULT_BANKS = ((3, 7), (1, 4), (5, 0))
GROUP_TAGS = ("grouped0", "woven1", "grouped2")
H_CODE_TAGS = ("h_codes0", "h_codes0", "h_codes2", "gated0")
H_SCALE_TAGS = ("h_scales0", "h_scales1", "h_scales0", "h_scales3")
SPLIT = 192
PERMUTED_TAGS = (("gathered", "woven2"), ("woven1", "woven3"))


def tile_moe_shr_glu_gelu_kernel(
    tc, xT, w1_words, w1_scales, w3_words, w3_scales, w2_words, w2_scales, gate, offs, out
):
    nc = tc.nc
    with ExitStack() as ctx:
        keep = ctx.enter_context(tc.tile_pool(name="keep", bufs=1))
        psum = ctx.enter_context(tc.psum_pool(name="psum", bufs=1))

        offsets = keep.tile([P, T // 16], U16, name="offsets")
        x_rows = xT.rearrange("(p d) t -> p d t", d=4)
        x_planes = [keep.tile([P, T if d else 6 * C], F32, name="x_plane%d" % d) for d in range(4)]
        nc.gpsimd.memset(x_planes[0][:, T:], 0.0)

        def x_plane(d):
            return x_planes[d][:]

        w1s = keep.tile([P, MATRICES * H], U8, name="w1s", align_bytes=64)
        w3s = keep.tile([P, MATRICES * H], U8, name="w3s", align_bytes=64)
        w2s = keep.tile([P, MATRICES * N], U8, name="w2s", align_bytes=64)
        nc.vector.memset(w1s[:].bitcast(I32), 0)
        nc.gpsimd.memset(w2s[:].bitcast(I32), 0)

        zeros = keep.tile([P, 1], F32, name="zeros")
        nc.vector.memset(zeros[:], 0.0)
        gelu_unread = keep.tile([P, 1], F32, name="gelu_unread")
        nc.scalar.activation(gelu_unread[:], zeros[:, 0:1], GELU)

        nc.vector.memset(w3s[:].bitcast(I32), 0)

        identity = keep.tile([P, P], F32, name="identity")
        make_identity(nc, identity[:])

        def load_scales(plane, scales, rows=range(4)):
            source = scales[:, 0].rearrange("e (q r) i -> r q e i", r=4)
            for r in rows:
                nc.sync.dma_start(
                    plane[:].bitcast(I32)[r:P:32, :].rearrange("q (e i) -> q e i", e=MATRICES), source[r].bitcast(I32)
                )

        def load_words(tile, words, experts, count):
            nc.sync.dma_start(
                tile[:].bitcast(I32).rearrange("p (e b) -> p e b", e=count),
                words[experts, 0].rearrange("e p b -> p e b").bitcast(I32),
            )

        w1w, w3w = {}, {}

        def load_matrices(words, source, experts):
            members = range(experts.start, experts.stop, experts.step)
            name = "w%d_words%d" % (1 if words is w1w else 3, experts.start)
            tile = keep.tile([P, len(members) * 2 * H], U8, name=name, align_bytes=64)
            load_words(tile, source, experts, len(members))
            for n, e in enumerate(members):
                words[e] = tile[:, n * 2 * H : (n + 1) * 2 * H]

        nc.sync.dma_start(x_plane(0)[:, :T], x_rows[:, 0, :])
        nc.sync.dma_start(offsets[:], offs)
        for d in range(1, 4):
            nc.sync.dma_start(x_plane(d), x_rows[:, d, :])
        load_scales(w1s, w1_scales)
        load_matrices(w1w, w1_words, slice(0, 1, 1))
        load_matrices(w1w, w1_words, slice(1, MATRICES, E - 1))
        load_matrices(w3w, w3_words, slice(0, 1, 1))
        load_scales(w3s, w3_scales)
        load_matrices(w3w, w3_words, slice(1, MATRICES, E - 1))
        load_matrices(w1w, w1_words, slice(2, E, 1))
        load_matrices(w3w, w3_words, slice(2, E, 1))
        w2w = keep.tile([P, MATRICES * 2 * N], U8, name="w2w", align_bytes=64)
        load_words(w2w, w2_words, slice(0, MATRICES), MATRICES)
        load_scales(w2s, w2_scales)
        gate_rows = keep.tile([P, T], F32, name="gate_rows")
        nc.sync.dma_start(gate_rows[:], gate[0:P, :])

        def chunk_offsets(c, count=1):
            return offsets[:, LIST_COLUMNS * c : LIST_COLUMNS * (c + count)]

        gathered = keep.tile([P, 4, T - C], BF16, name="gathered", align_bytes=64)
        woven = [keep.tile([P, C, 4], BF16, name="woven%d" % c, align_bytes=64) for c in range(E)]
        x_codes, x_scales = {}, {}

        def gather_woven(c, d):
            nc.vector.tensor_copy(woven[c][:, :, d], x_plane(d).indirect(chunk_offsets(c)))

        def gather_on_vector(c, d):
            nc.vector.tensor_copy(gathered[:, d, (c - 1) * C : c * C], x_plane(d).indirect(chunk_offsets(c)))

        def gather_on_scalar(c, d):
            nc.scalar.activation(gathered[:, d, (c - 1) * C :], x_plane(d).indirect(chunk_offsets(c, E - c)), COPY)

        def weave(c):
            nc.vector.tensor_copy(
                woven[c][:].rearrange("p (s i) d -> p s d i", i=4),
                gathered[:, :, (c - 1) * C : c * C].rearrange("p d (s i) -> p s d i", i=4),
            )

        def quantise_tokens(c):
            x_codes[c] = keep.tile([P, C], U32, name="x_codes", tag="x_codes%d" % c, align_bytes=64)
            x_scales[c] = keep.tile([P, C], U8, name="x_scales%d" % c, align_bytes=64)
            nc.vector.quantize_mx(
                out=x_codes[c][:].bitcast(FP8X4), scales=x_scales[c][:], in_=woven[c][:].rearrange("p s d -> p (s d)")
            )

        def warm_up():
            warm_codes = keep.tile([P, C], U32, name="warm_codes", align_bytes=64)
            warm_scales = keep.tile([P, C], U8, name="warm_scales", align_bytes=64)
            values = gathered[:].rearrange("p d s -> p (d s)")[:, T - C : 2 * T - C]
            nc.vector.quantize_mx(out=warm_codes[:].bitcast(FP8X4), scales=warm_scales[:], in_=values)
            warm_unread = psum.tile([P, 2 * C], F32, name="warm_unread", tag="bank7")
            for n in range(WARM_PASSES):
                nc.tensor.matmul_mx(
                    out=warm_unread[:],
                    lhsT=warm_codes[:].bitcast(FP8X4),
                    lhsT_scale=warm_scales[:],
                    rhs=warm_codes[:].bitcast(U8).bitcast(FP4X4),
                    rhs_scale=warm_codes[:].bitcast(U8)[:, : 2 * C],
                    start=True,
                    stop=True,
                )

        gather_woven(0, 0)
        gather_on_scalar(1, 0)
        gather_woven(0, 1)
        gather_on_vector(1, 1)
        gather_on_scalar(2, 1)
        gather_on_vector(1, 2)
        gather_woven(0, 2)
        warm_up()
        gather_woven(0, 3)
        gather_on_vector(1, 3)
        for d in range(2, 4):
            gather_on_scalar(2, d)
        quantise_tokens(0)
        weave(1)
        weave(2)
        quantise_tokens(1)
        weave(3)
        quantise_tokens(2)
        quantise_tokens(3)

        permuted = {}

        def permute(name, words, scales, tag):
            new_words = keep.tile([P, 2 * H], U8, name="new_words", tag=tag[0], align_bytes=64)
            new_scales = keep.tile([P, H], U8, name="new_scales", tag=tag[1], align_bytes=64)
            nc.gpsimd.tensor_copy(
                new_scales[:].rearrange("p (d m) -> p d m", d=4),
                scales[:, E * H :].rearrange("p (m d) -> p d m", d=4),
            )
            nc.gpsimd.tensor_copy(
                new_words[:].rearrange("p (d m b) -> p d m b", d=4, b=2),
                words[E].rearrange("p (m d b) -> p d m b", d=4, b=2),
            )
            permuted[name] = (new_words, new_scales)

        permute("w1", w1w, w1s, PERMUTED_TAGS[0])
        permute("w3", w3w, w3s, PERMUTED_TAGS[1])

        def project(i, name, words, scales, bank):
            c, kind = UNITS[i]
            sums = psum.tile([P, H], F32, name="sums", tag="bank%d" % bank)
            if i < 6:
                e = (c, E)[kind]
                nc.tensor.matmul_mx(
                    out=sums[:],
                    lhsT=x_codes[c][:].bitcast(FP8X4),
                    lhsT_scale=x_scales[c][:],
                    rhs=words[e].bitcast(FP4X4),
                    rhs_scale=scales[:, e * H : (e + 1) * H],
                    start=True,
                    stop=True,
                )
                return sums[:].rearrange("s (q u e) -> s u q e", u=2, e=2)
            new_words, new_scales = permuted[name]
            for d in range(4):
                nc.tensor.matmul_mx(
                    out=sums[:, d * C : (d + 1) * C],
                    lhsT=new_words[:, 2 * d * P : 2 * (d + 1) * P].bitcast(FP4X4),
                    lhsT_scale=new_scales[:, d * P : (d + 1) * P],
                    rhs=x_codes[c][:].bitcast(FP8X4),
                    rhs_scale=x_scales[c][:],
                    start=True,
                    stop=True,
                )
            return sums[:].rearrange("p (d s) -> p s d", d=4)

        a_sums, b_sums, gelus, hidden, turned, grouped, h_codes = {}, {}, {}, {}, {}, {}, {}

        def a_pass(i):
            a_sums[i] = project(i, "w1", w1w, w1s, A_BANK[i])

        def b_pass(i):
            b_sums[i] = project(i, "w3", w3w, w3s, B_BANK[i])

        def parts(i):
            if i == len(UNITS) - 1:
                return (slice(0, C // 2), slice(C // 2, C))
            return (slice(None),)

        def gelu(i):
            gelus[i] = keep.tile([P, 2, P, 2] if i < 6 else [P, C, 4], F32, name="gelu%d" % i, align_bytes=64)
            for part in parts(i):
                nc.scalar.activation(gelus[i][:, part], a_sums[i][:, part], GELU)

        grouped[3] = keep.tile([P, 2, C, 4], BF16, name="grouped3", align_bytes=64)

        def product(i):
            if i < 6:
                hidden[i] = keep.tile([P, 2, P, 2], BF16, name="hidden%d" % i, align_bytes=64)[:]
            else:
                hidden[i] = grouped[3][:, i - 6]
            for part in parts(i):
                nc.vector.tensor_tensor(hidden[i][:, part], gelus[i][:, part], b_sums[i][:, part], MULT)

        def turn(n):
            turned[n] = psum.tile([P, 2, 2, C], F32, name="turned", tag="bank%d" % TURN_BANK[n])
            for k, i in enumerate(TURNED_PAIRS[n]):
                words = hidden[i].rearrange("s u q e -> s (u q e)").bitcast(F32)
                for u in range(2):
                    nc.tensor.transpose(turned[n][:, k, u, :], words[:, u * P : (u + 1) * P], identity[:])

        def group(n):
            grouped[n] = keep.tile([P, 2, C, 4], BF16, name="grouped", tag=GROUP_TAGS[n], align_bytes=64)
            nc.scalar.copy(
                grouped[n][:].rearrange("p k s d -> p (k s d)").bitcast(F32).rearrange("p (k s u) -> p k s u", k=2, u=2),
                turned[n][:].rearrange("p k u s -> p k s u"),
            )

        def quantise_hidden(n):
            codes = keep.tile([P, 2 * C], U32, name="h_codes", tag=H_CODE_TAGS[n], align_bytes=64)
            scales = keep.tile([P, 2 * C], U8, name="h_scales", tag=H_SCALE_TAGS[n], align_bytes=64)
            nc.vector.quantize_mx(
                out=codes[:].bitcast(FP8X4), scales=scales[:], in_=grouped[n][:].rearrange("p k s d -> p (k s d)")
            )
            h_codes[n] = (codes, scales)

        def last_pass(result, e, v, n, first, last):
            column = e * N + v * P
            codes, scales = h_codes[n]
            nc.tensor.matmul_mx(
                out=result,
                lhsT=w2w[:, 2 * column : 2 * (column + P)].bitcast(FP4X4),
                lhsT_scale=w2s[:, column : column + P],
                rhs=codes[:, first:last].bitcast(FP8X4),
                rhs_scale=scales[:, first:last],
                start=True,
                stop=True,
            )

        y, ys, gated = {}, {}, {}
        summed = keep.tile([P, 2, T], F32, name="summed", align_bytes=64)

        def last_layer(c):
            y[c] = psum.tile([P, 2, C], F32, name="y", tag="bank%d" % RESULT_BANKS[c][0])
            ys[c] = psum.tile([P, 2, C], F32, name="ys", tag="bank%d" % RESULT_BANKS[c][1])
            for v in range(2):
                last_pass(y[c][:, v, :], c, v, c, 0, C)
            for v in range(2):
                last_pass(ys[c][:, v, :], E, v, c, C, 2 * C)

        def last_routed():
            y[2] = psum.tile([P, 2, 2 * C], F32, name="y", tag="bank%d" % RESULT_BANKS[2][0])
            for k in range(2):
                for v in range(2):
                    last_pass(y[2][:, v, k * C : (k + 1) * C], 2 + k, v, 2, k * C, (k + 1) * C)

        def last_shared():
            ys[2] = psum.tile([P, 2, 2 * C], F32, name="ys", tag="bank%d" % RESULT_BANKS[2][1])
            for v in range(2):
                last_pass(ys[2][:, v, :], E, v, 3, 0, 2 * C)

        def slots(n):
            return slice(n * C, (n + 1) * C if n < 2 else T)

        def apply_gate(n):
            width = C if n < 2 else 2 * C
            gated[n] = keep.tile([P, 2, width], F32, name="gated%d" % n, align_bytes=64)
            weights = gate_rows[:, slots(n)].unsqueeze(1).to_broadcast([P, 2, width])
            nc.vector.tensor_tensor(gated[n][:], y[n][:], weights, MULT)

        def add_both(n):
            nc.vector.tensor_tensor(summed[:, :, slots(n)], gated[n][:], ys[n][:], ADD)

        def add_half(n, v):
            nc.vector.tensor_tensor(summed[:, v, slots(n)], gated[n][:, v, :], ys[n][:, v, :], ADD)

        windows = [keep.tile([P, T], F32, name="window%d" % v, align_bytes=64) for v in range(2)]

        def scatter_on_scalar(first, last, v):
            nc.scalar.activation(windows[v][:].indirect(offsets[:, first // 16 : last // 16]), summed[:, v, first:last], COPY)

        def copy_scatter_on_vector(first, last, v):
            nc.vector.tensor_copy(windows[v][:].indirect(offsets[:, first // 16 : last // 16]), summed[:, v, first:last])

        a_pass(0)
        a_pass(1)
        gelu(0)
        gelu(1)
        a_pass(2)
        b_pass(0)
        b_pass(1)
        gelu(2)
        a_pass(3)
        b_pass(2)
        gelu(3)
        b_pass(3)
        product(0)
        a_pass(4)
        product(1)
        gelu(4)
        a_pass(5)
        b_pass(4)
        product(2)
        gelu(5)
        turn(0)
        group(0)
        a_pass(6)
        b_pass(5)
        product(3)
        gelu(6)
        a_pass(7)
        product(4)
        b_pass(6)
        b_pass(7)
        turn(1)
        gelu(7)
        product(5)
        quantise_hidden(0)
        last_layer(0)
        turn(2)
        group(1)
        product(6)
        group(2)
        product(7)
        quantise_hidden(1)
        apply_gate(0)
        last_layer(1)
        quantise_hidden(2)
        last_routed()
        add_both(0)
        quantise_hidden(3)
        last_shared()
        apply_gate(1)
        apply_gate(2)
        add_both(1)
        add_half(2, 1)
        add_half(2, 0)
        scatter_on_scalar(0, C, 0)
        scatter_on_scalar(0, C, 1)
        scatter_on_scalar(C, SPLIT, 0)
        copy_scatter_on_vector(SPLIT, T, 0)
        scatter_on_scalar(C, T, 1)
        nc.sync.dma_start(out[0:P, :], windows[0][:])
        nc.scalar.dma_start(out[P : 2 * P, :], windows[1][:])
